import numpy as np, ml_dtypes
CORES = [2,3,42,43,82,83,122,123]
N = 8
BF = ml_dtypes.bfloat16
def gentries(a):
    return np.ascontiguousarray(a.reshape(8, 16, -1).transpose(0, 2, 1)).reshape(8, -1)
def gtable(e):
    e = np.asarray(e); return np.ascontiguousarray(e.reshape(8, -1, 16).transpose(0, 2, 1)).reshape(128, -1).astype(np.int32)
V, NB, S0, T, RO = 1536, 3328, 1024, 256, 3
def dist(b, c, v):
    pk = np.take_along_axis(b, c.reshape(N, 8, 1, 16 * T), 3).reshape(N, 8, 16, 16, T)
    return np.add.reduce(np.abs(pk - v[:, :, :, None, :]), axis=2)
def parts(rng):
    c = rng.integers(0, NB, (N, 8, 16, V)); p = rng.integers(0, V, (N, 8, 16, V)); sh = rng.integers(0, S0, (N, 8, V))
    b = rng.integers(0, 256, (N, 8, 16, NB)); h = rng.integers(600, 1150, (N, 8, 1, S0)) + rng.integers(-100, 101, (N, 8, 16, S0))
    v = rng.integers(0, 256, (N, 8, 16, T)); o = rng.integers(0, V, (N, 8, T)); dr = rng.integers(0, 256, (N, 8, 16, RO))
    return c, p, sh, b, h, v, o, dr
def apart(rng, sh):
    o = np.ascontiguousarray(np.argsort(rng.random((N, 8, V)), axis=-1)[..., :T]); lab = np.ascontiguousarray(np.argsort(rng.random((N, 8, S0)), axis=-1)[..., :T])
    np.put_along_axis(sh, o, lab, 2)
    return o, lab
def back(a):
    return np.roll(a, -1, axis=0)
def trail(rng, g, c, p, sh, b, h, v, o):
    k = rng.integers(0, 3, (N, 1, V)); at = np.zeros((RO, N, T), np.int64); j = np.arange(RO * T); i = np.arange(T); m1 = min(S0, 2 * T)
    for q in range(N):
        u = rng.permutation(V)[:RO * T]; m = rng.permutation(S0)[:m1]
        at[:, q] = u.reshape(RO, T); sh[q, g, u] = m[j % m1]; k[q, 0, u] = j // m1
        if S0 == T and q % 2:
            x = u[T:2 * T]; sh[q, g, x] = m[i % (T // 2)]; k[q, 0, x] = 1 + i // (T // 2)
            at[2, q, :T // 2] = x[T // 2:]; k[q, 0, at[2, q, T // 2:]] = 1
    for t in range(RO - 1):
        to = back(at[t + 1])
        for q in range(N): p[q, g][:, at[t, q]] = to[q]
    b[:, g] = rng.integers(0, 64, (N, 16, NB)) + 32 + 80 * (np.arange(NB) % 3)
    c[:, g] = 3 * rng.integers(0, NB // 3, (N, 16, V)) + k
    v[:, g] = v[:, g] >> 4; h[:, g] = 0; o[:, g] = at[0]
def pack(c, p, sh, b, h, v, o, dr):
    def bf(x): return np.ascontiguousarray(x.reshape(N, 128, -1)).astype(np.float32).astype(BF)
    return {"rec": (p * 4096 + c).reshape(N, 128, V).astype(np.int32), "shp": sh.astype(np.int32), "box": bf(b), "bound": h.reshape(N, 128, S0).astype(np.int32),
            "tv": bf(v), "ob": np.stack([gtable(a) for a in o]), "dr": bf(dr)}
def setup_inputs(rng):
    return pack(*parts(rng))
def setup_inputs_ties(rng):
    c, p, sh, b, h, v, o, dr = parts(rng); o, lab = apart(rng, sh)
    c[:, :, 8:] = c[:, :, 7::-1].copy()
    v[..., :1] = np.take_along_axis(b, np.take_along_axis(c[:, :, 5], o[..., :1], 2)[:, :, None, :], 3)
    e = dist(b, np.take_along_axis(c, o[:, :, None, :], 3), v)
    m = rng.integers(0, 4, (N, 8, 1, T)); row = np.arange(16)[:, None]
    hit = np.where(m == 1, rng.random(e.shape) < 0.2, np.where(m == 2, row == 15, (m == 3) & (row == 0)))
    np.put_along_axis(h, lab[:, :, None, :] + np.zeros((1, 1, 16, 1), np.int64), np.maximum(e - 1 + hit, 0), 3)
    return pack(c, p, sh, b, h, v, o, dr)
def setup_inputs_crowd(rng):
    c, p, sh, b, h, v, o, dr = parts(rng); k = rng.permutation(V)[:12].reshape(4, 3); k[0] = k[0, 0]
    for j in range(4):
        o[:, 2 * j] = k[j][rng.integers(0, 3, (N, T))]; p[:, 2 * j] = k[j][rng.integers(0, 3, (N, 16, V))]
    sh[:, 1::2] = rng.choice(np.array([0, S0 - 1, S0 // 2]), (N, 4, V)); sh[:, 3] = rng.integers(0, S0, (N, 1))
    z = [1, 5, 7]
    b[:, z] = b[:, z] >> 3; v[:, z] = v[:, z] >> rng.integers(0, 4, (N, 3, 1, T)); h[:, z] = h[:, z] // 8
    return pack(c, p, sh, b, h, v, o, dr)
def setup_inputs_thin(rng):
    c, p, sh, b, h, v, o, dr = parts(rng); s2 = sh.copy(); o2, lab = apart(rng, s2)
    o[:, 3] = o2[:, 3]; sh[:, 3] = s2[:, 3]
    b[:, 3] = np.maximum(b[:, 3], 1); v[:, 3] = 0
    h[:, 0] = 0; h[:, 1] = 4080; h[:, 2, :, ::2] = 0; h[:, 2, :, 1::2] = 4080; h[:, 3] = 0
    h[:, 4] = 0; h[:, 4, 15] = 4080; h[:, 5] = 0; h[:, 5, 0] = 4080
    b[:, 6] = b[:, 6] >> (3 + np.arange(N) % 5)[:, None, None]; v[:, 6] = 255 - (v[:, 6] >> rng.integers(3, 8, (N, 1, T)))
    trail(rng, 7, c, p, sh, b, h, v, o)
    return pack(c, p, sh, b, h, v, o, dr)
def setup_inputs_ends(rng):
    c, p, sh, b, h, v, o, dr = parts(rng)
    c[:, ::3] = rng.choice(np.array([0, NB - 1]), (N, 3, 16, V)); p[:, 1:6:2] = rng.choice(np.array([0, V - 1]), (N, 3, 16, V))
    sh[:, 2:6:3] = rng.choice(np.array([0, S0 - 1]), (N, 2, V)); o[:, :3] = rng.choice(np.array([0, V - 1]), (N, 3, T))
    b[:, 4] = 0; v[:, 4] = 255; h[:, 4] = rng.choice(np.array([4079, 4080]), (N, 16, S0), p=np.array([0.96, 0.04]))
    b[:, 7] = rng.choice(np.array([0, 255]), (N, 16, NB)); v[:, 7] = rng.choice(np.array([0, 255]), (N, 16, T)); h[:, 7] = rng.integers(1000, 2100, (N, 16, S0))
    dr[:, ::2] = rng.choice(np.array([0, 255]), (N, 4, 16, RO))
    return pack(c, p, sh, b, h, v, o, dr)
def setup_inputs_spread(rng):
    c, p, sh, b, h, v, o, dr = parts(rng)
    b = b >> rng.integers(0, 8, (N, 8, 1, NB)); v = v >> rng.integers(0, 8, (N, 8, 1, T)); dr = dr >> rng.integers(0, 8, (N, 8, 1, RO))
    h = np.minimum(np.exp2(12 * rng.random((N, 8, 1, S0))) * (0.5 + rng.random((N, 8, 16, S0))), 4080).astype(np.int64)
    c = (NB * rng.random(c.shape) ** 2).astype(np.int64); p = (V * rng.random(p.shape) ** 3).astype(np.int64)
    sh = (S0 * rng.random(sh.shape) ** 2).astype(np.int64); o = (V * rng.random(o.shape) ** 3).astype(np.int64)
    return pack(c, p, sh, b, h, v, o, dr)
def check_inputs(d):
    bad = []
    for k, lo, hi in (("rec", 0, 4096 * V - 1), ("shp", 0, S0 - 1), ("box", 0, 255), ("bound", 0, 4080), ("tv", 0, 255), ("ob", 0, V - 1), ("dr", 0, 255)):
        x = np.asarray(d[k]).astype(np.float64)
        if not (np.min(x) >= lo and np.max(x) <= hi and np.all(np.floor(x) == x)): bad.append("range of " + k)
    if np.max(np.asarray(d["rec"]).astype(np.int64) & 4095) >= NB: bad.append("box numbers of rec")
    return bad
def reference(rec, shp, box, bound, tv, ob, dr):
    w = rec.astype(np.int64).reshape(N, 8, 16, V); sh = shp.astype(np.int64)
    b = np.zeros((N, 8, 16, NB + RO * T), np.int64); b[..., :NB] = box.astype(np.float32).astype(np.int64).reshape(N, 8, 16, NB)
    h = np.zeros((N, 8, 16, S0 + RO * T), np.int64); h[..., :S0] = bound.astype(np.int64).reshape(N, 8, 16, S0)
    nx = np.tile(np.arange(S0 + RO * T), (N, 8, 1))
    v = tv.astype(np.float32).astype(np.int64).reshape(N, 8, 16, T); o = np.stack([gentries(a) for a in ob]).astype(np.int64)
    drift = dr.astype(np.float32).astype(np.int64).reshape(N, 8, 16, RO)
    for t in range(RO):
        s = np.take_along_axis(sh, o, 2); n = np.take_along_axis(nx, s, 2)
        x = np.take_along_axis(w, o[:, :, None, :], 3)
        x = np.where((n != s)[:, :, None, :], np.roll(x, -1, axis=2), x)
        c = x & 4095; p = x >> 12; e = dist(b, c, v)
        hn = np.take_along_axis(h, n[:, :, None, :], 3); fit = e <= hn; has = np.any(fit, axis=2)
        a = np.where(has, np.argmax(fit, axis=2), np.argmin(e, axis=2))[:, :, None, :]
        ba = np.take_along_axis(b, np.take_along_axis(c, a, 2), 3); go = np.take_along_axis(p, a, 2)[:, :, 0]; hs = has[:, :, None, :]
        y = np.where((np.arange(16)[:, None] == a) & hs, p * 4096 + NB + T * t + np.arange(T), x)
        b[..., NB + T * t:NB + T * (t + 1)] = np.where(hs, (ba + v) >> 1, 0)
        makes = ~has & (np.take_along_axis(nx, n, 2) == n); wider = np.maximum(hn, e)
        for q in range(N):
            for g in range(8):
                i = np.unique(o[q, g], return_index=True)[1]
                w[q, g][:, o[q, g, i]] = y[q, g][:, i]; sh[q, g, o[q, g, i]] = n[q, g, i]
                j = np.flatnonzero(makes[q, g]); j = j[np.unique(n[q, g, j], return_index=True)[1]]
                h[q, g][:, S0 + T * t + j] = wider[q, g][:, j]; nx[q, g, n[q, g, j]] = S0 + T * t + j
        v = np.where(hs, (ba + drift[..., t:t + 1]) & 255, v); o = go
        if t < RO - 1:
            v = np.roll(v, 1, axis=0); o = np.roll(o, 1, axis=0)
    return {"yr": w.reshape(N, 128, V).astype(np.float32), "yh": h[..., S0:].reshape(N, 128, RO * T).astype(np.float32), "yv": v.reshape(N, 128, T).astype(np.float32).astype(BF)}

@@ -1,0 +1,712 @@
+import math
+from concourse.mybir import AluOpType, ActivationFunctionType
+
+NV, NB, S0, NT, RO = 1536, 3328, 1024, 256, 3
+BIG = float(2 ** 24)
+MAGIC = float(3 * 2 ** 22)
+LNB = math.log(1.8)
+HB = (1024, 1536, 2304)
+
+F, B, H, I32, U = "float32", "bfloat16", "float16", "int32", "uint16"
+_S = {
+    "obi": (16, I32), "dri": (4, B), "reci": (NV, I32), "bndi": (S0, I32), "shpi": (384, I32), "shph": (384, H),
+    "rct": (NV + NT, F), "boxt": (NB + 2 * NT, B), "hh": (8 + 2816, F), "sht": (NV + NT, F), "nx": (2304, F), "tab": (2048, F),
+    "o0": (16, U), "o1": (16, U), "o2": (16, U), "v0": (NT, B), "v1": (NT, B), "v2": (NT, B),
+    "ox0": (16, U), "ox1": (16, U), "ox2": (16, U), "ox3": (16, U), "ox4": (16, U), "ox5": (16, U),
+    "vs0": (NT, B), "vs1": (NT, B), "vs2": (NT, B),
+    "xi": (NT, I32), "c32": (NT, I32), "c16": (NT, U), "xx0": (384, F), "xx1": (384, F), "xs": (NT, F), "xq": (NT, F), "p16": (NT, H),
+    "bh0": (4096, B), "bh1": (4096, B), "mx0": (2048, B), "mx1": (2048, B), "vT": (NT, B),
+    "sW": (NT, H), "nW": (NT, H), "oW": (NT, H), "nq": (NT, H), "rotW": (NT, B), "r256": (NT, F),
+    "sLf": (16, F), "s16": (16, U), "nLf": (16, F), "n16": (16, U), "oLf": (16, F), "rL": (16, F), "r2L": (16, F),
+    "t1": (16, F), "t2": (16, F), "t3": (16, F), "hl": (16, U), "xsl": (16, U), "ycol": (16, F), "nqL": (16, F),
+    "hn": (NT, F), "hnT": (NT, F), "nf": (NT, F), "uu": (NT, F), "sc": (NT, F), "d0": (NT, F), "iar": (NT, B),
+    "u4": (16, F), "w16": (16, F), "cwa": (32, B), "cwc": (32, B),
+    "ohT": (NT, B), "rpT": (NT, B), "nhT": (NT, B), "dg0": (NT, H), "dg1": (NT, H),
+    "nhL": (16, F), "akL": (16, F), "akw": (16, F), "XX": (NT, B), "sg": (NT, B), "tp": (NT, F), "bt": (NT, F),
+    "eqo": (2176, B), "eqn": (2176, B), "So": (NT, B), "Sn": (NT, B),
+    "lo1": (16, F), "lo2": (16, F), "lo3": (16, F), "ol": (16, U), "thA": (16, F),
+    "wn": (16, F), "ln1": (16, F), "ln2": (16, F), "ln3": (16, F), "nl": (16, U), "y1": (16, F), "yl": (16, U),
+    "yo0": (NT, F), "yo1": (NT, F), "yo2": (NT, F),
+    "cf": (24, F), "ci": (8, I32), "cj": (8, I32), "kq": (144, F), "kg": (128, F), "kgb": (128, B),
+    "Ib": (128, B), "Ih": (128, H), "nIh": (128, H), "I4k": (128, H), "If": (128, F), "If4": (128, F), "Rf": (128, F), "Rb": (128, F),
+    "BI": (128, B), "nBI": (128, B), "hI": (128, B), "qI": (128, B), "mI": (128, B), "Bb": (128, B), "nB": (128, B), "B16": (128, B),
+    "one": (128, B), "oneh": (128, H), "s2": (8, B), "sm": (8, B), "s16b": (8, B), "Zb": (144, B), "Zh": (144, H),
+    "EE": (2048, B), "e16": (16, F), "e4": (4, F), "sq": (512, H),
+    "ia": (128, B), "rl": (8, U), "rli": (8, I32), "iL": (16, F), "iH": (16, F), "i16": (16, F), "wL": (16, F), "thL": (16, F),
+    "c16i": (8, H), "d15": (16, F), "d20": (16, F), "nr": (3 * NT, H), "db1": (4, F), "db2": (4, F), "db3": (4, F),
+}
+PLACE = {}
+SCRATCH = {}
+for _k, (_n, _d) in _S.items():
+    if _n <= 16 and _k not in ("obi", "dri", "o0", "o1", "o2", "ox0", "ox1", "ox2", "ox3"):
+        _at = SCRATCH.get("pool_" + _d, (0, [128, 0]))[1][1]
+        PLACE[_k] = ("pool_" + _d, _at)
+        SCRATCH["pool_" + _d] = ("sbuf", [128, _at + 16], _d)
+    else:
+        SCRATCH[_k] = ("sbuf", [128, _n], _d)
+for _b in range(8):
+    SCRATCH["P%d" % _b] = ("psum", [128, 512], F)
+_DMA = ["l%d" % k for k in range(16)]
+_ARR = ["a%s%d%d" % (k, t, h) for k in "ov" for t in range(2) for h in range(2)]
+SEMAPHORES = ["sV", "sS", "sP", "sG", "sent"] + _DMA + _ARR
+
+A = AluOpType
+AF = ActivationFunctionType
+GUESS = ((1.56, 3.8, 0.52, 110, 4200, 150.0), (1.04, 1.6, 0.5, 60, 3000, 250.0), (1.56, 3.8, 0.5, 250, 3000, 250.0))
+
+
+def vw(name, lo=0, hi=None, step=1):
+    return (name, lo, _S[name][0] if hi is None else hi, step)
+
+
+def ind(win, off):
+    return ("@", win, off)
+
+
+def wide(x):
+    return x[0][0] == "P" or _S[x[0]][1] in (F, I32)
+
+
+def count(x):
+    return 16 * (x[2][2] - x[2][1]) if x[0] == "@" else (x[2] - x[1] + x[3] - 1) // x[3]
+
+
+def declare(guess):
+    RHO, SCAT, PEC, HOP, NET, RATE = guess
+    ops = []
+    part = ["c"]
+
+    def add(eng, kind, args, rd, wr, cost, **kw):
+        r = []
+        w = []
+        for x in rd:
+            if isinstance(x, tuple):
+                r += [x[1], x[2]] if x[0] == "@" else [x]
+        for x in wr:
+            if x[0] == "@":
+                w.append(x[1])
+                r.append(x[2])
+            else:
+                w.append(x)
+        name = part[0] + ((w or r or [("",)])[0][0] if part[0] != "c" else "")
+        ops.append(dict(part=name, eng=eng, kind=kind, args=args, rd=r, wr=w, cost=cost, **kw))
+
+    def vcost(out, in_, two=False):
+        n = count(out)
+        if out[0] == "@":
+            return 60 + SCAT * n
+        if in_[0] == "@":
+            return 60 + RHO * n
+        return max(64, n * (2 if two else (1 if wide(out) or wide(in_) else 0.5)))
+
+    def cp(out, in_, **kw):
+        add("V", "cp", (out, in_), [in_], [out], vcost(out, in_), **kw)
+
+    def tt(out, a, b, op):
+        psum = a[0][0] == "P" or b[0][0] == "P"
+        add("V", "tt", (out, a, b, op), [a, b], [out], max(64, count(out)) if psum else vcost(out, a, True))
+
+    def ts(out, a, s1, op0, s2=None, op1=None):
+        add("V", "ts", (out, a, s1, s2, op0, op1), [a, s1, s2], [out], vcost(out, a))
+
+    def ms(out, c):
+        add("V", "ms", (out, c), [], [out], vcost(out, out))
+
+    def scan(out, d0, d1):
+        add("V", "scan", (out, d0, d1), [d0, d1], [out], count(out))
+
+    def act(out, in_, func=AF.Identity, bias=0.0, scale=1.0):
+        n = count(out)
+        cost = 80 + RHO * n if in_[0] == "@" else max(64, n) + (1500 if func == AF.Exp else 0)
+        add("S", "act", (out, in_, func, bias, scale), [in_, bias, scale], [out], cost)
+
+    def mms(items, **kw):
+        rd = []
+        for x in items:
+            rd += [y for y in x[1:3] if y not in rd]
+        add("P", "mm", items, rd, [items[0][0]], sum(PEC * max(64, count(x[2])) * (4 if wide(x[1]) else 1) for x in items), **kw)
+
+    def mm(out, l, r, start=True, stop=True, **kw):
+        mms([(out, l, r, start, stop)], **kw)
+
+    def group(out, *pairs_):
+        mms([(out, l, r, k == 0, k == len(pairs_) - 1) for k, (l, r) in enumerate(pairs_)])
+
+    def iota(out, pat, base, cm):
+        add("G", "iota", (out, pat, base, cm), [], [out], 160 + 2 * count(out))
+
+    nd = [0, 0]
+
+    def dma(q, kind, args, rd, wr, nbytes):
+        nd[1] = nbytes + (nd[1] if kind != "store" or args[0] == "yr" else 0)
+        add(q, kind, args, rd, wr, 60, sem=_DMA[nd[0]], lat=2200 + nd[1] / RATE)
+        nd[0] += 1
+
+    def P(b, lo, hi, step=1):
+        return ("P%d" % b, lo, hi, step)
+
+    def diag(out, src, z, extra=None):
+        mms([(out, vw(z, 15 - r, 143 - r), vw(src, r, NT, 16), r == 0, r == 15 and extra is None) for r in range(16)]
+            + ([extra + (False, True)] if extra else []))
+
+    dma("S", "load", ("obi", "ob", 0, 16), [], [vw("obi")], 8192)
+    dma("Q", "load", ("reci", "rec", 0, NV), [], [vw("reci")], 786432)
+    dma("S", "shp", (), [], [vw("shpi")], 49152)
+    dma("S", "load", ("v0", "tv", 0, NT), [], [vw("v0")], 65536)
+    dma("S", "load", ("dri", "dr", 0, 3), [], [vw("dri", 0, 3)], 768)
+    dma("Q", "load", ("boxt", "box", 0, NB), [], [vw("boxt", 0, NB)], 851968)
+    dma("Q", "load", ("bndi", "bound", 0, S0), [], [vw("bndi")], 524288)
+    for k in range(1, 7):
+        ops[k]["soft"] = {k - 1}
+    cp(vw("o0"), vw("obi"))
+
+    col = lambda k: vw("cf", k, k + 1)
+    iota(vw("kq"), [[1, 144]], 0, 0)
+    iota(vw("ci", 0, 1), [[1, 1]], 0, 1)
+    iota(vw("tab", 0, 256), [[1, 256]], 0, 0)
+    iota(vw("rli"), [[1, 8]], 0, 0)
+    iota(vw("kg"), [[16, 8], [0, 16]], 0, 0)
+    iota(vw("ia"), [[0, 8], [1, 16]], -15, 0)
+    cp(col(0), vw("ci", 0, 1))
+    ts(vw("cj", 0, 1), vw("ci", 0, 1), 15, A.bitwise_and)
+    cp(col(1), vw("cj", 0, 1))
+    tt(col(2), col(0), col(1), A.subtract)
+    ts(col(3), col(2), 15.0, A.add)
+    ts(col(4), col(2), 0.0625, A.mult)
+    ts(col(5), col(0), -1.0, A.add)
+    ts(col(6), col(1), 0.0, A.is_equal, 16.0, A.mult)
+    ts(col(7), col(0), 1.0, A.add)
+    ts(col(8), col(1), 15.0, A.is_equal, -16.0, A.mult)
+    ts(col(9), col(0), 0.0, A.is_equal)
+    for t in range(RO):
+        ts(col(10 + t), col(0), 1.0, A.is_equal, float(NB + NT * t), A.mult)
+    ts(col(13), col(0), 16.0, A.mult)
+    ts(col(16), col(0), 4.0, A.mult)
+    ms(col(14), 128 * LNB)
+    ms(col(15), -4095.0 / 8192)
+    kq = vw("kq", 0, 128)
+    for name, s in (("Ib", 1.0), ("Ih", 1.0), ("nIh", -1.0), ("I4k", 4096.0)):
+        ts(vw(name), kq, col(0), A.is_equal, s, A.mult)
+    for name, s in (("If", 1.0), ("If4", 4096.0), ("BI", BIG), ("nBI", -BIG), ("hI", 0.5), ("qI", -0.25), ("mI", -128.0)):
+        act(vw(name), vw("Ib"), AF.Identity, 0.0, s)
+    ts(vw("Bb"), vw("kg"), col(2), A.is_equal)
+    act(vw("nB"), vw("Bb"), AF.Identity, 0.0, -4096.0)
+    act(vw("B16"), vw("Bb"), AF.Identity, 0.0, 0.0625)
+    for name, k0, k1 in (("Rf", 5, 6), ("Rb", 7, 8)):
+        tt(col(k0), col(k0), col(k1), A.add)
+        ts(vw(name), kq, col(k0), A.is_equal)
+    for name, s in (("s2", 8192.0), ("sm", -4096.0), ("s16b", 0.0625)):
+        ts(vw(name), vw("kq", 0, 8), col(4), A.is_equal, s, A.mult)
+    ts(vw("Zb"), vw("kq"), col(3), A.is_equal)
+    ts(vw("Zh"), vw("kq"), col(3), A.is_equal)
+    ms(vw("one"), 1.0)
+    ts(vw("oneh"), kq, 0.0, A.is_ge)
+    ts(vw("e16"), vw("kq", 0, 16), -128.0, A.mult, col(13), A.add)
+    cp(vw("kgb"), vw("kg"))
+    for q in range(16):
+        ts(vw("EE", 128 * q, 128 * q + 128), vw("kgb"), vw("e16", q, q + 1), A.is_equal)
+    ms(vw("d0"), -1.0)
+    ms(vw("d0", 0, NT, 16), 3.0e7)
+    cp(vw("rl"), vw("rli"))
+    ts(vw("iL"), vw("kq", 0, 16), 16.0, A.mult, col(1), A.add)
+    act(vw("wL"), vw("iL"), AF.Exp, col(14), -LNB)
+    ts(vw("thL"), vw("wL"), 40.0, A.mult)
+    ts(vw("c16i"), vw("iL", 0, 8), 16.0, A.mult, 15.0, A.add)
+    ts(vw("iH", 0, 8), vw("iL", 0, 8), 16.0, A.mult)
+    ts(vw("iH", 8, 16), vw("iL", 0, 8), 16.0, A.mult)
+    ts(vw("i16"), vw("iL"), 16.0, A.mult)
+    ts(vw("d15"), vw("iL"), float(NV), A.add)
+    ts(vw("d20"), vw("iL"), 2048.0, A.add)
+    for n in (256, 512, 1024):
+        act(vw("tab", n, 2 * n), vw("tab", 0, n), AF.Identity, float(n))
+    iota(vw("nx"), [[1, 2304]], 0, 0)
+    for t in range(RO):
+        ts(vw("nr", NT * t, NT * t + NT), vw("tab", 0, NT), col(9), A.mult, col(10 + t), A.add)
+    ts(vw("db1", 0, 3), vw("dri", 0, 3), -255.5, A.add)
+    ts(vw("db2", 0, 3), vw("dri", 0, 3), -128.0, A.add)
+    ts(vw("db3", 0, 3), vw("dri", 0, 3), -1.0, A.mult)
+    for name, lo, n in (("xx0", 128, 128), ("xx1", 128, 128), ("rct", NV, NT), ("sht", NV, NT), ("bh0", 2048, 2048), ("bh1", 2048, 2048)):
+        iota(vw(name, lo, lo + n), [[0, n]], 0, 0)
+    ms(vw("hh", 0, 8), 0.0)
+    cp(vw("shph"), vw("shpi"), rows=32)
+    ts(vw("e4"), vw("kq", 0, 4), -4.0, A.mult, col(16), A.add)
+    for k in range(4):
+        ts(vw("sq", 128 * k, 128 * k + 128), vw("kg"), vw("e4", k, k + 1), A.is_equal)
+        mm(P(4 + k, 0, 384), vw("sq", 128 * k, 128 * k + 128), vw("shph"), rows=32)
+        act(vw("sht", 384 * k, 384 * k + 384), P(4 + k, 0, 384))
+    for k in range(3):
+        cp(vw("rct", 512 * k, 512 * k + 512), vw("reci", 512 * k, 512 * k + 512))
+    for k in range(2):
+        cp(vw("hh", 8 + 512 * k, 520 + 512 * k), vw("bndi", 512 * k, 512 * k + 512))
+
+    def pairs(eq, W, Lf, wt, Sb):
+        at = 0
+        for m in range(16):
+            n = NT - 16 * m
+            ts(vw(eq, at, at + n), vw(W, 16 * m, NT), vw(Lf, m, m + 1), A.is_equal, vw(wt, m, m + 1), A.mult)
+            mm(P(6, 16 * m, NT), vw("Bb"), vw(eq, at, at + n), m == 0, m == 15)
+            at += n
+        act(vw(Sb), P(6, 0, NT))
+        diag(P(6, 256, 272), Sb, "Zb")
+
+    for t in range(RO):
+        o, v, vs = "o%d" % t, "v%d" % t, "vs%d" % t
+        rot = t > 0
+        hw = lambda name, h: vw(name, 128 * h, 128 * h + 128)
+        hl_ = lambda name, h: vw(name, 8 * h, 8 * h + 8)
+        nW = "nW" if rot else "sW"
+        nLf = "nLf" if rot else "sLf"
+        xs = lambda h: hw("xs", h) if rot else vw("xx%d" % h, 0, 128)
+        bias = lambda name: vw(name, t, t + 1)
+        if rot:
+            for h in range(2):
+                add("X", "recv", ("ao%d%d" % (t - 1, h),), [], [hl_(o, h)], 0, after=("so", t - 1, h))
+                add("X", "recv", ("av%d%d" % (t - 1, h),), [], [hw(v, h)], 0, after=("sv", t - 1, h))
+
+        def lists(h):
+            if t == 0:
+                ts(hw("c32", h), ind(vw("reci"), hl_(o, h)), 4095, A.bitwise_and)
+            else:
+                cp(hw("xi", h), ind(vw("rct", 0, NV), hl_(o, h)))
+                ts(hw("c32", h), hw("xi", h), 4095, A.bitwise_and)
+            cp(hw("c16", h), hw("c32", h))
+            act(vw("xx%d" % h, 0, 128), ind(vw("rct", 0, NV), hl_(o, h)))
+            mm(P(2 + h, 128, 256), hw(v, h), vw("Ib"))
+            act(hw("vT", h), P(2 + h, 128, 256))
+            act(vw("bh%d" % h, 2063, 4096, 16), hw(v, h), AF.Identity, bias("db3"))
+
+        def main(h):
+            bh, mx = "bh%d" % h, "mx%d" % h
+            mm(P(2 + h, 0, 128), hw(v, h), vw("nB"), True, False)
+            for q in range(4):
+                act(vw(bh, 512 * q, 512 * q + 512), ind(vw("boxt", 0, NB + NT * t), vw("c16", 128 * h + 32 * q, 128 * h + 32 * q + 32)))
+                mm(P(q % 2, 0, 512), hw("vT", h), vw("EE", 512 * q, 512 * q + 512))
+                tt(vw(mx, 512 * q, 512 * q + 512), vw(bh, 512 * q, 512 * q + 512), P(q % 2, 0, 512), A.max)
+            mms([(P(2 + h, a, 128, 16), vw(bh, a, 2048, 16), vw("sm"), False, False) for a in range(16)])
+            mms([(P(2 + h, a, 128, 16), vw(mx, a, 2048, 16), vw("s2"), False, a == 15) for a in range(16)])
+
+        def shapes():
+            ps, pn, pq, p7 = P(5, 256, 272), P(5, 272, 288), P(5, 288, 304), P(7, 256, 512)
+            cp(vw("sW"), ind(vw("sht", 0, NV), vw(o)))
+            diag(ps, "sW", "Zh")
+            ts(vw("s16"), ps, 0.0625, A.mult)
+            act(vw("sLf"), ps, AF.Identity, 0.0, 1.0 if rot else 0.0625)
+            if rot:
+                for h in range(2):
+                    mm(P(7, 256, 384), vw("Rf"), vw("xx%d" % h, 0, 128))
+                    act(vw("xx%d" % h, 256, 384), P(7, 256, 384))
+                cp(vw("nW"), ind(vw("nx", 0, 2048), vw("s16")))
+                diag(pn, "nW", "Zh")
+                tt(vw("rL"), vw("sLf"), pn, A.not_equal)
+                ts(vw("r2L"), vw("rL"), 4096.0, A.mult)
+                tt(vw("t1"), vw("r2L"), pn, A.add)
+                ts(vw("hl"), vw("t1"), 0.0625, A.mult)
+                act(vw("nLf"), pn, AF.Identity, 0.0, 0.0625)
+                tt(vw("t2"), vw("iH"), vw("r2L"), A.add)
+                ts(vw("xsl"), vw("t2"), 0.0625, A.mult)
+                group(p7, (vw("Ih"), vw("nW")), (vw("nIh"), vw("sW")))
+                act(vw("rotW"), p7, AF.Sign)
+                mms([(P(7, 8 * h, 8 * h + 8), hw("rotW", h), vw("s16b"), True, True) for h in range(2)])
+                act(vw("d0", 1, NT, 16), P(7, 0, 16), AF.Identity, -1.0, 16.0)
+                for h in range(2):
+                    group(P(7, 128 * h, 128 * h + 128), (hw("rotW", h), vw("B16")), (vw("Ib"), vw("ia")))
+                act(vw("iar"), P(7, 0, NT))
+                act(vw("hn"), ind(vw("hh", 8, 8 + HB[t]), vw("hl")))
+            else:
+                cp(vw("hn"), ind(vw("bndi"), vw("s16")))
+            mms([(P(7, 128 * h, 128 * h + 128), hw("hn", h), vw("If4"), True, True) for h in range(2)])
+            act(vw("hnT"), P(7, 0, NT))
+            for h in range(2):
+                if rot:
+                    cp(hw("xs", h), ind(vw("xx%d" % h), hl_("xsl", h)))
+                act(hw("xq", h), xs(h), AF.Identity, col(15), 1.0 / 4096)
+            ts(vw("p16"), vw("xq"), MAGIC, A.add, -MAGIC, A.add)
+            if t == 1:
+                act(vw("r256"), vw("rotW"), AF.Identity, 0.0, 256.0)
+            if t == 2:
+                cp(vw("n16"), vw("nLf"))
+                tt(vw("nq"), ind(vw("nx", 0, 2048), vw("n16")), vw("nW"), A.is_equal)
+                diag(pq, "nq", "Zh")
+                ts(vw("nqL"), pq, 0.0625, A.mult)
+
+        def owners():
+            cp(vw("oW"), ind(vw("tab", 0, NV), vw(o)))
+            cp(vw("oLf"), vw(o))
+            pairs("eqo", "oW", "oLf", "wL", "So")
+            tt(vw("lo1"), vw("thL"), P(6, 256, 272), A.is_le)
+            tt(vw("lo2"), vw("lo1"), vw("d15"), A.mult)
+            tt(vw("lo3"), vw("lo2"), vw("oLf"), A.max)
+            cp(vw("ol"), vw("lo3"))
+
+        def choose(h):
+            e = P(2 + h, 0, 128)
+            dg = "dg%d" % h
+            tt(hw("nf", h), hw("hnT", h), e, A.is_lt)
+            tt(hw("uu", h), hw("nf", h), e, A.mult)
+            scan(hw("sc", h), hw("d0", h), hw("uu", h))
+            ends = vw("sc", 128 * h + 15, 128 * h + 128, 16)
+            ts(hl_("u4", h), ends, MAGIC * 4096, A.add, -MAGIC * 4096, A.add)
+            wa = vw("cwa", 16 * h, 16 * h + 8)
+            wc = vw("cwc", 16 * h, 16 * h + 8)
+            tt(wa, ends, hl_("u4", h), A.subtract)
+            if rot:
+                ts(hl_("w16", h), ends, 1.0, A.is_equal, -16.0, A.mult)
+                tt(wc, ends, hl_("w16", h), A.add)
+            else:
+                cp(wc, ends)
+            tt(hw("ohT", h), ind(wa, vw("rl")), hw("iar", h) if rot else vw("ia"), A.is_equal)
+            act(hw("rpT", h), ind(wc, vw("rl")))
+            mm(P(4, 0, 128), hw("ohT", h), vw("Ib"))
+            mm(P(4, 128, 256), hw("rpT", h), vw("Ib"))
+            tt(vw(dg, 0, 128), hw("p16", h), P(4, 0, 128), A.mult)
+            ts(vw(dg, 128, 256), P(4, 128, 256), 0.0625, A.mult, 128.0, A.min)
+            diag(P(4, 256, 272), dg, "Zh", (P(4, 264, 272), vw("Ih"), vw("c16i")))
+            ox = "ox%d" % (2 * t + h)
+            cp(vw(ox), P(4, 256, 272))
+            if t < 2:
+                add("G", "send", (vw(ox, 0, 8), hl_("o%d" % (t + 1), h), "ao%d%d" % (t, h)), [vw(ox, 0, 8)], [], 900, tag=("so", t, h))
+            ts(hl_("nhL", h), P(4, 264, 272), 2048.0, A.is_ge)
+            act(hw("XX", h), ind(vw("bh%d" % h), vw(ox, 8, 16)))
+            act(hw("sg", h), hw("XX", h), AF.Sign, bias("db1"))
+            group(P(2 + h, 128, 256), (vw("Ib"), hw("XX", h)), (vw("mI"), hw("sg", h)))
+            act(hw(vs, h), P(2 + h, 128, 256), AF.Identity, bias("db2"))
+            if t < 2:
+                add("G", "send", (hw(vs, h), hw("v%d" % (t + 1), h), "av%d%d" % (t, h)), [hw(vs, h)], [], 900, tag=("sv", t, h))
+            act(hw("nhT", h), hw("rpT", h), AF.Relu)
+            group(P(5, 128, 256), (hw("ohT", h), vw("BI")), (vw("one"), vw("nBI")), (hw("nhT", h), vw("nBI")), (vw("I4k"), hw("p16", h)),
+                  (vw("oneh"), vw("nr", NT * t + 128 * h, NT * t + 128 * h + 128)))
+            act(hw("tp", h), P(5, 128, 256))
+            tt(ind(vw("rct"), hl_("ol", h)), xs(h), hw("tp", h), A.max)
+            if t < 2:
+                group(P(2 + h, 256, 384), (vw("hI"), hw("XX", h)), (vw("hI"), hw(v, h)), (vw("one"), vw("qI")))
+                act(hw("bt", h), P(2 + h, 256, 384), AF.Identity, MAGIC)
+                act(vw("boxt", NB + NT * t + 128 * h, NB + NT * t + 128 * h + 128), hw("bt", h), AF.Identity, -MAGIC)
+            if t == 2:
+                tt(hl_("akL", h), hl_("nhL", h), hl_("nqL", h), A.mult)
+                tt(hl_("akw", h), hl_("akL", h), hl_("wL", h), A.mult)
+            else:
+                tt(hl_("akw", h), hl_("nhL", h), hl_("wL", h), A.mult)
+
+        def makers():
+            ak = "akL" if t == 2 else "nhL"
+            if t == 1:
+                cp(ind(vw("sht"), vw("ol")), vw("nW"))
+            c1 = 8 + HB[t] + (256 if rot else 0)
+            if rot:
+                tt(vw("t3"), vw("i16"), vw("r2L"), A.subtract)
+                act(vw("ycol"), vw("t3"), AF.Identity, float(c1), 0.0625)
+            else:
+                ts(vw("ycol"), vw("iL"), float(c1), A.add)
+            mms([(P(7, 128 * h, 128 * h + 128), hw("uu", h), vw("If"), True, True) for h in range(2)])
+            act(vw("hh", c1, c1 + NT), P(7, 0, NT), AF.Identity, 0.0, 1.0 / 4096)
+            if rot:
+                mm(P(7, 256, 512), vw("Rf"), vw("hh", c1, c1 + NT))
+                act(vw("hh", c1 - NT, c1), P(7, 256, 512))
+            if t < 2:
+                mm(P(7, 0, NT), vw("Rb"), vw("hh", c1, c1 + NT))
+                act(vw("hh", c1 + NT, c1 + 2 * NT), P(7, 0, NT))
+            pairs("eqn", nW, nLf, "akw", "Sn")
+            tt(vw("thA"), vw("thL"), vw(ak), A.mult)
+            tt(vw("wn"), vw("thA"), P(6, 256, 272), A.is_gt)
+            if t < 2:
+                tt(vw("ln1"), vw("thA"), P(6, 256, 272), A.is_le)
+                tt(vw("ln2"), vw("ln1"), vw("d20"), A.mult)
+                tt(vw("ln3"), vw("ln2"), vw(nLf), A.max)
+                cp(vw("nl"), vw("ln3"))
+                if t == 0:
+                    cp(ind(vw("nx"), vw("nl")), vw("tab", 1024, 1280))
+                else:
+                    tt(ind(vw("nx"), vw("nl")), vw("tab", 1792, 2048), vw("r256"), A.subtract)
+            tt(vw("y1"), vw("wn"), vw("ycol"), A.mult)
+            cp(vw("yl"), vw("y1"))
+            act(vw("yo%d" % t), ind(vw("hh", 0, c1 + NT), vw("yl")))
+            dma("Q", "store", ("yh", "yo%d" % t, NT * t, 0, NT), [vw("yo%d" % t)], [], 131072)
+
+        for name, fn, h in (("l0", lists, 0), ("l1", lists, 1), ("m0", main, 0), ("s0", shapes, None), ("oo", owners, None),
+                            ("m1", main, 1), ("c0", choose, 0), ("c1", choose, 1), ("kk", makers, None)):
+            part[0] = "%s%d" % (name, t)
+            if h is None:
+                fn()
+            else:
+                fn(h)
+    dma("Q", "store", ("yv", "vs2", 0, 0, NT), [vw("vs2")], [], 65536)
+    dma("Q", "store", ("yr", "rct", 0, 0, 768), [vw("rct", 0, 768)], [], 393216)
+    dma("S", "store", ("yr", "rct", 768, 768, 768), [vw("rct", 768, NV)], [], 393216)
+    return ops, link(ops, HOP, NET)
+
+
+def link(ops, hop, net):
+    last = {}
+    tags = {}
+    phase = {}
+    for i, op in enumerate(ops):
+        deps = set()
+        sides = [(x, False) for x in op["rd"]] + [(x, True) for x in op["wr"]]
+        for x, w in sides:
+            if x[0][0] == "P":
+                before, now = phase.get(x[0], ([], []))
+                if now and ops[now[-1]]["eng"] != op["eng"]:
+                    before, now = (now[-1:] if ops[now[-1]]["eng"] == "P" else now), []
+                deps.update(before)
+                if op["eng"] == "P":
+                    op["soft"] = set(now[-1:])
+                phase[x[0]] = (before, now + [i])
+                continue
+            for j, y, wj in last.get(x[0], []):
+                if j != i and x[1] < y[2] and y[1] < x[2] and (w or wj):
+                    deps.add(j)
+        for x, w in sides:
+            if x[0][0] == "P":
+                continue
+            old = last.get(x[0], [])
+            if w and x[3] == 1:
+                old = [z for z in old if not (x[1] <= z[1][1] and z[1][2] <= x[2])]
+            last[x[0]] = old + [(i, x, w)]
+        op["deps"] = deps
+        if "tag" in op:
+            tags[op["tag"]] = i
+    pre = []
+    for op in ops:
+        p = [(j, hop + ops[j].get("lat", 0)) for j in sorted(op["deps"])] + [(j, 0) for j in op.get("soft", ()) if j not in op["deps"]]
+        if "after" in op:
+            p.append((tags[op["after"]], net))
+        pre.append(p)
+    return pre
+
+
+def place(cost, eng, before, key):
+    n = len(cost)
+    after = [[] for _ in cost]
+    left = [len(p) for p in before]
+    for i, p in enumerate(before):
+        for j, l in p:
+            after[j].append(i)
+    ready = sorted((key[i], i) for i in range(n) if not left[i])
+    slots = [[] for _ in range(6)]
+    t0 = [0.0] * n
+    while ready:
+        i = ready.pop(0)[1]
+        c = cost[i]
+        s = max([t0[j] + cost[j] + l for j, l in before[i]] + [0.0])
+        sl = slots[eng[i]]
+        lo = 0
+        while lo < len(sl) and sl[lo][1] <= s:
+            lo += 1
+        while lo < len(sl) and sl[lo][0] < s + c:
+            s = max(s, sl[lo][1])
+            lo += 1
+        sl.insert(lo, (s, s + c))
+        t0[i] = s
+        for k in after[i]:
+            left[k] -= 1
+            if not left[k]:
+                ready.append((key[k], k))
+        ready.sort()
+    return t0
+
+
+def run(order, eng, cost, lat, pre):
+    n = len(cost)
+    free = [0.0] * 6
+    last = [-1] * 6
+    t = [0.0] * n
+    why = [0] * n
+    end = 0.0
+    top = 0
+    for i in order:
+        e = eng[i]
+        s = free[e]
+        w = -2 - last[e]
+        for j, l in pre[i]:
+            if t[j] + l >= s:
+                s = t[j] + l
+                w = j
+        why[i] = w
+        s += cost[i]
+        t[i] = free[e] = s
+        last[e] = i
+        if s + lat[i] > end:
+            end = s + lat[i]
+            top = i
+    return end, why, top
+
+
+def arrange(plans, rounds):
+    ops, pre = plans[0]
+    n = len(ops)
+    eng = ["VSPGQX".index(o["eng"]) for o in ops]
+    tabs = [([o["cost"] for o in p[0]], [o.get("lat", 0) for o in p[0]], p[1]) for p in plans]
+    state = [12345]
+
+    def rnd(k):
+        state[0] = (state[0] * 1103515245 + 12345) % 2147483648
+        return (state[0] >> 8) % k
+
+    cost, lat, _ = tabs[0]
+    succ = [[] for _ in ops]
+    for i, p in enumerate(pre):
+        for j, l in p:
+            succ[j].append((i, l))
+    tail = [0.0 if succ[i] else lat[i] for i in range(n)]
+    prio = [0.0] * n
+    for i in range(n - 1, -1, -1):
+        prio[i] = cost[i] + max([l + prio[k] for k, l in succ[i]] + [tail[i]])
+    best = place(cost, eng, pre, [-p for p in prio])
+    length = lambda t0: max(t0[i] + cost[i] + tail[i] for i in range(n))
+    back = [succ[i] + [(n, tail[i])] for i in range(n)] + [[]]
+    for _ in range(100):
+        w = rnd(1000) + 1
+        tb = place(cost + [0.0], eng + [5], back, [rnd(w) - best[i] - cost[i] - tail[i] for i in range(n)] + [-1e18])
+        t0 = place(cost, eng, pre, [-tb[i] - cost[i] for i in range(n)])
+        if length(t0) < length(best):
+            best = t0
+    cur = sorted(range(n), key=lambda i: (best[i], i))
+    above = [set(j for j, l in p) for p in pre]
+    res = [run(cur, eng, *tb) for tb in tabs]
+    unit = [r[0] for r in res]
+    now = low = float(len(res))
+    keep = cur
+    for k in range(rounds):
+        _, why, i = res[rnd(len(res))]
+        held = []
+        while why[i] != -1:
+            if why[i] < -1:
+                held.append((i, -2 - why[i]))
+                i = -2 - why[i]
+            else:
+                i = why[i]
+        if not held:
+            continue
+        i, j = held[rnd(len(held))]
+        a = cur.index(j)
+        for _ in range((0, 0, 0, 1, 2, 4)[rnd(6)]):
+            p = a - 1
+            while p >= 0 and eng[cur[p]] != eng[i]:
+                p -= 1
+            if p >= 0:
+                a = p
+        b = cur.index(i)
+        need = set(above[i])
+        moved = [i]
+        for x in cur[b - 1:a:-1]:
+            if x in need:
+                moved.append(x)
+                need |= above[x]
+        if cur[a] in need:
+            continue
+        inside = set(moved)
+        new = cur[:a] + moved[::-1] + [x for x in cur[a:b] if x not in inside] + cur[b + 1:]
+        r = [run(new, eng, *tb) for tb in tabs]
+        v = sum(x[0] / u for x, u in zip(r, unit))
+        heat = 0.002 * (1.0 - k / rounds) + 0.0001
+        if v <= now or rnd(1000) < 1000 * math.exp((now - v) / heat):
+            cur, now, res = new, v, r
+            if v < low:
+                keep, low = new, v
+    return keep
+
+
+PLANS = [declare(x) for x in GUESS]
+OPS = PLANS[0][0]
+ORDER = arrange(PLANS, 30000)
+
+
+def rank_program(g, core, T, topo):
+    rank = T.rank_of(core)
+    if rank is None:
+        return
+    nxt = T.cores[(rank + 1) % len(T.cores)]
+    prv = T.cores[(rank - 1) % len(T.cores)]
+    rid, pid, _ = topo.addr(nxt)
+    eng = topo.engines(core, nxt)[:8]
+    mask = sum(1 << e for e in eng)
+    n_in = len(topo.engines(prv, core)[:8])
+    Q = {"V": g.vector, "S": g.scalar, "P": g.tensor, "G": g, "Q": g.sync}
+
+    def ap(x, rows=128):
+        if not isinstance(x, tuple):
+            return x
+        if x[0] == "@":
+            return ap(x[1]).indirect(ap(x[2]))
+        name, at = PLACE.get(x[0], (x[0], 0))
+        return T[name][0:rows, at + x[1]:at + x[2]] if x[3] == 1 else T[name][0:rows, at + x[1]:at + x[2]:x[3]]
+
+    needed = set()
+    for op in OPS:
+        needed |= op["deps"]
+    mark = {}
+    cnt = {e: 0 for e in "VSPG"}
+    for i in ORDER:
+        op = OPS[i]
+        if op["kind"] == "recv":
+            mark[i] = (op["args"][0], n_in)
+        elif "sem" in op:
+            mark[i] = (op["sem"], 16)
+        elif i in needed:
+            cnt[op["eng"]] += 1
+            mark[i] = ("s" + op["eng"], cnt[op["eng"]])
+    seen = {e: {} for e in Q}
+    known = {}
+    top = {}
+    sends = 0
+    for i in ORDER:
+        op = OPS[i]
+        e, k, a = op["eng"], op["kind"], op["args"]
+        if k == "recv":
+            top[a[0]] = n_in
+            continue
+        q = Q[e]
+        want = {}
+        for j in op["deps"]:
+            s, c = mark[j]
+            want[s] = max(want.get(s, 0), c)
+        want = {s: c for s, c in want.items() if seen[e].get(s, 0) < c}
+        for s in sorted(want):
+            if not any(known.get((z, want[z]), {}).get(s, 0) >= want[s] for z in want if z != s):
+                q.wait_ge(T.sem[s], want[s])
+        for s in want:
+            seen[e][s] = max(seen[e].get(s, 0), want[s])
+            for z, c in known.get((s, want[s]), {}).items():
+                seen[e][z] = max(seen[e].get(z, 0), c)
+        if k == "send":
+            g.remote_dma(ap(a[1]), ap(a[0]), T.sem[a[2]], T.sem.sent, pid, rid, mask)
+            sends += 1
+            continue
+        rows = op.get("rows", 128)
+        if k == "shp":
+            ins = q.dma_start(T.shpi[0:32, :], T.shp[:])
+        elif k == "load":
+            ins = q.dma_start(T[a[0]][:, a[2]:a[3]], T[a[1]][:, a[2]:a[3]])
+        elif k == "store":
+            ins = q.dma_start(T[a[0]][:, a[2]:a[2] + a[4]], T[a[1]][:, a[3]:a[3] + a[4]])
+        elif k == "cp":
+            ins = q.tensor_copy(ap(a[0], rows), ap(a[1], rows))
+        elif k == "tt":
+            ins = q.tensor_tensor(ap(a[0]), ap(a[1]), ap(a[2]), a[3])
+        elif k == "ts":
+            if a[5] is None:
+                ins = q.tensor_scalar(ap(a[0]), ap(a[1]), ap(a[2]), None, a[4])
+            else:
+                ins = q.tensor_scalar(ap(a[0]), ap(a[1]), ap(a[2]), ap(a[3]), a[4], a[5])
+        elif k == "ms":
+            ins = q.memset(ap(a[0]), a[1])
+        elif k == "scan":
+            ins = q.tensor_tensor_scan(ap(a[0]), ap(a[1]), ap(a[2]), 0.0, A.add, A.min)
+        elif k == "act":
+            ins = q.activation(ap(a[0]), ap(a[1]), a[2], ap(a[3]), ap(a[4]))
+        elif k == "mm":
+            for x in a:
+                ins = q.matmul(ap(x[0]), ap(x[1], rows), ap(x[2], rows), x[3], x[4])
+        elif k == "iota":
+            if _S[a[0][0]][1] == I32:
+                ins = q.iota(ap(a[0]), a[1], a[2], a[3])
+            else:
+                ins = q.iota(ap(a[0]), a[1], a[2], a[3], allow_small_or_imprecise_dtypes=True)
+        if i in mark:
+            s, c = mark[i]
+            ins.then_inc(T.sem[s], 16 if "sem" in op else 1)
+            top[s] = c
+            known[(s, c)] = dict(seen[e])
+    top["sent"] = sends * len(eng)
+    for s in sorted(top):
+        g.wait_ge(T.sem[s], top[s])

@@ -22,7 +22,7 @@ _S = {
     "hn": (NT, F), "hnT": (NT, F), "nf": (NT, F), "uu": (NT, F), "sc": (NT, F), "d0": (NT, F), "iar": (NT, B),
     "u4": (16, F), "w16": (16, F), "cwa": (32, B), "cwc": (32, B),
     "ohT": (NT, B), "rpT": (NT, B), "nhT": (NT, B), "dg0": (NT, H), "dg1": (NT, H),
-    "nhL": (16, F), "akL": (16, F), "akw": (16, F), "XX": (NT, B), "sg": (NT, B), "tp": (NT, F), "bt": (NT, F),
+    "nhL": (16, F), "akw": (16, F), "XX": (NT, B), "sg": (NT, B), "tp": (NT, F), "bt": (NT, F),
     "eqo": (2176, B), "eqn": (2176, B), "So": (NT, B), "Sn": (NT, B),
     "lo1": (16, F), "lo2": (16, F), "lo3": (16, F), "ol": (16, U), "thA": (16, F),
     "wn": (16, F), "ln1": (16, F), "ln2": (16, F), "ln3": (16, F), "nl": (16, U), "y1": (16, F), "yl": (16, U),
@@ -52,7 +52,7 @@ SEMAPHORES = ["sV", "sS", "sP", "sG", "sent"] + _DMA + _ARR
 
 A = AluOpType
 AF = ActivationFunctionType
-GUESS = ((1.56, 3.8, 0.52, 110, 4200, 150.0), (1.04, 1.6, 0.5, 60, 3000, 250.0), (1.56, 3.8, 0.5, 250, 3000, 250.0))
+GUESS = ((1.56, 3.8, 0.52, 170, 4200, 160.0), (1.3, 3.0, 0.7, 100, 3000, 250.0), (1.8, 4.5, 0.5, 250, 3000, 220.0))
 
 
 def vw(name, lo=0, hi=None, step=1):
@@ -155,7 +155,8 @@ def declare(guess):
     dma("S", "load", ("v0", "tv", 0, NT), [], [vw("v0")], 65536)
     dma("S", "load", ("dri", "dr", 0, 3), [], [vw("dri", 0, 3)], 768)
     dma("Q", "load", ("boxt", "box", 0, NB), [], [vw("boxt", 0, NB)], 851968)
-    dma("Q", "load", ("bndi", "bound", 0, S0), [], [vw("bndi")], 524288)
+    dma("Q", "load", ("bndi", "bound", 0, S0), [vw("reci")], [vw("bndi")], 524288)
+    ops[-1]["lat"] = 1490000 / RATE
     for k in range(1, 7):
         ops[k]["soft"] = {k - 1}
     cp(vw("o0"), vw("obi"))
@@ -262,6 +263,7 @@ def declare(guess):
             for h in range(2):
                 add("X", "recv", ("ao%d%d" % (t - 1, h),), [], [hl_(o, h)], 0, after=("so", t - 1, h))
                 add("X", "recv", ("av%d%d" % (t - 1, h),), [], [hw(v, h)], 0, after=("sv", t - 1, h))
+            dma("Q", "store", ("yh", "yo%d" % (t - 1), NT * (t - 1), 0, NT), [vw("yo%d" % (t - 1)), vw(v)], [], 131072)
 
         def lists(h):
             if t == 0:
@@ -327,7 +329,8 @@ def declare(guess):
                 cp(vw("n16"), vw("nLf"))
                 tt(vw("nq"), ind(vw("nx", 0, 2048), vw("n16")), vw("nW"), A.is_equal)
                 diag(pq, "nq", "Zh")
-                ts(vw("nqL"), pq, 0.0625, A.mult)
+                tt(vw("nqL"), vw("wL"), pq, A.mult)
+                ts(vw("nqL"), vw("nqL"), 0.0625, A.mult)
 
         def owners():
             cp(vw("oW"), ind(vw("tab", 0, NV), vw(o)))
@@ -364,7 +367,8 @@ def declare(guess):
             ox = "ox%d" % (2 * t + h)
             cp(vw(ox), P(4, 256, 272))
             if t < 2:
-                add("G", "send", (vw(ox, 0, 8), hl_("o%d" % (t + 1), h), "ao%d%d" % (t, h)), [vw(ox, 0, 8)], [], 900, tag=("so", t, h))
+                add("G", "send", (vw(ox, 0, 8), hl_("o%d" % (t + 1), h), "ao%d%d" % (t, h)), [vw(ox, 0, 8)], [],
+                    900 + (2000 if t + h == 0 else 0), tag=("so", t, h))
             ts(hl_("nhL", h), P(4, 264, 272), 2048.0, A.is_ge)
             act(hw("XX", h), ind(vw("bh%d" % h), vw(ox, 8, 16)))
             act(hw("sg", h), hw("XX", h), AF.Sign, bias("db1"))
@@ -381,14 +385,9 @@ def declare(guess):
                 group(P(2 + h, 256, 384), (vw("hI"), hw("XX", h)), (vw("hI"), hw(v, h)), (vw("one"), vw("qI")))
                 act(hw("bt", h), P(2 + h, 256, 384), AF.Identity, MAGIC)
                 act(vw("boxt", NB + NT * t + 128 * h, NB + NT * t + 128 * h + 128), hw("bt", h), AF.Identity, -MAGIC)
-            if t == 2:
-                tt(hl_("akL", h), hl_("nhL", h), hl_("nqL", h), A.mult)
-                tt(hl_("akw", h), hl_("akL", h), hl_("wL", h), A.mult)
-            else:
-                tt(hl_("akw", h), hl_("nhL", h), hl_("wL", h), A.mult)
+            tt(hl_("akw", h), hl_("nhL", h), hl_("nqL" if t == 2 else "wL", h), A.mult)
 
         def makers():
-            ak = "akL" if t == 2 else "nhL"
             if t == 1:
                 cp(ind(vw("sht"), vw("ol")), vw("nW"))
             c1 = 8 + HB[t] + (256 if rot else 0)
@@ -406,7 +405,7 @@ def declare(guess):
                 mm(P(7, 0, NT), vw("Rb"), vw("hh", c1, c1 + NT))
                 act(vw("hh", c1 + NT, c1 + 2 * NT), P(7, 0, NT))
             pairs("eqn", nW, nLf, "akw", "Sn")
-            tt(vw("thA"), vw("thL"), vw(ak), A.mult)
+            ts(vw("thA"), vw("akw"), 40.0, A.mult)
             tt(vw("wn"), vw("thA"), P(6, 256, 272), A.is_gt)
             if t < 2:
                 tt(vw("ln1"), vw("thA"), P(6, 256, 272), A.is_le)
@@ -420,7 +419,8 @@ def declare(guess):
             tt(vw("y1"), vw("wn"), vw("ycol"), A.mult)
             cp(vw("yl"), vw("y1"))
             act(vw("yo%d" % t), ind(vw("hh", 0, c1 + NT), vw("yl")))
-            dma("Q", "store", ("yh", "yo%d" % t, NT * t, 0, NT), [vw("yo%d" % t)], [], 131072)
+            if t == 2:
+                dma("Q", "store", ("yh", "yo2", NT * t, 0, NT), [vw("yo2")], [], 131072)
 
         for name, fn, h in (("l0", lists, 0), ("l1", lists, 1), ("m0", main, 0), ("s0", shapes, None), ("oo", owners, None),
                             ("m1", main, 1), ("c0", choose, 0), ("c1", choose, 1), ("kk", makers, None)):
@@ -531,12 +531,12 @@ def run(order, eng, cost, lat, pre):
     return end, why, top
 
 
-def arrange(plans, rounds):
+def arrange(plans, rounds, seed):
     ops, pre = plans[0]
     n = len(ops)
     eng = ["VSPGQX".index(o["eng"]) for o in ops]
     tabs = [([o["cost"] for o in p[0]], [o.get("lat", 0) for o in p[0]], p[1]) for p in plans]
-    state = [12345]
+    state = [seed]
 
     def rnd(k):
         state[0] = (state[0] * 1103515245 + 12345) % 2147483648
@@ -598,17 +598,17 @@ def arrange(plans, rounds):
         new = cur[:a] + moved[::-1] + [x for x in cur[a:b] if x not in inside] + cur[b + 1:]
         r = [run(new, eng, *tb) for tb in tabs]
         v = sum(x[0] / u for x, u in zip(r, unit))
-        heat = 0.002 * (1.0 - k / rounds) + 0.0001
+        heat = 0.0015 * (1.0 - k / rounds) + 0.0001
         if v <= now or rnd(1000) < 1000 * math.exp((now - v) / heat):
             cur, now, res = new, v, r
             if v < low:
                 keep, low = new, v
-    return keep
+    return sum(run(keep, eng, *tb)[0] for tb in tabs), keep
 
 
 PLANS = [declare(x) for x in GUESS]
 OPS = PLANS[0][0]
-ORDER = arrange(PLANS, 30000)
+ORDER = min(arrange(PLANS, 9000, s) for s in (6, 777, 31, 58))[1]
 
 
 def rank_program(g, core, T, topo):

@@ -2,38 +2,39 @@ import math
 from concourse.mybir import AluOpType, ActivationFunctionType
 
 NV, NB, S0, NT, RO = 1536, 3328, 1024, 256, 3
-BIG = float(2 ** 24)
 MAGIC = float(3 * 2 ** 22)
-LNB = math.log(1.8)
-HB = (1024, 1536, 2304)
+BETA = 1.8
+SO = 512
+EW = SO + NV + NT
+HS = (1, 0)
 
 F, B, H, I32, U = "float32", "bfloat16", "float16", "int32", "uint16"
 _S = {
     "obi": (16, I32), "dri": (4, B), "reci": (NV, I32), "bndi": (S0, I32), "shpi": (384, I32), "shph": (384, H),
-    "rct": (NV + NT, F), "boxt": (NB + 2 * NT, B), "hh": (8 + 2816, F), "sht": (NV + NT, F), "nx": (2304, F), "tab": (2048, F),
+    "rct": (NV + NT, F), "boxt": (NB + 2 * NT, B), "eb": (EW, F), "sht": (NV + NT, F), "tab": (NV, F),
     "o0": (16, U), "o1": (16, U), "o2": (16, U), "v0": (NT, B), "v1": (NT, B), "v2": (NT, B),
     "ox0": (16, U), "ox1": (16, U), "ox2": (16, U), "ox3": (16, U), "ox4": (16, U), "ox5": (16, U),
     "vs0": (NT, B), "vs1": (NT, B), "vs2": (NT, B),
-    "xi": (NT, I32), "c32": (NT, I32), "c16": (NT, U), "xx0": (384, F), "xx1": (384, F), "xs": (NT, F), "xq": (NT, F), "p16": (NT, H),
-    "bh0": (4096, B), "bh1": (4096, B), "mx0": (2048, B), "mx1": (2048, B), "vT": (NT, B),
-    "sW": (NT, H), "nW": (NT, H), "oW": (NT, H), "nq": (NT, H), "rotW": (NT, B), "r256": (NT, F),
-    "sLf": (16, F), "s16": (16, U), "nLf": (16, F), "n16": (16, U), "oLf": (16, F), "rL": (16, F), "r2L": (16, F),
-    "t1": (16, F), "t2": (16, F), "t3": (16, F), "hl": (16, U), "xsl": (16, U), "ycol": (16, F), "nqL": (16, F),
-    "hn": (NT, F), "hnT": (NT, F), "nf": (NT, F), "uu": (NT, F), "sc": (NT, F), "d0": (NT, F), "iar": (NT, B),
-    "u4": (16, F), "w16": (16, F), "cwa": (32, B), "cwc": (32, B),
-    "ohT": (NT, B), "rpT": (NT, B), "nhT": (NT, B), "dg0": (NT, H), "dg1": (NT, H),
-    "nhL": (16, F), "akw": (16, F), "XX": (NT, B), "sg": (NT, B), "tp": (NT, F), "bt": (NT, F),
-    "eqo": (2176, B), "eqn": (2176, B), "So": (NT, B), "Sn": (NT, B),
-    "lo1": (16, F), "lo2": (16, F), "lo3": (16, F), "ol": (16, U), "thA": (16, F),
-    "wn": (16, F), "ln1": (16, F), "ln2": (16, F), "ln3": (16, F), "nl": (16, U), "y1": (16, F), "yl": (16, U),
-    "yo0": (NT, F), "yo1": (NT, F), "yo2": (NT, F),
-    "cf": (24, F), "ci": (8, I32), "cj": (8, I32), "kq": (144, F), "kg": (128, F), "kgb": (128, B),
-    "Ib": (128, B), "Ih": (128, H), "nIh": (128, H), "I4k": (128, H), "If": (128, F), "If4": (128, F), "Rf": (128, F), "Rb": (128, F),
-    "BI": (128, B), "nBI": (128, B), "hI": (128, B), "qI": (128, B), "mI": (128, B), "Bb": (128, B), "nB": (128, B), "B16": (128, B),
-    "one": (128, B), "oneh": (128, H), "s2": (8, B), "sm": (8, B), "s16b": (8, B), "Zb": (144, B), "Zh": (144, H),
-    "EE": (2048, B), "e16": (16, F), "e4": (4, F), "sq": (512, H),
-    "ia": (128, B), "rl": (8, U), "rli": (8, I32), "iL": (16, F), "iH": (16, F), "i16": (16, F), "wL": (16, F), "thL": (16, F),
-    "c16i": (8, H), "d15": (16, F), "d20": (16, F), "nr": (3 * NT, H), "db1": (4, F), "db2": (4, F), "db3": (4, F),
+    "xi": (NT, I32), "c32": (NT, I32), "p32": (NT, I32), "c16": (NT, U),
+    "bh0": (4096, B), "bh1": (4096, B),
+    "sW": (NT, H), "nW": (NT, H), "oW": (NT, H), "nF": (NT, F), "hn": (NT, F), "sgW": (NT, B), "nsg": (NT, B), "rotW": (NT, B),
+    "sLf": (16, F), "s16": (16, U), "nLf": (16, F), "n16": (16, U), "t3": (16, F), "ycol": (16, F), "nqL": (16, F),
+    "cT": (NT, F), "rp": (NT, F), "sc": (288, F), "st": (288, B), "eS": (NT, F), "dg0": (NT, H), "dg1": (NT, H),
+    "yy": (NT, F), "zz": (NT, F), "nhL": (16, F), "akw": (16, F), "XX": (NT, B), "sg": (NT, B), "bt": (NT, F),
+    "eqo": (1152, B), "eqn": (2176, B), "So": (NT, B), "Sn": (NT, B),
+    "lo": (32, F), "lp": (32, F), "ld": (32, F), "ol": (16, U), "wd": (32, F), "nd": (32, F), "ln": (32, F), "nl": (16, U),
+    "y1": (16, F), "yl": (16, U),
+    "hy": (8 + 2 * NT, F), "dat": (NT, F), "seen": (NT, F), "yc16": (16, U), "yo0": (NT, F), "yo1": (NT, F), "yo2": (NT, F),
+    "cf": (32, F), "ci": (8, I32), "cj": (8, I32), "kq": (144, F), "kg": (128, F),
+    "Ib": (128, B), "II": (256, B), "nII": (256, B), "Ih": (128, H), "nI8k": (128, H), "B4k": (128, H), "I37": (128, B),
+    "If": (128, F), "nI26": (128, F), "nI23": (128, F), "Rf": (128, F), "Rb": (128, F), "RI": (128, F),
+    "Bb": (128, B), "nB3": (384, B), "KW": (128, B), "RW": (128, B),
+    "one": (256, B), "m0": (128, B), "s2": (24, B), "sm": (24, B), "sr": (8, B),
+    "Zb": (144, B), "Zh": (144, H), "ZK": (144, B), "Zq": (144, B),
+    "cl": (128, B), "cr": (256, B), "tl": (128, B), "tr": (256, B), "d0": (128, F), "bits": (NT, B),
+    "e4": (4, F), "sq": (512, H), "bc": (16, F), "fa": (16, F), "fb": (16, F), "fc": (16, F), "fd": (16, F), "fe": (16, F), "z16": (16, F),
+    "iL": (16, F), "wL": (16, F), "c16i": (8, H), "yc": (16, F),
+    "db1": (4, F), "db2": (4, F), "db3": (4, F),
 }
 PLACE = {}
 SCRATCH = {}
@@ -52,11 +53,21 @@ SEMAPHORES = ["sV", "sS", "sP", "sG", "sent"] + _DMA + _ARR
 
 A = AluOpType
 AF = ActivationFunctionType
-GUESS = ((1.56, 3.8, 0.52, 170, 4200, 160.0), (1.3, 3.0, 0.7, 100, 3000, 250.0), (1.8, 4.5, 0.5, 250, 3000, 220.0))
+GUESS = ((1.56, 3.8, 0.55, 170, 4200, 180.0, 1.0), (1.3, 3.0, 0.65, 120, 3000, 250.0, 1.2), (1.8, 4.5, 0.5, 250, 3500, 200.0, 1.4))
+Q4 = ((0, 32, 0), (32, 64, 0), (64, 96, 0), (96, 128, 0))
+Q2 = ((0, 64, 0), (64, 128, 0))
+Q3 = ((0, 64, 0), (64, 96, 0), (96, 128, 0))
+V0 = ((0, 32, 0), (32, 64, 1), (64, 128, 0))
+V1 = ((0, 32, 0), (32, 64, 0), (64, 96, 0), (96, 128, 1))
+V2 = ((0, 40, 0), (40, 64, 1), (64, 104, 0), (104, 128, 1))
+CUT = ((V0, Q2), (Q4, Q2), (Q4, Q2))
+ON = {"sht": 0, "eb": (1, 1), "seen": 0, "yo": (0, 0, 0), "split": (0, 0, 0)}
+CH = 64
 
 
-def vw(name, lo=0, hi=None, step=1):
-    return (name, lo, _S[name][0] if hi is None else hi, step)
+def vw(name, lo=0, hi=None, step=1, p=None):
+    x = (name, lo, _S[name][0] if hi is None else hi, step)
+    return x + (p,) if p else x
 
 
 def ind(win, off):
@@ -72,9 +83,10 @@ def count(x):
 
 
 def declare(guess):
-    RHO, SCAT, PEC, HOP, NET, RATE = guess
+    RHO, SCAT, PEC, HOP, NET, RATE, SLOW = guess
     ops = []
     part = ["c"]
+    allv = ON["sht"] and all(ON["eb"])
 
     def add(eng, kind, args, rd, wr, cost, **kw):
         r = []
@@ -89,7 +101,7 @@ def declare(guess):
             else:
                 w.append(x)
         name = part[0] + ((w or r or [("",)])[0][0] if part[0] != "c" else "")
-        ops.append(dict(part=name, eng=eng, kind=kind, args=args, rd=r, wr=w, cost=cost, **kw))
+        ops.append(dict(part=name, eng=eng, kind=kind, args=args, rd=r, wr=w, cost=cost * (1 if kind == "send" else SLOW), **kw))
 
     def vcost(out, in_, two=False):
         n = count(out)
@@ -99,12 +111,12 @@ def declare(guess):
             return 60 + RHO * n
         return max(64, n * (2 if two else (1 if wide(out) or wide(in_) else 0.5)))
 
-    def cp(out, in_, **kw):
-        add("V", "cp", (out, in_), [in_], [out], vcost(out, in_), **kw)
+    def cp(out, in_):
+        add("V", "cp", (out, in_), [in_], [out], vcost(out, in_))
 
     def tt(out, a, b, op):
         psum = a[0][0] == "P" or b[0][0] == "P"
-        add("V", "tt", (out, a, b, op), [a, b], [out], max(64, count(out)) if psum else vcost(out, a, True))
+        add("V", "tt", [(out, a, b, op)], [a, b], [out], max(64, count(out)) if psum else vcost(out, a, True))
 
     def ts(out, a, s1, op0, s2=None, op1=None):
         add("V", "ts", (out, a, s1, s2, op0, op1), [a, s1, s2], [out], vcost(out, a))
@@ -112,28 +124,34 @@ def declare(guess):
     def ms(out, c):
         add("V", "ms", (out, c), [], [out], vcost(out, out))
 
-    def scan(out, d0, d1):
-        add("V", "scan", (out, d0, d1), [d0, d1], [out], count(out))
+    def scan(out, d0, d1, first, op0, op1):
+        add("V", "scan", (out, d0, d1, first, op0, op1), [d0, d1, first], [out], max(64, count(out)))
 
-    def act(out, in_, func=AF.Identity, bias=0.0, scale=1.0):
+    def act(out, in_, func=AF.Identity, bias=0.0, scale=1.0, more=0):
         n = count(out)
-        cost = 80 + RHO * n if in_[0] == "@" else max(64, n) + (1500 if func == AF.Exp else 0)
-        add("S", "act", (out, in_, func, bias, scale), [in_, bias, scale], [out], cost)
+        cost = 80 + SCAT * n if out[0] == "@" else 80 + RHO * n if in_[0] == "@" else max(64, n)
+        add("S", "act", (out, in_, func, bias, scale), [in_, bias, scale], [out], cost + more)
 
-    def mms(items, **kw):
+    def silu(out, in_):
+        act(out, in_, AF.Silu)
+
+    def mms(items):
         rd = []
         for x in items:
             rd += [y for y in x[1:3] if y not in rd]
-        add("P", "mm", items, rd, [items[0][0]], sum(PEC * max(64, count(x[2])) * (4 if wide(x[1]) else 1) for x in items), **kw)
+        add("P", "mm", items, rd, [items[0][0]], sum(PEC * max(64, count(x[2])) * (4 if wide(x[1]) else 1) for x in items))
 
-    def mm(out, l, r, start=True, stop=True, **kw):
-        mms([(out, l, r, start, stop)], **kw)
+    def mm(out, l, r, start=True, stop=True):
+        mms([(out, l, r, start, stop)])
 
     def group(out, *pairs_):
         mms([(out, l, r, k == 0, k == len(pairs_) - 1) for k, (l, r) in enumerate(pairs_)])
 
-    def iota(out, pat, base, cm):
+    def iota(out, pat, base, cm=0):
         add("G", "iota", (out, pat, base, cm), [], [out], 160 + 2 * count(out))
+
+    def fill(out, c):
+        iota(out, [[0, count(out)]], c)
 
     nd = [0, 0]
 
@@ -145,8 +163,8 @@ def declare(guess):
     def P(b, lo, hi, step=1):
         return ("P%d" % b, lo, hi, step)
 
-    def diag(out, src, z, extra=None):
-        mms([(out, vw(z, 15 - r, 143 - r), vw(src, r, NT, 16), r == 0, r == 15 and extra is None) for r in range(16)]
+    def diag(out, src, z, extra=None, lo=0, hi=NT):
+        mms([(out, vw(z, 15 - r, 143 - r), vw(src, lo + r, hi, 16), r == 0, r == 15 and extra is None) for r in range(16)]
             + ([extra + (False, True)] if extra else []))
 
     dma("S", "load", ("obi", "ob", 0, 16), [], [vw("obi")], 8192)
@@ -162,92 +180,127 @@ def declare(guess):
     cp(vw("o0"), vw("obi"))
 
     col = lambda k: vw("cf", k, k + 1)
-    iota(vw("kq"), [[1, 144]], 0, 0)
+    bc = lambda k: vw("bc", k, k + 1)
+    iota(vw("kq"), [[1, 144]], 0)
     iota(vw("ci", 0, 1), [[1, 1]], 0, 1)
-    iota(vw("tab", 0, 256), [[1, 256]], 0, 0)
-    iota(vw("rli"), [[1, 8]], 0, 0)
-    iota(vw("kg"), [[16, 8], [0, 16]], 0, 0)
-    iota(vw("ia"), [[0, 8], [1, 16]], -15, 0)
+    iota(vw("kg"), [[16, 8], [0, 16]], 0)
+    iota(vw("tab"), [[1, NV]], 0)
     cp(col(0), vw("ci", 0, 1))
     ts(vw("cj", 0, 1), vw("ci", 0, 1), 15, A.bitwise_and)
     cp(col(1), vw("cj", 0, 1))
     tt(col(2), col(0), col(1), A.subtract)
     ts(col(3), col(2), 15.0, A.add)
     ts(col(4), col(2), 0.0625, A.mult)
-    ts(col(5), col(0), -1.0, A.add)
-    ts(col(6), col(1), 0.0, A.is_equal, 16.0, A.mult)
-    ts(col(7), col(0), 1.0, A.add)
-    ts(col(8), col(1), 15.0, A.is_equal, -16.0, A.mult)
-    ts(col(9), col(0), 0.0, A.is_equal)
-    for t in range(RO):
-        ts(col(10 + t), col(0), 1.0, A.is_equal, float(NB + NT * t), A.mult)
-    ts(col(13), col(0), 16.0, A.mult)
-    ts(col(16), col(0), 4.0, A.mult)
-    ms(col(14), 128 * LNB)
-    ms(col(15), -4095.0 / 8192)
+    k16 = vw("kq", 0, 16)
     kq = vw("kq", 0, 128)
-    for name, s in (("Ib", 1.0), ("Ih", 1.0), ("nIh", -1.0), ("I4k", 4096.0)):
+    ts(vw("bc"), k16, col(1), A.is_equal, 4096.0, A.mult)
+    ts(col(5), bc(0), 1.0 / 256, A.mult, col(0), A.add)
+    ts(col(5), col(5), -1.0, A.add)
+    ts(col(7), bc(15), -1.0 / 256, A.mult, col(0), A.add)
+    ts(col(7), col(7), 1.0, A.add)
+    ts(col(9), col(1), -2048.0, A.add)
+    ts(col(16), col(0), 4.0, A.mult)
+    for name, s in (("Ib", 1.0), ("Ih", 1.0), ("nI8k", -8192.0)):
         ts(vw(name), kq, col(0), A.is_equal, s, A.mult)
-    for name, s in (("If", 1.0), ("If4", 4096.0), ("BI", BIG), ("nBI", -BIG), ("hI", 0.5), ("qI", -0.25), ("mI", -128.0)):
+    for name, s in (("If", 1.0), ("nI26", -2.0 ** 26), ("nI23", -2.0 ** -23), ("I37", 2.0 ** 37)):
         act(vw(name), vw("Ib"), AF.Identity, 0.0, s)
+    for k in range(2):
+        act(vw("II", 128 * k, 128 * k + 128), vw("Ib"))
+    act(vw("nII"), vw("II"), AF.Identity, 0.0, -1.0)
     ts(vw("Bb"), vw("kg"), col(2), A.is_equal)
-    act(vw("nB"), vw("Bb"), AF.Identity, 0.0, -4096.0)
-    act(vw("B16"), vw("Bb"), AF.Identity, 0.0, 0.0625)
-    for name, k0, k1 in (("Rf", 5, 6), ("Rb", 7, 8)):
-        tt(col(k0), col(k0), col(k1), A.add)
-        ts(vw(name), kq, col(k0), A.is_equal)
-    for name, s in (("s2", 8192.0), ("sm", -4096.0), ("s16b", 0.0625)):
-        ts(vw(name), vw("kq", 0, 8), col(4), A.is_equal, s, A.mult)
+    ts(vw("B4k"), vw("Bb"), 4096.0, A.mult)
+    for k, s in enumerate((32.0, 2.0 ** 26, 1.0)):
+        act(vw("nB3", 128 * k, 128 * k + 128), vw("Bb"), AF.Identity, 0.0, -s)
+        ts(vw("s2", 8 * k, 8 * k + 8), vw("kq", 0, 8), col(4), A.is_equal, 2 * s, A.mult)
+    act(vw("sm"), vw("s2"), AF.Identity, 0.0, -0.5)
+    ts(vw("Rf"), kq, col(5), A.is_equal)
+    ts(vw("Rb"), kq, col(7), A.is_equal)
+    add("G", "sel", (vw("RI"), vw("Rf"), [[-1, 128]], A.not_equal, -1.0, 0, 1), [vw("Rf")], [vw("RI")], 460)
     ts(vw("Zb"), vw("kq"), col(3), A.is_equal)
     ts(vw("Zh"), vw("kq"), col(3), A.is_equal)
-    ms(vw("one"), 1.0)
-    ts(vw("oneh"), kq, 0.0, A.is_ge)
-    ts(vw("e16"), vw("kq", 0, 16), -128.0, A.mult, col(13), A.add)
-    cp(vw("kgb"), vw("kg"))
-    for q in range(16):
-        ts(vw("EE", 128 * q, 128 * q + 128), vw("kgb"), vw("e16", q, q + 1), A.is_equal)
-    ms(vw("d0"), -1.0)
-    ms(vw("d0", 0, NT, 16), 3.0e7)
-    cp(vw("rl"), vw("rli"))
-    ts(vw("iL"), vw("kq", 0, 16), 16.0, A.mult, col(1), A.add)
-    act(vw("wL"), vw("iL"), AF.Exp, col(14), -LNB)
-    ts(vw("thL"), vw("wL"), 40.0, A.mult)
-    ts(vw("c16i"), vw("iL", 0, 8), 16.0, A.mult, 15.0, A.add)
-    ts(vw("iH", 0, 8), vw("iL", 0, 8), 16.0, A.mult)
-    ts(vw("iH", 8, 16), vw("iL", 0, 8), 16.0, A.mult)
-    ts(vw("i16"), vw("iL"), 16.0, A.mult)
-    ts(vw("d15"), vw("iL"), float(NV), A.add)
-    ts(vw("d20"), vw("iL"), 2048.0, A.add)
-    for n in (256, 512, 1024):
-        act(vw("tab", n, 2 * n), vw("tab", 0, n), AF.Identity, float(n))
-    iota(vw("nx"), [[1, 2304]], 0, 0)
-    for t in range(RO):
-        ts(vw("nr", NT * t, NT * t + NT), vw("tab", 0, NT), col(9), A.mult, col(10 + t), A.add)
-    ts(vw("db1", 0, 3), vw("dri", 0, 3), -255.5, A.add)
-    ts(vw("db2", 0, 3), vw("dri", 0, 3), -128.0, A.add)
+    fill(vw("one"), 1)
+    ms(vw("m0", p=(0, 1)), 0.0)
+    ms(vw("m0", 0, 128, 16, p=(0, 1)), 1.0)
+    ms(vw("d0"), 0.0)
+    ms(vw("d0", 0, 128, 16), -3.0e7)
+    for h in range(2):
+        fill(vw("sc", 144 * h + 128, 144 * h + 144), 0)
+        fill(vw("st", 144 * h, 144 * h + 1), 1)
+    ms(vw("z16"), 0.0)
+    ts(vw("fa"), k16, col(1), A.is_ge, 1.0 / BETA, A.max)
+    scan(vw("fb"), vw("fa"), vw("z16"), BETA ** 64, A.mult, A.max)
+    ms(vw("fc"), BETA ** -16)
+    ms(vw("fc", 0, 1), BETA ** 64)
+    scan(vw("wL"), vw("fc"), vw("z16"), vw("fb", 15, 16), A.mult, A.max)
+    ts(vw("fd"), k16, col(1), A.is_lt, 1.0, A.add)
+    scan(vw("fe"), vw("fd"), vw("z16"), 0.5, A.mult, A.max)
+    ts(col(10), col(1), 10.5, A.is_lt, vw("fe", 15, 16), A.mult)
+    ts(col(10), bc(11), -0.25, A.mult, col(10), A.add)
+    ts(col(10), bc(12), 2.0 ** -13, A.mult, col(10), A.add)
+    ts(col(11), bc(10), bc(11), A.subtract, 2.0 ** -13, A.mult)
+    ts(col(12), bc(10), bc(11), A.add, -2.0 ** -13, A.mult)
+    ts(col(13), bc(8), 64.0, A.add)
+    act(vw("KW"), vw("Bb"), AF.Identity, 0.0, col(10))
+    act(vw("RW"), vw("Bb"), AF.Identity, 0.0, col(11))
+    act(vw("ZK"), vw("Zb"), AF.Identity, 0.0, col(10))
+    act(vw("Zq"), vw("Zb"), AF.Identity, 0.0, col(12))
+    ts(vw("sr"), vw("s2", 16, 24), col(11), A.mult, 8.0, A.mult)
+    ts(vw("bits", 0, 1), bc(9), bc(10), A.add)
+    for k in range(8):
+        act(vw("bits", 2 ** k, 2 ** (k + 1)), vw("bits", 0, 2 ** k), AF.Identity, bc(k))
+    fill(vw("cl"), 0)
+    for p, c in ((0, 2.0 ** 17), (32, 1.0), (64, -2.0 ** 25), (96, 2112 * 2.0 ** 26)):
+        ms(vw("cl", p=(p, p + 1)), c)
+    iota(vw("cr", 0, 128), [[0, 8], [1, 16]], 0)
+    iota(vw("cr", 0, 128, p=(0, 32)), [[-1, 8], [0, 16]], 7)
+    ms(vw("cr", 0, 128, p=(64, 128)), 0.0)
+    fill(vw("cr", 128, 256), 0)
+    ms(vw("cr", 128, 256, p=(64, 128)), 1.0)
+    fill(vw("tl"), 0)
+    iota(vw("tl", p=(0, 1)), [[0, 8], [1, 16]], 0)
+    for p, c in ((32, 1.0), (64, -2048.0), (96, 1.0)):
+        ms(vw("tl", p=(p, p + 1)), c)
+    iota(vw("tr"), [[1, NT]], 0)
+    fill(vw("tr", p=(0, 1)), 8192)
+    ms(vw("tr", p=(64, 65)), 8192.0)
+    mm(P(0, 256, 384), vw("cl", p=(0, 64)), vw("cr", 0, 128, p=(0, 64)))
+    for h in range(2):
+        act(vw("cT", 128 * h, 128 * h + 128), P(0, 256, 384))
+    ts(vw("iL"), k16, 16.0, A.mult, col(1), A.add)
+    ts(vw("c16i"), vw("iL", 0, 8), 16.0, A.mult, 2048.0, A.add)
+    fill(vw("ld"), 0)
+    fill(vw("nd"), 0)
+    ts(vw("ld", 1, 32, 2), vw("iL"), float(NV), A.add)
+    ts(vw("wd", 1, 32, 2), vw("iL"), float(SO + NV), A.add)
+    ts(vw("yc"), vw("iL"), float(8 + NT), A.add)
+    ts(vw("db1", 0, 3), vw("dri", 0, 3), -1.0, A.mult, 256.0, A.add)
+    cp(vw("db2", 0, 3), vw("dri", 0, 3))
     ts(vw("db3", 0, 3), vw("dri", 0, 3), -1.0, A.mult)
-    for name, lo, n in (("xx0", 128, 128), ("xx1", 128, 128), ("rct", NV, NT), ("sht", NV, NT), ("bh0", 2048, 2048), ("bh1", 2048, 2048)):
-        iota(vw(name, lo, lo + n), [[0, n]], 0, 0)
-    ms(vw("hh", 0, 8), 0.0)
-    cp(vw("shph"), vw("shpi"), rows=32)
+    fill(vw("eb", 0, SO), 64)
+    fill(vw("eb", SO + S0 + NT, EW), 64)
+    fill(vw("rct", NV, NV + NT), 0)
+    fill(vw("sht", NV, NV + NT), 0)
+    fill(vw("hy", 0, 8), 0)
+    cp(vw("shph", p=(0, 32)), vw("shpi", p=(0, 32)))
     ts(vw("e4"), vw("kq", 0, 4), -4.0, A.mult, col(16), A.add)
     for k in range(4):
         ts(vw("sq", 128 * k, 128 * k + 128), vw("kg"), vw("e4", k, k + 1), A.is_equal)
-        mm(P(4 + k, 0, 384), vw("sq", 128 * k, 128 * k + 128), vw("shph"), rows=32)
-        act(vw("sht", 384 * k, 384 * k + 384), P(4 + k, 0, 384))
+        mm(P(4 + k, 0, 384), vw("sq", 128 * k, 128 * k + 128, p=(0, 32)), vw("shph", p=(0, 32)))
+        act(vw("sht", 384 * k, 384 * k + 384), P(4 + k, 0, 384), AF.Identity if k or allv else AF.Silu, float(SO), 1.0, 0 if k or allv else 1560)
     for k in range(3):
         cp(vw("rct", 512 * k, 512 * k + 512), vw("reci", 512 * k, 512 * k + 512))
     for k in range(2):
-        cp(vw("hh", 8 + 512 * k, 520 + 512 * k), vw("bndi", 512 * k, 512 * k + 512))
+        ts(vw("eb", SO + 512 * k, SO + 512 * k + 512), vw("bndi", 512 * k, 512 * k + 512), 64.0, A.add)
 
-    def pairs(eq, W, Lf, wt, Sb):
+    def pairs(eq, W, Lf, wt, Sb, end):
         at = 0
-        for m in range(16):
-            n = NT - 16 * m
-            ts(vw(eq, at, at + n), vw(W, 16 * m, NT), vw(Lf, m, m + 1), A.is_equal, vw(wt, m, m + 1), A.mult)
-            mm(P(6, 16 * m, NT), vw("Bb"), vw(eq, at, at + n), m == 0, m == 15)
+        for k, m in enumerate([8 * h + x for h in HS for x in range(8)]):
+            n = end(m) - 16 * m
+            ts(vw(eq, at, at + n), vw(W, 16 * m, end(m)), Lf(m), A.is_equal, vw(wt, m, m + 1), A.mult)
+            cuts = (0, 128, n) if m == 0 and n > 128 else (0, n)
+            mms([(P(6, 16 * m + x, 16 * m + y), vw("Bb"), vw(eq, at + x, at + y), k == 0, k == 15) for x, y in zip(cuts, cuts[1:])])
             at += n
-        act(vw(Sb), P(6, 0, NT))
+        act(vw(Sb), P(6, 0, NT), AF.Identity, 0.0, 1.0 / 40)
         diag(P(6, 256, 272), Sb, "Zb")
 
     for t in range(RO):
@@ -255,10 +308,8 @@ def declare(guess):
         rot = t > 0
         hw = lambda name, h: vw(name, 128 * h, 128 * h + 128)
         hl_ = lambda name, h: vw(name, 8 * h, 8 * h + 8)
-        nW = "nW" if rot else "sW"
-        nLf = "nLf" if rot else "sLf"
-        xs = lambda h: hw("xs", h) if rot else vw("xx%d" % h, 0, 128)
         bias = lambda name: vw(name, t, t + 1)
+        fill(vw("tr", p=(96, 97)), NB + NT * t)
         if rot:
             for h in range(2):
                 add("X", "recv", ("ao%d%d" % (t - 1, h),), [], [hl_(o, h)], 0, after=("so", t - 1, h))
@@ -266,164 +317,169 @@ def declare(guess):
             dma("Q", "store", ("yh", "yo%d" % (t - 1), NT * (t - 1), 0, NT), [vw("yo%d" % (t - 1)), vw(v)], [], 131072)
 
         def lists(h):
-            if t == 0:
-                ts(hw("c32", h), ind(vw("reci"), hl_(o, h)), 4095, A.bitwise_and)
-            else:
-                cp(hw("xi", h), ind(vw("rct", 0, NV), hl_(o, h)))
-                ts(hw("c32", h), hw("xi", h), 4095, A.bitwise_and)
+            cp(hw("xi", h), ind(vw("rct", 0, NV) if rot else vw("reci"), hl_(o, h)))
+            ts(hw("c32", h), hw("xi", h), 4095, A.bitwise_and)
+            ts(hw("p32", h), hw("xi", h), 12, A.arith_shift_right)
             cp(hw("c16", h), hw("c32", h))
-            act(vw("xx%d" % h, 0, 128), ind(vw("rct", 0, NV), hl_(o, h)))
-            mm(P(2 + h, 128, 256), hw(v, h), vw("Ib"))
-            act(hw("vT", h), P(2 + h, 128, 256))
-            act(vw("bh%d" % h, 2063, 4096, 16), hw(v, h), AF.Identity, bias("db3"))
 
         def main(h):
-            bh, mx = "bh%d" % h, "mx%d" % h
-            mm(P(2 + h, 0, 128), hw(v, h), vw("nB"), True, False)
-            for q in range(4):
-                act(vw(bh, 512 * q, 512 * q + 512), ind(vw("boxt", 0, NB + NT * t), vw("c16", 128 * h + 32 * q, 128 * h + 32 * q + 32)))
-                mm(P(q % 2, 0, 512), hw("vT", h), vw("EE", 512 * q, 512 * q + 512))
-                tt(vw(mx, 512 * q, 512 * q + 512), vw(bh, 512 * q, 512 * q + 512), P(q % 2, 0, 512), A.max)
-            mms([(P(2 + h, a, 128, 16), vw(bh, a, 2048, 16), vw("sm"), False, False) for a in range(16)])
-            mms([(P(2 + h, a, 128, 16), vw(mx, a, 2048, 16), vw("s2"), False, a == 15) for a in range(16)])
+            bh = "bh%d" % h
+            e = 2 + h
 
-        def shapes():
-            ps, pn, pq, p7 = P(5, 256, 272), P(5, 272, 288), P(5, 288, 304), P(7, 256, 512)
-            cp(vw("sW"), ind(vw("sht", 0, NV), vw(o)))
-            diag(ps, "sW", "Zh")
-            ts(vw("s16"), ps, 0.0625, A.mult)
-            act(vw("sLf"), ps, AF.Identity, 0.0, 1.0 if rot else 0.0625)
-            if rot:
-                for h in range(2):
-                    mm(P(7, 256, 384), vw("Rf"), vw("xx%d" % h, 0, 128))
-                    act(vw("xx%d" % h, 256, 384), P(7, 256, 384))
-                cp(vw("nW"), ind(vw("nx", 0, 2048), vw("s16")))
-                diag(pn, "nW", "Zh")
-                tt(vw("rL"), vw("sLf"), pn, A.not_equal)
-                ts(vw("r2L"), vw("rL"), 4096.0, A.mult)
-                tt(vw("t1"), vw("r2L"), pn, A.add)
-                ts(vw("hl"), vw("t1"), 0.0625, A.mult)
-                act(vw("nLf"), pn, AF.Identity, 0.0, 0.0625)
-                tt(vw("t2"), vw("iH"), vw("r2L"), A.add)
-                ts(vw("xsl"), vw("t2"), 0.0625, A.mult)
-                group(p7, (vw("Ih"), vw("nW")), (vw("nIh"), vw("sW")))
-                act(vw("rotW"), p7, AF.Sign)
-                mms([(P(7, 8 * h, 8 * h + 8), hw("rotW", h), vw("s16b"), True, True) for h in range(2)])
-                act(vw("d0", 1, NT, 16), P(7, 0, 16), AF.Identity, -1.0, 16.0)
-                for h in range(2):
-                    group(P(7, 128 * h, 128 * h + 128), (hw("rotW", h), vw("B16")), (vw("Ib"), vw("ia")))
-                act(vw("iar"), P(7, 0, NT))
-                act(vw("hn"), ind(vw("hh", 8, 8 + HB[t]), vw("hl")))
-            else:
-                cp(vw("hn"), ind(vw("bndi"), vw("s16")))
-            mms([(P(7, 128 * h, 128 * h + 128), hw("hn", h), vw("If4"), True, True) for h in range(2)])
-            act(vw("hnT"), P(7, 0, NT))
-            for h in range(2):
+            def bounds():
+                mm(P(e, 128, 256), hw("hn", h), vw("nI26"), False, False)
                 if rot:
-                    cp(hw("xs", h), ind(vw("xx%d" % h), hl_("xsl", h)))
-                act(hw("xq", h), xs(h), AF.Identity, col(15), 1.0 / 4096)
-            ts(vw("p16"), vw("xq"), MAGIC, A.add, -MAGIC, A.add)
+                    mms([(P(e, 128, 256), hw("sgW", h), vw("I37"), False, False), (P(e, 0, 128, 16), hw("sgW", h), vw("sr"), False, False)])
+
+            mm(P(h, 0, 128), vw("Ib"), hw(v, h))
+            rows = (0, 128 if rot else 96)
+            mms([(P(e, 0, 384), hw(v, h), vw("nB3"), True, False), (P(e, 0, 256), vw("cl", p=rows), vw("cr", p=rows), False, False)])
+            for lo, hi, on in CUT[t][HS.index(h)]:
+                (cp if on else act)(vw(bh, 16 * lo, 16 * hi), ind(vw("boxt", 0, NB + NT * t), vw("c16", 128 * h + lo, 128 * h + hi)))
+            if rot and h == HS[1]:
+                bounds()
+            mms([(P(e, a, 384, 16), vw(bh, a, 2048, 16), vw("sm"), False, False) for a in range(16)])
+            if rot and h == HS[0]:
+                bounds()
+            for k in range(0, 128, CH):
+                for q in range(4):
+                    calls = [(vw(bh, 2048 + 128 * a + k, 2048 + 128 * a + k + CH), vw(bh, 16 * k + a, 16 * (k + CH), 16), P(h, k, k + CH), A.max)
+                             for a in range(4 * q, 4 * q + 4)]
+                    add("V", "tt", calls, [vw(bh, 16 * k, 16 * (k + CH)), P(h, k, k + CH)], [x[0] for x in calls], 4 * max(64, CH))
+            for q in range(4):
+                if q == 3 and not rot:
+                    bounds()
+                mms([(P(e, a, 384, 16), vw(bh, 2048 + 128 * a, 2176 + 128 * a), vw("s2"), False, a == 15) for a in range(4 * q, 4 * q + 4)])
+            act(vw(bh, 2048, 4096, 16), hw(v, h), AF.Identity, bias("db3"))
+
+        def shapes(h):
+            if not ON["split"][t] and h == HS[1]:
+                return
+            hs = (h,) if ON["split"][t] else HS
+            lo, hi = min(hs), max(hs) + 1
+            W = lambda name, step=1: vw(name, 128 * lo, 128 * hi, step)
+            L = lambda name: vw(name, 8 * lo, 8 * hi)
+            ps = P(4 + h, 272, 272 + 8 * (hi - lo))
+            cp(W("sW"), ind(vw("sht", 0, NV), L(o)))
+            diag(ps, "sW", "Zh", None, 128 * lo, 128 * hi)
+            ts(L("s16"), ps, 0.0625, A.mult, 0.0 if rot else -float(SO), A.add)
+            act(L("sLf"), ps, AF.Identity, 0.0, 0.0625)
+            if not rot:
+                cp(W("hn"), ind(vw("bndi"), L("s16")))
+                return
+            act(W("hn"), ind(vw("eb", 0, SO + S0 + NT), L("s16")))
+            act(W("sgW"), W("hn"), AF.Sign, -4152.0)
+            for k in hs:
+                group(P(7, 8 * k, 8 * k + 8), (hw("sgW", k), vw("sr")), (vw("cl", p=(0, 32)), vw("cr", 0, 128, 16, p=(0, 32))))
+            act(W("cT", 16), P(7, 8 * lo, 8 * hi))
+            if HS[1] not in hs:
+                return
+            pk = P(7, 16, 32)
+            mm(P(7, 256, 512), vw("RW"), vw("sgW"))
+            diag(pk, "sgW", "ZK")
+            act(vw("rotW"), P(7, 256, 512))
+            tt(vw("nLf"), vw("sLf"), pk, A.max)
+            ts(vw("t3"), pk, 0.0, A.is_gt, -float(NT), A.mult)
+            tt(vw("ycol"), vw("t3"), vw("yc"), A.add)
+            mm(P(7, 256, 512), vw("KW"), vw("sgW"))
+            tt(vw("nF" if t == 1 else "nW"), vw("sW"), P(7, 256, 512), A.max)
             if t == 1:
-                act(vw("r256"), vw("rotW"), AF.Identity, 0.0, 256.0)
-            if t == 2:
-                cp(vw("n16"), vw("nLf"))
-                tt(vw("nq"), ind(vw("nx", 0, 2048), vw("n16")), vw("nW"), A.is_equal)
-                diag(pq, "nq", "Zh")
-                tt(vw("nqL"), vw("wL"), pq, A.mult)
-                ts(vw("nqL"), vw("nqL"), 0.0625, A.mult)
+                cp(vw("yc16"), vw("ycol"))
 
         def owners():
-            cp(vw("oW"), ind(vw("tab", 0, NV), vw(o)))
-            cp(vw("oLf"), vw(o))
-            pairs("eqo", "oW", "oLf", "wL", "So")
-            tt(vw("lo1"), vw("thL"), P(6, 256, 272), A.is_le)
-            tt(vw("lo2"), vw("lo1"), vw("d15"), A.mult)
-            tt(vw("lo3"), vw("lo2"), vw("oLf"), A.max)
-            cp(vw("ol"), vw("lo3"))
+            cp(vw("oW"), ind(vw("tab"), vw(o)))
+            cp(vw("lo", 1, 32, 2), vw(o))
+            pairs("eqo", "oW", lambda m: vw("lo", 2 * m + 1, 2 * m + 2), "wL", "So", lambda m: 128 * (m // 8 + 1))
+            tt(vw("lo", 0, 32, 2), vw("wL"), P(6, 256, 272), A.is_le)
+            scan(vw("lp"), vw("ld"), vw("lo"), 0.0, A.mult, A.max)
+            cp(vw("ol"), vw("lp", 1, 32, 2))
+            if t == 1:
+                for h in HS:
+                    (cp if ON["sht"] else silu)(ind(vw("sht"), hl_("ol", h)), hw("nF", h))
+            if t == 2:
+                cp(vw("n16"), vw("nLf"))
+                act(vw("nsg"), ind(vw("eb", 0, SO + NV), vw("n16")), AF.Sign, -4152.0)
+                diag(P(6, 272, 288), "nsg", "Zq")
+                tt(vw("nqL"), vw("wL"), P(6, 272, 288), A.mult)
 
         def choose(h):
-            e = P(2 + h, 0, 128)
+            e, w = 2 + h, 4 + h
             dg = "dg%d" % h
-            tt(hw("nf", h), hw("hnT", h), e, A.is_lt)
-            tt(hw("uu", h), hw("nf", h), e, A.mult)
-            scan(hw("sc", h), hw("d0", h), hw("uu", h))
-            ends = vw("sc", 128 * h + 15, 128 * h + 128, 16)
-            ts(hl_("u4", h), ends, MAGIC * 4096, A.add, -MAGIC * 4096, A.add)
-            wa = vw("cwa", 16 * h, 16 * h + 8)
-            wc = vw("cwc", 16 * h, 16 * h + 8)
-            tt(wa, ends, hl_("u4", h), A.subtract)
-            if rot:
-                ts(hl_("w16", h), ends, 1.0, A.is_equal, -16.0, A.mult)
-                tt(wc, ends, hl_("w16", h), A.add)
-            else:
-                cp(wc, ends)
-            tt(hw("ohT", h), ind(wa, vw("rl")), hw("iar", h) if rot else vw("ia"), A.is_equal)
-            act(hw("rpT", h), ind(wc, vw("rl")))
-            mm(P(4, 0, 128), hw("ohT", h), vw("Ib"))
-            mm(P(4, 128, 256), hw("rpT", h), vw("Ib"))
-            tt(vw(dg, 0, 128), hw("p16", h), P(4, 0, 128), A.mult)
-            ts(vw(dg, 128, 256), P(4, 128, 256), 0.0625, A.mult, 128.0, A.min)
-            diag(P(4, 256, 272), dg, "Zh", (P(4, 264, 272), vw("Ih"), vw("c16i")))
+            st = lambda k: vw("st", 144 * h + k, 144 * h + k + 128)
+            tt(hw("rp", h), hw("cT", h), P(e, 128, 256), A.max)
+            sc = lambda k: vw("sc", 144 * h + k, 144 * h + k + 128)
+            scan(sc(0), hw("rp", h), P(e, 0, 128), 3.0e7, A.min, A.min)
+            act(hw("eS", h), P(e, 256, 384))
+            scan(P(h, 128, 256), vw("d0"), sc(15), 0.0, A.add, A.max)
+            tt(st(1), sc(0), P(h, 128, 256), A.is_equal)
+            mm(P(w, 0, 256), vw("m0", p=(0, 1)), vw("one", p=(0, 1)), True, False)
+            mm(P(w, 128, 256), hw("rp", h), vw("nI23"), False, False)
+            mms([(P(w, 0, 256), st(1), vw("II"), False, False), (P(w, 0, 256), st(0), vw("nII"), False, True)])
+            tt(vw(dg, 0, 128), hw("p32", h), P(w, 0, 128), A.mult)
+            ts(vw(dg, 128, 256), P(w, 128, 256), 0.5, A.is_gt, col(9), A.mult)
+            diag(P(w, 256, 272), dg, "Zh", (P(w, 264, 272), vw("Ih"), vw("c16i")))
             ox = "ox%d" % (2 * t + h)
-            cp(vw(ox), P(4, 256, 272))
+            cp(vw(ox), P(w, 256, 272))
             if t < 2:
                 add("G", "send", (vw(ox, 0, 8), hl_("o%d" % (t + 1), h), "ao%d%d" % (t, h)), [vw(ox, 0, 8)], [],
-                    900 + (2000 if t + h == 0 else 0), tag=("so", t, h))
-            ts(hl_("nhL", h), P(4, 264, 272), 2048.0, A.is_ge)
+                    900 + (2000 if (t, h) == (0, HS[0]) else 0), tag=("so", t, h))
+            ts(hl_("nhL", h), P(w, 264, 272), 2048.0, A.is_ge)
+            tt(hl_("akw", h), hl_("nhL", h), hl_("nqL" if t == 2 else "wL", h), A.mult)
             act(hw("XX", h), ind(vw("bh%d" % h), vw(ox, 8, 16)))
-            act(hw("sg", h), hw("XX", h), AF.Sign, bias("db1"))
-            group(P(2 + h, 128, 256), (vw("Ib"), hw("XX", h)), (vw("mI"), hw("sg", h)))
-            act(hw(vs, h), P(2 + h, 128, 256), AF.Identity, bias("db2"))
+            ts(hw("sg", h), hw("XX", h), bias("db1"), A.is_ge, -256.0, A.mult)
+            group(P(h, 256, 384), (vw("Ib"), hw("XX", h)), (vw("Ib"), hw("sg", h)))
+            act(hw(vs, h), P(h, 256, 384), AF.Identity, bias("db2"))
             if t < 2:
                 add("G", "send", (hw(vs, h), hw("v%d" % (t + 1), h), "av%d%d" % (t, h)), [hw(vs, h)], [], 900, tag=("sv", t, h))
-            act(hw("nhT", h), hw("rpT", h), AF.Relu)
-            group(P(5, 128, 256), (hw("ohT", h), vw("BI")), (vw("one"), vw("nBI")), (hw("nhT", h), vw("nBI")), (vw("I4k"), hw("p16", h)),
-                  (vw("oneh"), vw("nr", NT * t + 128 * h, NT * t + 128 * h + 128)))
-            act(hw("tp", h), P(5, 128, 256))
-            tt(ind(vw("rct"), hl_("ol", h)), xs(h), hw("tp", h), A.max)
+            group(P(e, 384, 512), (vw("tl"), hw("tr", h)), (vw("nI8k"), vw(dg, 128, 256)), (vw("B4k"), vw(dg, 0, 128)))
+            tt(hw("yy", h), hw("xi", h), P(e, 384, 512), A.max)
+            if rot:
+                mm(P(e, 0, 128), vw("RI"), hw("yy", h))
+                tt(hw("zz", h), hw("rotW", h), P(e, 0, 128), A.mult)
+                tt(ind(vw("rct"), hl_("ol", h)), hw("yy", h), hw("zz", h), A.add)
+            else:
+                cp(ind(vw("rct"), hl_("ol", h)), hw("yy", h))
             if t < 2:
-                group(P(2 + h, 256, 384), (vw("hI"), hw("XX", h)), (vw("hI"), hw(v, h)), (vw("one"), vw("qI")))
-                act(hw("bt", h), P(2 + h, 256, 384), AF.Identity, MAGIC)
+                group(P(w, 0, 128), (vw("Ib"), hw("XX", h)), (vw("Ib"), hw(v, h)))
+                act(hw("bt", h), P(w, 0, 128), AF.Identity, MAGIC, 0.5 - 2.0 ** -11)
                 act(vw("boxt", NB + NT * t + 128 * h, NB + NT * t + 128 * h + 128), hw("bt", h), AF.Identity, -MAGIC)
-            tt(hl_("akw", h), hl_("nhL", h), hl_("nqL" if t == 2 else "wL", h), A.mult)
 
         def makers():
-            if t == 1:
-                cp(ind(vw("sht"), vw("ol")), vw("nW"))
-            c1 = 8 + HB[t] + (256 if rot else 0)
+            yo = vw("yo%d" % t)
+            hs = vw("hy", 8 + NT, 8 + 2 * NT) if rot else vw("eb", SO + S0, SO + S0 + NT)
+            mms([(P(7, 128 * h, 128 * h + 128), hw("eS", h), vw("If"), True, True) for h in range(2)])
+            act(hs, P(7, 0, NT), AF.Identity, 0.0 if rot else 64.0)
             if rot:
-                tt(vw("t3"), vw("i16"), vw("r2L"), A.subtract)
-                act(vw("ycol"), vw("t3"), AF.Identity, float(c1), 0.0625)
+                mm(P(7, 256, 512), vw("Rf"), hs)
+                act(vw("hy", 8, 8 + NT), P(7, 256, 512))
+                if t == 1:
+                    (cp if ON["seen"] else act)(vw("seen"), ind(vw("hy"), vw("yc16")))
+                    group(P(7, 0, NT), (vw("Rb"), vw("seen")), (vw("Ib"), vw("bits")))
+                    act(vw("dat"), P(7, 0, NT), AF.Identity, col(13))
             else:
-                ts(vw("ycol"), vw("iL"), float(c1), A.add)
-            mms([(P(7, 128 * h, 128 * h + 128), hw("uu", h), vw("If"), True, True) for h in range(2)])
-            act(vw("hh", c1, c1 + NT), P(7, 0, NT), AF.Identity, 0.0, 1.0 / 4096)
-            if rot:
-                mm(P(7, 256, 512), vw("Rf"), vw("hh", c1, c1 + NT))
-                act(vw("hh", c1 - NT, c1), P(7, 256, 512))
-            if t < 2:
-                mm(P(7, 0, NT), vw("Rb"), vw("hh", c1, c1 + NT))
-                act(vw("hh", c1 + NT, c1 + 2 * NT), P(7, 0, NT))
-            pairs("eqn", nW, nLf, "akw", "Sn")
-            ts(vw("thA"), vw("akw"), 40.0, A.mult)
-            tt(vw("wn"), vw("thA"), P(6, 256, 272), A.is_gt)
-            if t < 2:
-                tt(vw("ln1"), vw("thA"), P(6, 256, 272), A.is_le)
-                tt(vw("ln2"), vw("ln1"), vw("d20"), A.mult)
-                tt(vw("ln3"), vw("ln2"), vw(nLf), A.max)
-                cp(vw("nl"), vw("ln3"))
-                if t == 0:
-                    cp(ind(vw("nx"), vw("nl")), vw("tab", 1024, 1280))
-                else:
-                    tt(ind(vw("nx"), vw("nl")), vw("tab", 1792, 2048), vw("r256"), A.subtract)
-            tt(vw("y1"), vw("wn"), vw("ycol"), A.mult)
+                ts(vw("ycol"), vw("iL"), float(SO + S0), A.add)
+                group(P(7, 256, 512), (vw("Rb"), hs), (vw("Ib"), vw("bits")))
+                act(vw("dat"), P(7, 256, 512))
+            key = "n" if t == 2 else "s"
+            pairs("eqn", key + "W", lambda m: vw(key + "Lf", m, m + 1), "akw", "Sn", lambda m: NT)
+            wn = vw("wd", 0, 32, 2)
+            tt(wn, vw("akw"), P(6, 256, 272), A.is_gt)
+            tt(vw("y1"), wn, vw("ycol"), A.mult)
             cp(vw("yl"), vw("y1"))
-            act(vw("yo%d" % t), ind(vw("hh", 0, c1 + NT), vw("yl")))
-            if t == 2:
-                dma("Q", "store", ("yh", "yo2", NT * t, 0, NT), [vw("yo2")], [], 131072)
+            if rot:
+                (cp if ON["yo"][t] else act)(yo, ind(vw("hy"), vw("yl")))
+            else:
+                act(yo, ind(vw("eb", 0, SO + S0 + NT), vw("yl")), AF.Identity, -64.0)
+            if t < 2:
+                tt(vw("nd", 1, 32, 2), vw("nLf" if rot else "sLf"), vw("wd", 1, 32, 2), A.subtract)
+                scan(vw("ln"), vw("nd"), vw("wd"), 0.0, A.mult, A.add)
+                cp(vw("nl"), vw("ln", 1, 32, 2))
+                (cp if ON["eb"][t] else silu)(ind(vw("eb"), vw("nl")), vw("dat"))
+            else:
+                dma("Q", "store", ("yh", "yo2", NT * t, 0, NT), [yo], [], 131072)
 
-        for name, fn, h in (("l0", lists, 0), ("l1", lists, 1), ("m0", main, 0), ("s0", shapes, None), ("oo", owners, None),
-                            ("m1", main, 1), ("c0", choose, 0), ("c1", choose, 1), ("kk", makers, None)):
+        for name, fn, h in (("l0", lists, HS[0]), ("l1", lists, HS[1]), ("s0", shapes, HS[0]), ("m0", main, HS[0]), ("s1", shapes, HS[1]),
+                            ("oo", owners, None), ("m1", main, HS[1]), ("c0", choose, HS[0]), ("c1", choose, HS[1]), ("kk", makers, None)):
             part[0] = "%s%d" % (name, t)
             if h is None:
                 fn()
@@ -433,6 +489,12 @@ def declare(guess):
     dma("Q", "store", ("yr", "rct", 0, 0, 768), [vw("rct", 0, 768)], [], 393216)
     dma("S", "store", ("yr", "rct", 768, 768, 768), [vw("rct", 768, NV)], [], 393216)
     return ops, link(ops, HOP, NET)
+
+
+def meet(x, y):
+    if x[1] >= y[2] or y[1] >= x[2] or (x[3] == y[3] == 2 and (x[1] - y[1]) % 2):
+        return False
+    return len(x) < 5 or len(y) < 5 or (x[4][0] < y[4][1] and y[4][0] < x[4][1])
 
 
 def link(ops, hop, net):
@@ -451,15 +513,17 @@ def link(ops, hop, net):
                 if op["eng"] == "P":
                     op["soft"] = set(now[-1:])
                 phase[x[0]] = (before, now + [i])
-                continue
+                if op["eng"] == "P":
+                    continue
             for j, y, wj in last.get(x[0], []):
-                if j != i and x[1] < y[2] and y[1] < x[2] and (w or wj):
+                if j != i and (w or wj) and meet(x, y):
                     deps.add(j)
         for x, w in sides:
-            if x[0][0] == "P":
+            if x[0][0] == "P" and op["eng"] == "P":
+                last[x[0]] = []
                 continue
             old = last.get(x[0], [])
-            if w and x[3] == 1:
+            if w and x[3] == 1 and len(x) < 5:
                 old = [z for z in old if not (x[1] <= z[1][1] and z[1][2] <= x[2])]
             last[x[0]] = old + [(i, x, w)]
         op["deps"] = deps
@@ -505,32 +569,6 @@ def place(cost, eng, before, key):
     return t0
 
 
-def run(order, eng, cost, lat, pre):
-    n = len(cost)
-    free = [0.0] * 6
-    last = [-1] * 6
-    t = [0.0] * n
-    why = [0] * n
-    end = 0.0
-    top = 0
-    for i in order:
-        e = eng[i]
-        s = free[e]
-        w = -2 - last[e]
-        for j, l in pre[i]:
-            if t[j] + l >= s:
-                s = t[j] + l
-                w = j
-        why[i] = w
-        s += cost[i]
-        t[i] = free[e] = s
-        last[e] = i
-        if s + lat[i] > end:
-            end = s + lat[i]
-            top = i
-    return end, why, top
-
-
 def arrange(plans, rounds, seed):
     ops, pre = plans[0]
     n = len(ops)
@@ -542,32 +580,53 @@ def arrange(plans, rounds, seed):
         state[0] = (state[0] * 1103515245 + 12345) % 2147483648
         return (state[0] >> 8) % k
 
-    cost, lat, _ = tabs[0]
-    succ = [[] for _ in ops]
-    for i, p in enumerate(pre):
-        for j, l in p:
-            succ[j].append((i, l))
-    tail = [0.0 if succ[i] else lat[i] for i in range(n)]
-    prio = [0.0] * n
-    for i in range(n - 1, -1, -1):
-        prio[i] = cost[i] + max([l + prio[k] for k, l in succ[i]] + [tail[i]])
-    best = place(cost, eng, pre, [-p for p in prio])
-    length = lambda t0: max(t0[i] + cost[i] + tail[i] for i in range(n))
-    back = [succ[i] + [(n, tail[i])] for i in range(n)] + [[]]
-    for _ in range(100):
-        w = rnd(1000) + 1
-        tb = place(cost + [0.0], eng + [5], back, [rnd(w) - best[i] - cost[i] - tail[i] for i in range(n)] + [-1e18])
-        t0 = place(cost, eng, pre, [-tb[i] - cost[i] for i in range(n)])
-        if length(t0) < length(best):
-            best = t0
+    cost = tabs[0][0]
+    key = [None] * n
+    for rank, goal in enumerate(GOALS):
+        far = {i: cost[i] for i in range(n) if ops[i]["part"] in goal and key[i] is None}
+        for i in range(n - 1, -1, -1):
+            if i in far:
+                for j, l in pre[i]:
+                    if key[j] is None:
+                        far[j] = max(far.get(j, 0), far[i] + l + cost[j])
+        for i, d in far.items():
+            key[i] = (rank, -d)
+    best = place(cost, eng, pre, [k or (len(GOALS), i) for i, k in enumerate(key)])
     cur = sorted(range(n), key=lambda i: (best[i], i))
     above = [set(j for j, l in p) for p in pre]
-    res = [run(cur, eng, *tb) for tb in tabs]
+    below = [set() for _ in ops]
+    for i, p in enumerate(pre):
+        for j, l in p:
+            below[j].add(i)
+    ends = [i for i in range(n) if not below[i]]
+
+    def run(order, a, old, cost, lat, pre):
+        t, why = (list(old[3]), list(old[1])) if old else ([0.0] * n, [0] * n)
+        last = [-1] * 6
+        for i in order[:a]:
+            last[eng[i]] = i
+        free = [t[i] if i >= 0 else 0.0 for i in last]
+        for i in order[a:]:
+            e = eng[i]
+            s = free[e]
+            w = -2 - last[e]
+            for j, l in pre[i]:
+                x = t[j] + l
+                if x >= s:
+                    s = x
+                    w = j
+            why[i] = w
+            t[i] = free[e] = s + cost[i]
+            last[e] = i
+        top = max(ends, key=lambda i: t[i] + lat[i])
+        return t[top] + lat[top], why, top, t
+
+    res = [run(cur, 0, None, *tb) for tb in tabs]
     unit = [r[0] for r in res]
     now = low = float(len(res))
     keep = cur
     for k in range(rounds):
-        _, why, i = res[rnd(len(res))]
+        _, why, i, _ = res[rnd(len(res))]
         held = []
         while why[i] != -1:
             if why[i] < -1:
@@ -579,36 +638,68 @@ def arrange(plans, rounds, seed):
             continue
         i, j = held[rnd(len(held))]
         a = cur.index(j)
-        for _ in range((0, 0, 0, 1, 2, 4)[rnd(6)]):
-            p = a - 1
-            while p >= 0 and eng[cur[p]] != eng[i]:
-                p -= 1
-            if p >= 0:
-                a = p
         b = cur.index(i)
-        need = set(above[i])
-        moved = [i]
-        for x in cur[b - 1:a:-1]:
-            if x in need:
-                moved.append(x)
-                need |= above[x]
-        if cur[a] in need:
-            continue
-        inside = set(moved)
-        new = cur[:a] + moved[::-1] + [x for x in cur[a:b] if x not in inside] + cur[b + 1:]
-        r = [run(new, eng, *tb) for tb in tabs]
-        v = sum(x[0] / u for x, u in zip(r, unit))
-        heat = 0.0015 * (1.0 - k / rounds) + 0.0001
-        if v <= now or rnd(1000) < 1000 * math.exp((now - v) / heat):
+        if rnd(2):
+            for _ in range((0, 0, 0, 1, 2, 4)[rnd(6)]):
+                p = a - 1
+                while p >= 0 and eng[cur[p]] != eng[i]:
+                    p -= 1
+                if p >= 0:
+                    a = p
+            need = set(above[i])
+            moved = [i]
+            for x in cur[b - 1:a:-1]:
+                if x in need:
+                    moved.append(x)
+                    need |= above[x]
+            if cur[a] in need:
+                continue
+            inside = set(moved)
+            new = cur[:a] + moved[::-1] + [x for x in cur[a:b] if x not in inside] + cur[b + 1:]
+        else:
+            for _ in range((0, 0, 1, 2, 4, 8)[rnd(6)]):
+                p = b + 1
+                while p < n and eng[cur[p]] != eng[i]:
+                    p += 1
+                if p < n:
+                    b = p
+            need = set(below[j])
+            moved = [j]
+            for x in cur[a + 1:b]:
+                if x in need:
+                    moved.append(x)
+                    need |= below[x]
+            if cur[b] in need:
+                continue
+            inside = set(moved)
+            new = cur[:a] + [x for x in cur[a:b + 1] if x not in inside] + moved + cur[b + 1:]
+        limit = now - (0.0015 * (1.0 - k / rounds) + 0.0001) * math.log((rnd(1000) + 1) / 1001.0)
+        r = []
+        for z, tb in enumerate(tabs):
+            r.append(run(new, a, res[z], *tb))
+            v = sum(x[0] / u for x, u in zip(r + res[z + 1:], unit))
+            if v > limit + 0.004:
+                break
+        if v <= limit and len(r) == len(tabs):
             cur, now, res = new, v, r
             if v < low:
                 keep, low = new, v
-    return sum(run(keep, eng, *tb)[0] for tb in tabs), keep
+    return sum(run(keep, 0, None, *tb)[0] for tb in tabs), keep
 
 
+GOALS = []
+for _t in range(2):
+    GOALS += [[x % {"t": _t, "a": 2 * _t + HS[0], "b": 2 * _t + HS[1]}] for x in
+              ("c0%(t)dox%(a)d", "c1%(t)dox%(b)d", "c0%(t)dvs%(t)d", "oo%(t)dsht", "c0%(t)drct", "c1%(t)drct", "c0%(t)dboxt", "c1%(t)dboxt",
+               "kk%(t)deb", "c1%(t)dvs%(t)d")]
+GOALS += [["c02ox%d" % (4 + HS[0])], ["c12ox%d" % (4 + HS[1])], ["kk2rct"], ["kk2yo2", "kk2vs2"]]
 PLANS = [declare(x) for x in GUESS]
 OPS = PLANS[0][0]
-ORDER = min(arrange(PLANS, 9000, s) for s in (6, 777, 31, 58))[1]
+ORDER = min(arrange(PLANS, 40000, s) for s in (5, 77, 31))[1]
+_pool = [i for i in ORDER if OPS[i]["kind"] in ("iota", "sel")]
+for _j, _i in zip(_pool, _pool[1:]):
+    if any(len(OPS[k]["args"][0]) > 4 and OPS[k]["args"][0][4][0] for k in (_i, _j)):
+        OPS[_i]["deps"].add(_j)
 
 
 def rank_program(g, core, T, topo):
@@ -623,13 +714,14 @@ def rank_program(g, core, T, topo):
     n_in = len(topo.engines(prv, core)[:8])
     Q = {"V": g.vector, "S": g.scalar, "P": g.tensor, "G": g, "Q": g.sync}
 
-    def ap(x, rows=128):
+    def ap(x):
         if not isinstance(x, tuple):
             return x
         if x[0] == "@":
             return ap(x[1]).indirect(ap(x[2]))
         name, at = PLACE.get(x[0], (x[0], 0))
-        return T[name][0:rows, at + x[1]:at + x[2]] if x[3] == 1 else T[name][0:rows, at + x[1]:at + x[2]:x[3]]
+        p0, p1 = x[4] if len(x) > 4 else (0, 128)
+        return T[name][p0:p1, at + x[1]:at + x[2]] if x[3] == 1 else T[name][p0:p1, at + x[1]:at + x[2]:x[3]]
 
     needed = set()
     for op in OPS:
@@ -672,7 +764,6 @@ def rank_program(g, core, T, topo):
             g.remote_dma(ap(a[1]), ap(a[0]), T.sem[a[2]], T.sem.sent, pid, rid, mask)
             sends += 1
             continue
-        rows = op.get("rows", 128)
         if k == "shp":
             ins = q.dma_start(T.shpi[0:32, :], T.shp[:])
         elif k == "load":
@@ -680,9 +771,10 @@ def rank_program(g, core, T, topo):
         elif k == "store":
             ins = q.dma_start(T[a[0]][:, a[2]:a[2] + a[4]], T[a[1]][:, a[3]:a[3] + a[4]])
         elif k == "cp":
-            ins = q.tensor_copy(ap(a[0], rows), ap(a[1], rows))
+            ins = q.tensor_copy(ap(a[0]), ap(a[1]))
         elif k == "tt":
-            ins = q.tensor_tensor(ap(a[0]), ap(a[1]), ap(a[2]), a[3])
+            for x in a:
+                ins = q.tensor_tensor(ap(x[0]), ap(x[1]), ap(x[2]), x[3])
         elif k == "ts":
             if a[5] is None:
                 ins = q.tensor_scalar(ap(a[0]), ap(a[1]), ap(a[2]), None, a[4])
@@ -691,12 +783,17 @@ def rank_program(g, core, T, topo):
         elif k == "ms":
             ins = q.memset(ap(a[0]), a[1])
         elif k == "scan":
-            ins = q.tensor_tensor_scan(ap(a[0]), ap(a[1]), ap(a[2]), 0.0, A.add, A.min)
+            ins = q.tensor_tensor_scan(ap(a[0]), ap(a[1]), ap(a[2]), ap(a[3]), a[4], a[5])
         elif k == "act":
-            ins = q.activation(ap(a[0]), ap(a[1]), a[2], ap(a[3]), ap(a[4]))
+            if a[0][0] == "@":
+                ins = q.activation(ap(a[0]), ap(a[1]), a[2])
+            else:
+                ins = q.activation(ap(a[0]), ap(a[1]), a[2], ap(a[3]), ap(a[4]))
         elif k == "mm":
             for x in a:
-                ins = q.matmul(ap(x[0]), ap(x[1], rows), ap(x[2], rows), x[3], x[4])
+                ins = q.matmul(ap(x[0]), ap(x[1]), ap(x[2]), x[3], x[4])
+        elif k == "sel":
+            ins = q.affine_select(ap(a[0]), ap(a[1]), a[2], a[3], a[4], a[5], a[6])
         elif k == "iota":
             if _S[a[0][0]][1] == I32:
                 ins = q.iota(ap(a[0]), a[1], a[2], a[3])

@@ -5,7 +5,8 @@ NV, NB, S0, NT, RO = 1536, 3328, 1024, 256, 3
 MAGIC = float(3 * 2 ** 22)
 BETA = 1.8
 SO = 512
-EW = SO + NV + NT
+EW = 8 + NV + NT
+KS = 2.0 ** -22
 HS = (1, 0)
 
 F, B, H, I32, U = "float32", "bfloat16", "float16", "int32", "uint16"
@@ -25,15 +26,15 @@ _S = {
     "lo": (32, F), "lp": (32, F), "ld": (32, F), "ol": (16, U), "wd": (32, F), "nd": (32, F), "ln": (32, F), "nl": (16, U),
     "y1": (16, F), "yl": (16, U),
     "hy": (8 + 2 * NT, F), "dat": (NT, F), "seen": (NT, F), "yc16": (16, U), "yo0": (NT, F), "yo1": (NT, F), "yo2": (NT, F),
-    "cf": (32, F), "ci": (8, I32), "cj": (8, I32), "kq": (144, F), "kg": (128, F),
-    "Ib": (128, B), "II": (256, B), "nII": (256, B), "Ih": (128, H), "nI8k": (128, H), "B4k": (128, H), "I37": (128, B),
-    "If": (128, F), "nI26": (128, F), "nI23": (128, F), "Rf": (128, F), "Rb": (128, F), "RI": (128, F),
-    "Bb": (128, B), "nB3": (384, B), "KW": (128, B), "RW": (128, B),
-    "one": (256, B), "m0": (128, B), "s2": (24, B), "sm": (24, B), "sr": (8, B),
-    "Zb": (144, B), "Zh": (144, H), "ZK": (144, B), "Zq": (144, B),
-    "cl": (128, B), "cr": (256, B), "tl": (128, B), "tr": (256, B), "d0": (128, F), "bits": (NT, B),
-    "e4": (4, F), "sq": (512, H), "bc": (16, F), "fa": (16, F), "fb": (16, F), "fc": (16, F), "fd": (16, F), "fe": (16, F), "z16": (16, F),
-    "iL": (16, F), "wL": (16, F), "c16i": (8, H), "yc": (16, F),
+    "cf": (32, F), "ci": (8, I32), "cj": (8, I32), "kq": (16, F),
+    "InI": (384, B), "nI8k": (128, B), "B4k": (128, B), "B0": (128, B),
+    "If": (128, F), "Rf": (128, F), "Rb": (128, F), "RI": (128, F),
+    "Bb": (128, B), "nB3": (384, B), "KW": (128, B), "Bq": (128, B), "Bm": (128, B), "wW": (NT, B), "RW": (128, B),
+    "one": (128, B), "pm": (256, B), "s2": (24, B), "sm": (24, B), "sr": (8, B),
+    "Zb": (144, B), "ZK": (144, B), "Zq": (144, B),
+    "cl": (128, B), "cr": (256, B), "tl": (128, B), "tr": (256, B), "d0": (128, B), "bits": (NT, B),
+    "sq": (512, B), "bc": (16, F), "fa": (16, F), "fb": (16, F), "fc": (16, F), "fd": (16, F), "fe": (16, F), "z16": (16, F),
+    "iL": (16, F), "wL": (16, F), "c16i": (8, B), "yc": (16, F),
     "db1": (4, F), "db2": (4, F), "db3": (4, F),
 }
 PLACE = {}
@@ -53,15 +54,15 @@ SEMAPHORES = ["sV", "sS", "sP", "sG", "sent"] + _DMA + _ARR
 
 A = AluOpType
 AF = ActivationFunctionType
-GUESS = ((1.56, 3.8, 0.55, 170, 4200, 180.0, 1.0), (1.3, 3.0, 0.65, 120, 3000, 250.0, 1.2), (1.8, 4.5, 0.5, 250, 3500, 200.0, 1.4))
+GUESS = ((1.56, 3.8, 0.55, 220, 3000, 300.0, 1300, 1.0), (1.3, 3.0, 0.6, 130, 2000, 400.0, 1000, 1.15), (1.8, 4.5, 0.5, 250, 3500, 240.0, 1600, 1.35))
 Q4 = ((0, 32, 0), (32, 64, 0), (64, 96, 0), (96, 128, 0))
 Q2 = ((0, 64, 0), (64, 128, 0))
 Q3 = ((0, 64, 0), (64, 96, 0), (96, 128, 0))
 V0 = ((0, 32, 0), (32, 64, 1), (64, 128, 0))
 V1 = ((0, 32, 0), (32, 64, 0), (64, 96, 0), (96, 128, 1))
 V2 = ((0, 40, 0), (40, 64, 1), (64, 104, 0), (104, 128, 1))
-CUT = ((V0, Q2), (Q4, Q2), (Q4, Q2))
-ON = {"sht": 0, "eb": (1, 1), "seen": 0, "yo": (0, 0, 0), "split": (0, 0, 0)}
+CUT = ((Q4, Q2), (Q4, Q4), (Q4, Q4))
+ON = {"sht": 1, "eb": (1, 1), "seen": 0, "yo": (0, 0, 0), "split": (0, 0, 0), "lin": 128, "fill": 72, "own": (0, 1, 1)}
 CH = 64
 
 
@@ -83,7 +84,7 @@ def count(x):
 
 
 def declare(guess):
-    RHO, SCAT, PEC, HOP, NET, RATE, SLOW = guess
+    RHO, SCAT, PEC, HOP, NET, RATE, FIX, SLOW = guess
     ops = []
     part = ["c"]
     allv = ON["sht"] and all(ON["eb"])
@@ -151,13 +152,19 @@ def declare(guess):
         add("G", "iota", (out, pat, base, cm), [], [out], 160 + 2 * count(out))
 
     def fill(out, c):
-        iota(out, [[0, count(out)]], c)
+        if vcost(out, out) <= ON["fill"]:
+            ms(out, float(c))
+        else:
+            iota(out, [[0, count(out)]], c)
+
+    def sel(out, in_, pat, cmp, other, base, cm):
+        add("G", "sel", (out, in_, pat, cmp, other, base, cm), [in_], [out], 200 + 2 * count(out))
 
     nd = [0, 0]
 
     def dma(q, kind, args, rd, wr, nbytes):
         nd[1] = nbytes + (nd[1] if kind != "store" or args[0] == "yr" else 0)
-        add(q, kind, args, rd, wr, 60, sem=_DMA[nd[0]], lat=2200 + nd[1] / RATE)
+        add(q, kind, args, rd, wr, 60, sem=_DMA[nd[0]], lat=FIX + nd[1] / RATE)
         nd[0] += 1
 
     def P(b, lo, hi, step=1):
@@ -174,123 +181,132 @@ def declare(guess):
     dma("S", "load", ("dri", "dr", 0, 3), [], [vw("dri", 0, 3)], 768)
     dma("Q", "load", ("boxt", "box", 0, NB), [], [vw("boxt", 0, NB)], 851968)
     dma("Q", "load", ("bndi", "bound", 0, S0), [vw("reci")], [vw("bndi")], 524288)
-    ops[-1]["lat"] = 1490000 / RATE
+    ops[-1]["lat"] = 1490000 / RATE + FIX - 2000
     for k in range(1, 7):
         ops[k]["soft"] = {k - 1}
     cp(vw("o0"), vw("obi"))
 
     col = lambda k: vw("cf", k, k + 1)
     bc = lambda k: vw("bc", k, k + 1)
-    iota(vw("kq"), [[1, 144]], 0)
+
+    def lin(out, in_, scale, bias=0.0):
+        if in_[0] != "@" and count(out) >= ON["lin"] and not wide(out) and not wide(in_):
+            ts(out, in_, scale, A.mult, bias, A.add)
+        else:
+            act(out, in_, AF.Identity, bias, scale)
+
+    k16 = vw("kq")
+    Ib, one = vw("InI", 0, 128), vw("one")
+    blk = vw("Bb", 0, 128, 16)
+    fill(one, 1)
+    sel(Ib, one, [[-1, 128]], A.is_equal, 0.0, 0, 1)
+    iota(k16, [[1, 16]], 0)
     iota(vw("ci", 0, 1), [[1, 1]], 0, 1)
-    iota(vw("kg"), [[16, 8], [0, 16]], 0)
-    iota(vw("tab"), [[1, NV]], 0)
-    cp(col(0), vw("ci", 0, 1))
+    sel(vw("B0"), one, [[-16, 8], [0, 16]], A.is_ge, 0.0, 0, 1)
+    sel(vw("Bb"), vw("B0"), [[16, 8], [0, 16]], A.is_ge, 0.0, 15, -1)
+    iota(vw("tab", 0, NT), [[1, NT]], 0)
+    for n, k in ((256, 256), (512, 512), (1024, 512)):
+        lin(vw("tab", n, n + k), vw("tab", 0, k), 1.0, float(n))
     ts(vw("cj", 0, 1), vw("ci", 0, 1), 15, A.bitwise_and)
     cp(col(1), vw("cj", 0, 1))
-    tt(col(2), col(0), col(1), A.subtract)
-    ts(col(3), col(2), 15.0, A.add)
-    ts(col(4), col(2), 0.0625, A.mult)
-    k16 = vw("kq", 0, 16)
-    kq = vw("kq", 0, 128)
     ts(vw("bc"), k16, col(1), A.is_equal, 4096.0, A.mult)
-    ts(col(5), bc(0), 1.0 / 256, A.mult, col(0), A.add)
-    ts(col(5), col(5), -1.0, A.add)
-    ts(col(7), bc(15), -1.0 / 256, A.mult, col(0), A.add)
-    ts(col(7), col(7), 1.0, A.add)
-    ts(col(9), col(1), -2048.0, A.add)
-    ts(col(16), col(0), 4.0, A.mult)
-    for name, s in (("Ib", 1.0), ("Ih", 1.0), ("nI8k", -8192.0)):
-        ts(vw(name), kq, col(0), A.is_equal, s, A.mult)
-    for name, s in (("If", 1.0), ("nI26", -2.0 ** 26), ("nI23", -2.0 ** -23), ("I37", 2.0 ** 37)):
-        act(vw(name), vw("Ib"), AF.Identity, 0.0, s)
-    for k in range(2):
-        act(vw("II", 128 * k, 128 * k + 128), vw("Ib"))
-    act(vw("nII"), vw("II"), AF.Identity, 0.0, -1.0)
-    ts(vw("Bb"), vw("kg"), col(2), A.is_equal)
-    ts(vw("B4k"), vw("Bb"), 4096.0, A.mult)
-    for k, s in enumerate((32.0, 2.0 ** 26, 1.0)):
-        act(vw("nB3", 128 * k, 128 * k + 128), vw("Bb"), AF.Identity, 0.0, -s)
-        ts(vw("s2", 8 * k, 8 * k + 8), vw("kq", 0, 8), col(4), A.is_equal, 2 * s, A.mult)
-    act(vw("sm"), vw("s2"), AF.Identity, 0.0, -0.5)
-    ts(vw("Rf"), kq, col(5), A.is_equal)
-    ts(vw("Rb"), kq, col(7), A.is_equal)
-    add("G", "sel", (vw("RI"), vw("Rf"), [[-1, 128]], A.not_equal, -1.0, 0, 1), [vw("Rf")], [vw("RI")], 460)
-    ts(vw("Zb"), vw("kq"), col(3), A.is_equal)
-    ts(vw("Zh"), vw("kq"), col(3), A.is_equal)
-    fill(vw("one"), 1)
-    ms(vw("m0", p=(0, 1)), 0.0)
-    ms(vw("m0", 0, 128, 16, p=(0, 1)), 1.0)
-    ms(vw("d0"), 0.0)
-    ms(vw("d0", 0, 128, 16), -3.0e7)
+    lin(col(9), col(1), 1.0, -2048.0)
+    lin(vw("InI", 128, 256), Ib, -1.0)
+    lin(vw("InI", 256, 384), Ib, 1.0)
+    lin(vw("If"), Ib, 1.0)
+    lin(vw("nI8k"), Ib, -8192.0)
+    lin(vw("B4k"), vw("Bb"), 4096.0)
+    for k, s in enumerate((32 * KS, 4.0, 1.0)):
+        lin(vw("nB3", 128 * k, 128 * k + 128), vw("Bb"), -s)
+        lin(vw("s2", 8 * k, 8 * k + 8), blk, 2 * s)
+    lin(vw("sm"), vw("s2"), -0.5)
+    lin(vw("Rf", 0, 127), vw("If", 1, 128), 1.0)
+    lin(vw("Rf", 15, 128, 16), vw("If", 0, 128, 16), 1.0)
+    lin(vw("Rb", 1, 128), vw("If", 0, 127), 1.0)
+    lin(vw("Rb", 0, 128, 16), vw("If", 15, 128, 16), 1.0)
+    sel(vw("RI"), vw("Rf"), [[-1, 128]], A.not_equal, -1.0, 0, 1)
+    fill(vw("Zb"), 0)
+    lin(vw("Zb", 15, 143, 16), blk, 1.0)
+    fill(vw("pm", 0, 128), 0.0625)
+    fill(vw("pm", 128, 256), -0.0625)
+    fill(vw("d0"), 0)
+    lin(vw("d0", 0, 128, 16), vw("one", 0, 8), -1.0)
     for h in range(2):
         fill(vw("sc", 144 * h + 128, 144 * h + 144), 0)
-        fill(vw("st", 144 * h, 144 * h + 1), 1)
-    ms(vw("z16"), 0.0)
+    fill(vw("st", 0, 288, 144), 1)
+    fill(vw("z16"), 0)
     ts(vw("fa"), k16, col(1), A.is_ge, 1.0 / BETA, A.max)
     scan(vw("fb"), vw("fa"), vw("z16"), BETA ** 64, A.mult, A.max)
-    ms(vw("fc"), BETA ** -16)
-    ms(vw("fc", 0, 1), BETA ** 64)
+    lin(vw("fc"), vw("one", 0, 16), BETA ** -16)
+    lin(vw("fc", 0, 1), vw("one", 0, 1), BETA ** 64)
     scan(vw("wL"), vw("fc"), vw("z16"), vw("fb", 15, 16), A.mult, A.max)
     ts(vw("fd"), k16, col(1), A.is_lt, 1.0, A.add)
-    scan(vw("fe"), vw("fd"), vw("z16"), 0.5, A.mult, A.max)
-    ts(col(10), col(1), 10.5, A.is_lt, vw("fe", 15, 16), A.mult)
-    ts(col(10), bc(11), -0.25, A.mult, col(10), A.add)
-    ts(col(10), bc(12), 2.0 ** -13, A.mult, col(10), A.add)
-    ts(col(11), bc(10), bc(11), A.subtract, 2.0 ** -13, A.mult)
-    ts(col(12), bc(10), bc(11), A.add, -2.0 ** -13, A.mult)
-    ts(col(13), bc(8), 64.0, A.add)
-    act(vw("KW"), vw("Bb"), AF.Identity, 0.0, col(10))
-    act(vw("RW"), vw("Bb"), AF.Identity, 0.0, col(11))
-    act(vw("ZK"), vw("Zb"), AF.Identity, 0.0, col(10))
-    act(vw("Zq"), vw("Zb"), AF.Identity, 0.0, col(12))
-    ts(vw("sr"), vw("s2", 16, 24), col(11), A.mult, 8.0, A.mult)
-    ts(vw("bits", 0, 1), bc(9), bc(10), A.add)
+    scan(vw("fe"), vw("fd"), vw("z16"), -0.5, A.mult, A.min)
+    ts(col(2), col(1), 10.5, A.is_lt, vw("fe", 15, 16), A.mult)
+    lin(col(3), bc(11), 0.25, col(2))
+    lin(col(10), bc(12), -2.0 ** -13, col(3))
+    lin(col(4), bc(11), 2.0 ** -13)
+    lin(col(11), bc(10), -2.0 ** -13, col(4))
+    lin(col(12), bc(10), 2.0 ** -13, col(4))
+    lin(col(13), bc(8), 1.0, 64.0)
+    lin(col(14), col(11), 16 * KS)
+    lin(vw("KW"), vw("Bb"), col(10))
+    lin(vw("RW"), vw("Bb"), col(11))
+    lin(vw("ZK"), vw("Zb"), col(10))
+    lin(vw("Zq"), vw("Zb"), col(12))
+    lin(vw("sr"), blk, col(14))
+    lin(col(15), col(11), 2.0 ** 90)
+    ts(vw("Bq"), vw("Bb"), col(15), A.mult, 2.0 ** 26, A.mult)
+    ts(vw("Bm"), vw("Bb"), -2.0 ** 90, A.mult, 2.0 ** 15, A.mult)
+    act(vw("wW", 0, 1), vw("fc", 0, 1), AF.Identity, 0.0, -2.5 * BETA ** 64)
     for k in range(8):
-        act(vw("bits", 2 ** k, 2 ** (k + 1)), vw("bits", 0, 2 ** k), AF.Identity, bc(k))
+        act(vw("wW", 2 ** k, 2 ** (k + 1)), vw("wW", 0, 2 ** k), AF.Identity, 0.0, BETA ** -(2 ** k))
+    lin(vw("bits", 0, 1), bc(9), 1.0, bc(10))
+    for k in range(8):
+        lin(vw("bits", 2 ** k, 2 ** (k + 1)), vw("bits", 0, 2 ** k), 1.0, bc(k))
+    row = lambda name, p, c, lo=0, hi=128, n=1: ms(vw(name, lo, hi, p=(p, p + n)), c)
     fill(vw("cl"), 0)
-    for p, c in ((0, 2.0 ** 17), (32, 1.0), (64, -2.0 ** 25), (96, 2112 * 2.0 ** 26)):
-        ms(vw("cl", p=(p, p + 1)), c)
+    for p, c in ((0, 2.0 ** 17 * KS), (32, KS), (64, -2.0), (96, 2112 * 4.0)):
+        row("cl", p, c)
     iota(vw("cr", 0, 128), [[0, 8], [1, 16]], 0)
     iota(vw("cr", 0, 128, p=(0, 32)), [[-1, 8], [0, 16]], 7)
-    ms(vw("cr", 0, 128, p=(64, 128)), 0.0)
+    row("cr", 64, 0.0, 0, 128, 64)
     fill(vw("cr", 128, 256), 0)
-    ms(vw("cr", 128, 256, p=(64, 128)), 1.0)
+    row("cr", 64, 1.0, 128, 256, 64)
     fill(vw("tl"), 0)
     iota(vw("tl", p=(0, 1)), [[0, 8], [1, 16]], 0)
     for p, c in ((32, 1.0), (64, -2048.0), (96, 1.0)):
-        ms(vw("tl", p=(p, p + 1)), c)
+        row("tl", p, c)
     iota(vw("tr"), [[1, NT]], 0)
     fill(vw("tr", p=(0, 1)), 8192)
-    ms(vw("tr", p=(64, 65)), 8192.0)
+    lin(vw("tr", p=(64, 65)), vw("tr", p=(64, 65)), 0.0, 8192.0)
     mm(P(0, 256, 384), vw("cl", p=(0, 64)), vw("cr", 0, 128, p=(0, 64)))
     for h in range(2):
         act(vw("cT", 128 * h, 128 * h + 128), P(0, 256, 384))
-    ts(vw("iL"), k16, 16.0, A.mult, col(1), A.add)
-    ts(vw("c16i"), vw("iL", 0, 8), 16.0, A.mult, 2048.0, A.add)
+    lin(vw("iL"), k16, 16.0, col(1))
+    lin(vw("c16i"), vw("iL", 0, 8), 16.0, 2048.0)
     fill(vw("ld"), 0)
     fill(vw("nd"), 0)
-    ts(vw("ld", 1, 32, 2), vw("iL"), float(NV), A.add)
-    ts(vw("wd", 1, 32, 2), vw("iL"), float(SO + NV), A.add)
-    ts(vw("yc"), vw("iL"), float(8 + NT), A.add)
-    ts(vw("db1", 0, 3), vw("dri", 0, 3), -1.0, A.mult, 256.0, A.add)
-    cp(vw("db2", 0, 3), vw("dri", 0, 3))
-    ts(vw("db3", 0, 3), vw("dri", 0, 3), -1.0, A.mult)
-    fill(vw("eb", 0, SO), 64)
-    fill(vw("eb", SO + S0 + NT, EW), 64)
+    lin(vw("ld", 1, 32, 2), vw("iL"), 1.0, float(NV))
+    lin(vw("wd", 1, 32, 2), vw("iL"), 1.0, float(SO + NV))
+    lin(vw("yc"), vw("iL"), 1.0, float(8 + NT))
+    lin(vw("db1", 0, 3), vw("dri", 0, 3), -1.0, 256.0)
+    lin(vw("db2", 0, 3), vw("dri", 0, 3), 1.0)
+    lin(vw("db3", 0, 3), vw("dri", 0, 3), -1.0)
+    fill(vw("eb", 0, 8), 64)
+    fill(vw("eb", 8 + S0 + NT, EW), 64)
     fill(vw("rct", NV, NV + NT), 0)
     fill(vw("sht", NV, NV + NT), 0)
     fill(vw("hy", 0, 8), 0)
     cp(vw("shph", p=(0, 32)), vw("shpi", p=(0, 32)))
-    ts(vw("e4"), vw("kq", 0, 4), -4.0, A.mult, col(16), A.add)
     for k in range(4):
-        ts(vw("sq", 128 * k, 128 * k + 128), vw("kg"), vw("e4", k, k + 1), A.is_equal)
+        sel(vw("sq", 128 * k, 128 * k + 128, p=(0, 32)), vw("one", p=(0, 32)), [[-4, 8], [0, 16]], A.is_equal, 0.0, -k, 1)
         mm(P(4 + k, 0, 384), vw("sq", 128 * k, 128 * k + 128, p=(0, 32)), vw("shph", p=(0, 32)))
         act(vw("sht", 384 * k, 384 * k + 384), P(4 + k, 0, 384), AF.Identity if k or allv else AF.Silu, float(SO), 1.0, 0 if k or allv else 1560)
     for k in range(3):
         cp(vw("rct", 512 * k, 512 * k + 512), vw("reci", 512 * k, 512 * k + 512))
     for k in range(2):
-        ts(vw("eb", SO + 512 * k, SO + 512 * k + 512), vw("bndi", 512 * k, 512 * k + 512), 64.0, A.add)
+        ts(vw("eb", 8 + 512 * k, 520 + 512 * k), vw("bndi", 512 * k, 512 * k + 512), 64.0, A.add)
 
     def pairs(eq, W, Lf, wt, Sb, end):
         at = 0
@@ -298,10 +314,11 @@ def declare(guess):
             n = end(m) - 16 * m
             ts(vw(eq, at, at + n), vw(W, 16 * m, end(m)), Lf(m), A.is_equal, vw(wt, m, m + 1), A.mult)
             cuts = (0, 128, n) if m == 0 and n > 128 else (0, n)
-            mms([(P(6, 16 * m + x, 16 * m + y), vw("Bb"), vw(eq, at + x, at + y), k == 0, k == 15) for x, y in zip(cuts, cuts[1:])])
+            mms([(P(6, 16 * m + x, 16 * m + y), vw("Bb"), vw(eq, at + x, at + y), k == 0 and bool(Sb), k == 15) for x, y in zip(cuts, cuts[1:])])
             at += n
-        act(vw(Sb), P(6, 0, NT), AF.Identity, 0.0, 1.0 / 40)
-        diag(P(6, 256, 272), Sb, "Zb")
+        if Sb:
+            act(vw(Sb), P(6, 0, NT), AF.Identity, 0.0, 1.0 / 40)
+            diag(P(6, 256, 272), Sb, "Zb")
 
     for t in range(RO):
         o, v, vs = "o%d" % t, "v%d" % t, "vs%d" % t
@@ -327,11 +344,11 @@ def declare(guess):
             e = 2 + h
 
             def bounds():
-                mm(P(e, 128, 256), hw("hn", h), vw("nI26"), False, False)
+                mm(P(e, 128, 256), hw("hn", h), vw("If"), False, False)
                 if rot:
-                    mms([(P(e, 128, 256), hw("sgW", h), vw("I37"), False, False), (P(e, 0, 128, 16), hw("sgW", h), vw("sr"), False, False)])
+                    mms([(P(e, 128, 256), hw("sgW", h), vw("nI8k"), False, False), (P(e, 0, 128, 16), hw("sgW", h), vw("sr"), False, False)])
 
-            mm(P(h, 0, 128), vw("Ib"), hw(v, h))
+            mm(P(h, 0, 128), Ib, hw(v, h))
             rows = (0, 128 if rot else 96)
             mms([(P(e, 0, 384), hw(v, h), vw("nB3"), True, False), (P(e, 0, 256), vw("cl", p=rows), vw("cr", p=rows), False, False)])
             for lo, hi, on in CUT[t][HS.index(h)]:
@@ -361,17 +378,17 @@ def declare(guess):
             L = lambda name: vw(name, 8 * lo, 8 * hi)
             ps = P(4 + h, 272, 272 + 8 * (hi - lo))
             cp(W("sW"), ind(vw("sht", 0, NV), L(o)))
-            diag(ps, "sW", "Zh", None, 128 * lo, 128 * hi)
-            ts(L("s16"), ps, 0.0625, A.mult, 0.0 if rot else -float(SO), A.add)
+            diag(ps, "sW", "Zb", None, 128 * lo, 128 * hi)
+            ts(L("s16"), ps, 0.0625, A.mult, (8.0 if rot else 0.0) - SO, A.add)
             act(L("sLf"), ps, AF.Identity, 0.0, 0.0625)
             if not rot:
-                cp(W("hn"), ind(vw("bndi"), L("s16")))
+                ts(W("hn"), ind(vw("bndi"), L("s16")), -4.0, A.mult)
                 return
-            act(W("hn"), ind(vw("eb", 0, SO + S0 + NT), L("s16")))
-            act(W("sgW"), W("hn"), AF.Sign, -4152.0)
+            lin(W("hn"), ind(vw("eb", 0, 8 + S0 + NT), L("s16")), -4.0)
+            act(W("sgW"), W("hn"), AF.Sign, 4 * 4152.0)
             for k in hs:
                 group(P(7, 8 * k, 8 * k + 8), (hw("sgW", k), vw("sr")), (vw("cl", p=(0, 32)), vw("cr", 0, 128, 16, p=(0, 32))))
-            act(W("cT", 16), P(7, 8 * lo, 8 * hi))
+            cp(W("cT", 16), P(7, 8 * lo, 8 * hi))
             if HS[1] not in hs:
                 return
             pk = P(7, 16, 32)
@@ -383,12 +400,17 @@ def declare(guess):
             tt(vw("ycol"), vw("t3"), vw("yc"), A.add)
             mm(P(7, 256, 512), vw("KW"), vw("sgW"))
             tt(vw("nF" if t == 1 else "nW"), vw("sW"), P(7, 256, 512), A.max)
-            if t == 1:
-                cp(vw("yc16"), vw("ycol"))
+            cp(vw("yc16"), vw("ycol"))
+            if t == 2:
+                ts(vw("n16"), vw("nLf"), 8.0 - SO, A.add)
+                act(vw("nsg"), ind(vw("eb", 0, 8 + NV), vw("n16")), AF.Sign, 4152.0, -1.0)
+                diag(P(7, 32, 48), "nsg", "Zq")
+                tt(vw("nqL"), vw("wL"), P(7, 32, 48), A.mult)
 
         def owners():
-            cp(vw("oW"), ind(vw("tab"), vw(o)))
-            cp(vw("lo", 1, 32, 2), vw(o))
+            for lo, hi in ((1, 2), (0, 1)) if ON["own"][t] else ((0, 2),):
+                cp(vw("oW", 128 * lo, 128 * hi), ind(vw("tab"), vw(o, 8 * lo, 8 * hi)))
+                cp(vw("lo", 16 * lo + 1, 16 * hi, 2), vw(o, 8 * lo, 8 * hi))
             pairs("eqo", "oW", lambda m: vw("lo", 2 * m + 1, 2 * m + 2), "wL", "So", lambda m: 128 * (m // 8 + 1))
             tt(vw("lo", 0, 32, 2), vw("wL"), P(6, 256, 272), A.is_le)
             scan(vw("lp"), vw("ld"), vw("lo"), 0.0, A.mult, A.max)
@@ -396,11 +418,6 @@ def declare(guess):
             if t == 1:
                 for h in HS:
                     (cp if ON["sht"] else silu)(ind(vw("sht"), hl_("ol", h)), hw("nF", h))
-            if t == 2:
-                cp(vw("n16"), vw("nLf"))
-                act(vw("nsg"), ind(vw("eb", 0, SO + NV), vw("n16")), AF.Sign, -4152.0)
-                diag(P(6, 272, 288), "nsg", "Zq")
-                tt(vw("nqL"), vw("wL"), P(6, 272, 288), A.mult)
 
         def choose(h):
             e, w = 2 + h, 4 + h
@@ -408,16 +425,16 @@ def declare(guess):
             st = lambda k: vw("st", 144 * h + k, 144 * h + k + 128)
             tt(hw("rp", h), hw("cT", h), P(e, 128, 256), A.max)
             sc = lambda k: vw("sc", 144 * h + k, 144 * h + k + 128)
-            scan(sc(0), hw("rp", h), P(e, 0, 128), 3.0e7, A.min, A.min)
+            scan(sc(0), hw("rp", h), P(e, 0, 128), 1.0, A.min, A.min)
             act(hw("eS", h), P(e, 256, 384))
             scan(P(h, 128, 256), vw("d0"), sc(15), 0.0, A.add, A.max)
             tt(st(1), sc(0), P(h, 128, 256), A.is_equal)
-            mm(P(w, 0, 256), vw("m0", p=(0, 1)), vw("one", p=(0, 1)), True, False)
-            mm(P(w, 128, 256), hw("rp", h), vw("nI23"), False, False)
-            mms([(P(w, 0, 256), st(1), vw("II"), False, False), (P(w, 0, 256), st(0), vw("nII"), False, True)])
+            mm(P(w, 0, 256), vw("Zb", 15, 143), vw("pm"), True, False)
+            mm(P(w, 128, 256), hw("rp", h), vw("If"), False, False)
+            mms([(P(w, 0, 256), st(1), vw("InI", 0, 256), False, False), (P(w, 0, 256), st(0), vw("InI", 128, 384), False, True)])
             tt(vw(dg, 0, 128), hw("p32", h), P(w, 0, 128), A.mult)
-            ts(vw(dg, 128, 256), P(w, 128, 256), 0.5, A.is_gt, col(9), A.mult)
-            diag(P(w, 256, 272), dg, "Zh", (P(w, 264, 272), vw("Ih"), vw("c16i")))
+            ts(vw(dg, 128, 256), P(w, 128, 256), -0.5, A.is_lt, col(9), A.mult)
+            diag(P(w, 256, 272), dg, "Zb", (P(w, 264, 272), Ib, vw("c16i")))
             ox = "ox%d" % (2 * t + h)
             cp(vw(ox), P(w, 256, 272))
             if t < 2:
@@ -427,7 +444,7 @@ def declare(guess):
             tt(hl_("akw", h), hl_("nhL", h), hl_("nqL" if t == 2 else "wL", h), A.mult)
             act(hw("XX", h), ind(vw("bh%d" % h), vw(ox, 8, 16)))
             ts(hw("sg", h), hw("XX", h), bias("db1"), A.is_ge, -256.0, A.mult)
-            group(P(h, 256, 384), (vw("Ib"), hw("XX", h)), (vw("Ib"), hw("sg", h)))
+            group(P(h, 256, 384), (Ib, hw("XX", h)), (Ib, hw("sg", h)))
             act(hw(vs, h), P(h, 256, 384), AF.Identity, bias("db2"))
             if t < 2:
                 add("G", "send", (hw(vs, h), hw("v%d" % (t + 1), h), "av%d%d" % (t, h)), [hw(vs, h)], [], 900, tag=("sv", t, h))
@@ -440,28 +457,36 @@ def declare(guess):
             else:
                 cp(ind(vw("rct"), hl_("ol", h)), hw("yy", h))
             if t < 2:
-                group(P(w, 0, 128), (vw("Ib"), hw("XX", h)), (vw("Ib"), hw(v, h)))
+                group(P(w, 0, 128), (Ib, hw("XX", h)), (Ib, hw(v, h)))
                 act(hw("bt", h), P(w, 0, 128), AF.Identity, MAGIC, 0.5 - 2.0 ** -11)
                 act(vw("boxt", NB + NT * t + 128 * h, NB + NT * t + 128 * h + 128), hw("bt", h), AF.Identity, -MAGIC)
 
         def makers():
             yo = vw("yo%d" % t)
-            hs = vw("hy", 8 + NT, 8 + 2 * NT) if rot else vw("eb", SO + S0, SO + S0 + NT)
+            hs = vw("hy", 8 + NT, 8 + 2 * NT) if rot else vw("eb", 8 + S0, 8 + S0 + NT)
             mms([(P(7, 128 * h, 128 * h + 128), hw("eS", h), vw("If"), True, True) for h in range(2)])
             act(hs, P(7, 0, NT), AF.Identity, 0.0 if rot else 64.0)
             if rot:
                 mm(P(7, 256, 512), vw("Rf"), hs)
                 act(vw("hy", 8, 8 + NT), P(7, 256, 512))
+                (cp if ON["seen"] else act)(vw("seen"), ind(vw("hy"), vw("yc16")))
                 if t == 1:
-                    (cp if ON["seen"] else act)(vw("seen"), ind(vw("hy"), vw("yc16")))
-                    group(P(7, 0, NT), (vw("Rb"), vw("seen")), (vw("Ib"), vw("bits")))
+                    group(P(7, 0, NT), (vw("Rb"), vw("seen")), (Ib, vw("bits")))
                     act(vw("dat"), P(7, 0, NT), AF.Identity, col(13))
             else:
-                ts(vw("ycol"), vw("iL"), float(SO + S0), A.add)
-                group(P(7, 256, 512), (vw("Rb"), hs), (vw("Ib"), vw("bits")))
+                lin(vw("ycol"), vw("iL"), 1.0, float(8 + S0))
+                group(P(7, 256, 512), (vw("Rb"), hs), (Ib, vw("bits")))
                 act(vw("dat"), P(7, 256, 512))
-            key = "n" if t == 2 else "s"
-            pairs("eqn", key + "W", lambda m: vw(key + "Lf", m, m + 1), "akw", "Sn", lambda m: NT)
+            if t == 2:
+                mms([(P(6, 0, NT), Ib, vw("wW"), True, False), (P(6, 0, NT), vw("Bq"), vw("nsg"), False, False)])
+                for h in HS:
+                    mm(P(6, 128 * h, 128 * h + 128), vw("Bm"), vw("dg%d" % h, 128, 256), False, False)
+                pairs("eqn", "nW", lambda m: vw("nLf", m, m + 1), "akw", None, lambda m: NT)
+                ts(P(6, 256, 512), P(6, 0, NT), 0.0, A.is_lt)
+                tt(yo, vw("seen"), P(6, 256, 512), A.mult)
+                dma("Q", "store", ("yh", "yo2", NT * t, 0, NT), [yo], [], 131072)
+                return
+            pairs("eqn", "sW", lambda m: vw("sLf", m, m + 1), "akw", "Sn", lambda m: NT)
             wn = vw("wd", 0, 32, 2)
             tt(wn, vw("akw"), P(6, 256, 272), A.is_gt)
             tt(vw("y1"), wn, vw("ycol"), A.mult)
@@ -469,14 +494,11 @@ def declare(guess):
             if rot:
                 (cp if ON["yo"][t] else act)(yo, ind(vw("hy"), vw("yl")))
             else:
-                act(yo, ind(vw("eb", 0, SO + S0 + NT), vw("yl")), AF.Identity, -64.0)
-            if t < 2:
-                tt(vw("nd", 1, 32, 2), vw("nLf" if rot else "sLf"), vw("wd", 1, 32, 2), A.subtract)
-                scan(vw("ln"), vw("nd"), vw("wd"), 0.0, A.mult, A.add)
-                cp(vw("nl"), vw("ln", 1, 32, 2))
-                (cp if ON["eb"][t] else silu)(ind(vw("eb"), vw("nl")), vw("dat"))
-            else:
-                dma("Q", "store", ("yh", "yo2", NT * t, 0, NT), [yo], [], 131072)
+                act(yo, ind(vw("eb", 0, 8 + S0 + NT), vw("yl")), AF.Identity, -64.0)
+            tt(vw("nd", 1, 32, 2), vw("nLf" if rot else "sLf"), vw("wd", 1, 32, 2), A.subtract)
+            scan(vw("ln"), vw("nd"), vw("wd"), 0.0, A.mult, A.add)
+            ts(vw("nl"), vw("ln", 1, 32, 2), 8.0 - SO, A.add)
+            (cp if ON["eb"][t] else silu)(ind(vw("eb"), vw("nl")), vw("dat"))
 
         for name, fn, h in (("l0", lists, HS[0]), ("l1", lists, HS[1]), ("s0", shapes, HS[0]), ("m0", main, HS[0]), ("s1", shapes, HS[1]),
                             ("oo", owners, None), ("m1", main, HS[1]), ("c0", choose, HS[0]), ("c1", choose, HS[1]), ("kk", makers, None)):
@@ -640,7 +662,7 @@ def arrange(plans, rounds, seed):
         a = cur.index(j)
         b = cur.index(i)
         if rnd(2):
-            for _ in range((0, 0, 0, 1, 2, 4)[rnd(6)]):
+            for _ in range((0, 0, 0, 1, 2, 4, 8, 16)[rnd(8)]):
                 p = a - 1
                 while p >= 0 and eng[cur[p]] != eng[i]:
                     p -= 1
@@ -657,7 +679,7 @@ def arrange(plans, rounds, seed):
             inside = set(moved)
             new = cur[:a] + moved[::-1] + [x for x in cur[a:b] if x not in inside] + cur[b + 1:]
         else:
-            for _ in range((0, 0, 1, 2, 4, 8)[rnd(6)]):
+            for _ in range((0, 0, 1, 2, 4, 8, 16, 32)[rnd(8)]):
                 p = b + 1
                 while p < n and eng[cur[p]] != eng[i]:
                     p += 1
@@ -687,7 +709,7 @@ def arrange(plans, rounds, seed):
     return sum(run(keep, 0, None, *tb)[0] for tb in tabs), keep
 
 
-GOALS = []
+GOALS = [["l00c16"], ["s00hn"], ["l10c16"], ["c00rp"], ["oo0ol"]]
 for _t in range(2):
     GOALS += [[x % {"t": _t, "a": 2 * _t + HS[0], "b": 2 * _t + HS[1]}] for x in
               ("c0%(t)dox%(a)d", "c1%(t)dox%(b)d", "c0%(t)dvs%(t)d", "oo%(t)dsht", "c0%(t)drct", "c1%(t)drct", "c0%(t)dboxt", "c1%(t)dboxt",
@@ -695,7 +717,7 @@ for _t in range(2):
 GOALS += [["c02ox%d" % (4 + HS[0])], ["c12ox%d" % (4 + HS[1])], ["kk2rct"], ["kk2yo2", "kk2vs2"]]
 PLANS = [declare(x) for x in GUESS]
 OPS = PLANS[0][0]
-ORDER = min(arrange(PLANS, 40000, s) for s in (5, 77, 31))[1]
+ORDER = min(arrange(PLANS, 20000, s) for s in (5, 77, 31, 8, 19, 23))[1]
 _pool = [i for i in ORDER if OPS[i]["kind"] in ("iota", "sel")]
 for _j, _i in zip(_pool, _pool[1:]):
     if any(len(OPS[k]["args"][0]) > 4 and OPS[k]["args"][0][4][0] for k in (_i, _j)):

@@ -15,21 +15,21 @@ _S = {
     "rct": (NV + NT, F), "boxt": (NB + 2 * NT, B), "eb": (EW, F), "sht": (NV + NT, F), "tab": (NV, F),
     "o0": (16, U), "o1": (16, U), "o2": (16, U), "v0": (NT, B), "v1": (NT, B), "v2": (NT, B),
     "ox0": (16, U), "ox1": (16, U), "ox2": (16, U), "ox3": (16, U), "ox4": (16, U), "ox5": (16, U),
-    "vs0": (NT, B), "vs1": (NT, B), "vs2": (NT, B),
+    "vs0": (NT, B), "vs1": (NT, B), "vs2": (NT, B), "XX": (NT, B),
     "xi": (NT, I32), "c32": (NT, I32), "p32": (NT, I32), "c16": (NT, U),
     "bh0": (4096, B), "bh1": (4096, B),
     "sW": (NT, H), "nW": (NT, H), "oW": (NT, H), "nF": (NT, F), "hn": (NT, F), "sgW": (NT, B), "nsg": (NT, B), "rotW": (NT, B),
     "sLf": (16, F), "s16": (16, U), "nLf": (16, F), "n16": (16, U), "t3": (16, F), "ycol": (16, F), "nqL": (16, F),
     "cT": (NT, F), "rp": (NT, F), "sc": (288, F), "st": (288, B), "eS": (NT, F), "dg0": (NT, H), "dg1": (NT, H),
-    "yy": (NT, F), "zz": (NT, F), "nhL": (16, F), "akw": (16, F), "XX": (NT, B), "sg": (NT, B), "bt": (NT, F),
+    "yy": (NT, F), "zz": (NT, F), "nhL": (16, F), "akw": (16, F), "sg": (NT, B), "bt": (NT, F),
     "eqo": (1152, B), "eqn": (2176, B), "So": (NT, B), "Sn": (NT, B),
     "lo": (32, F), "lp": (32, F), "ld": (32, F), "ol": (16, U), "wd": (32, F), "nd": (32, F), "ln": (32, F), "nl": (16, U),
     "y1": (16, F), "yl": (16, U),
     "hy": (8 + 2 * NT, F), "dat": (NT, F), "seen": (NT, F), "yc16": (16, U), "yo0": (NT, F), "yo1": (NT, F), "yo2": (NT, F),
     "cf": (32, F), "ci": (8, I32), "cj": (8, I32), "kq": (16, F),
-    "InI": (384, B), "nI8k": (128, B), "B4k": (128, B), "B0": (128, B),
+    "InI": (384, B), "nI8k": (128, B), "B4k": (128, B), "B0": (128, B), "mI": (128, B),
     "If": (128, F), "Rf": (128, F), "Rb": (128, F), "RI": (128, F),
-    "Bb": (128, B), "nB3": (384, B), "KW": (128, B), "Bq": (128, B), "Bm": (128, B), "wW": (NT, B), "RW": (128, B),
+    "Bb": (128, B), "nB3": (384, B), "nB4": (384, B), "KW": (128, B), "Bq": (128, B), "Bm": (128, B), "wW": (NT, B), "RW": (128, B),
     "one": (128, B), "pm": (256, B), "s2": (24, B), "sm": (24, B), "sr": (8, B),
     "Zb": (144, B), "ZK": (144, B), "Zq": (144, B),
     "cl": (128, B), "cr": (256, B), "tl": (128, B), "tr": (256, B), "d0": (128, B), "bits": (NT, B),
@@ -54,15 +54,17 @@ SEMAPHORES = ["sV", "sS", "sP", "sG", "sent"] + _DMA + _ARR
 
 A = AluOpType
 AF = ActivationFunctionType
-GUESS = ((1.56, 3.8, 0.55, 220, 3000, 300.0, 1300, 1.0), (1.3, 3.0, 0.6, 130, 2000, 400.0, 1000, 1.15), (1.8, 4.5, 0.5, 250, 3500, 240.0, 1600, 1.35))
+GUESS = ((1.56, 3.8, 0.5, 160, 3500, 300.0, 1300, 1.15), (1.3, 3.0, 0.58, 130, 2500, 400.0, 1000, 1.1), (1.8, 4.5, 0.5, 220, 4000, 240.0, 1600, 1.35),
+         (1.4, 3.5, 0.5, 170, 4500, 210.0, 1900, 1.0))
 Q4 = ((0, 32, 0), (32, 64, 0), (64, 96, 0), (96, 128, 0))
 Q2 = ((0, 64, 0), (64, 128, 0))
 Q3 = ((0, 64, 0), (64, 96, 0), (96, 128, 0))
 V0 = ((0, 32, 0), (32, 64, 1), (64, 128, 0))
 V1 = ((0, 32, 0), (32, 64, 0), (64, 96, 0), (96, 128, 1))
 V2 = ((0, 40, 0), (40, 64, 1), (64, 104, 0), (104, 128, 1))
-CUT = ((Q4, Q2), (Q4, Q4), (Q4, Q4))
-ON = {"sht": 1, "eb": (1, 1), "seen": 0, "yo": (0, 0, 0), "split": (0, 0, 0), "lin": 128, "fill": 72, "own": (0, 1, 1)}
+CUT = ((V0, Q2), (Q4, Q4), (Q4, Q4))
+ON = {"conv": (3, 2), "relu": ((0, 0), (0, 0), (0, 0)), "hs": (0, 1, 1), "sg": 0, "gc": (0, 0), "sht": 0, "eb": (1, 1), "seen": 0, "yo": (0, 0, 0), "split": (0, 0, 0), "lin": 128, "fill": 72}
+TG = 256
 CH = 64
 
 
@@ -160,6 +162,12 @@ def declare(guess):
     def sel(out, in_, pat, cmp, other, base, cm):
         add("G", "sel", (out, in_, pat, cmp, other, base, cm), [in_], [out], 200 + 2 * count(out))
 
+    def conv(out, in_, pool):
+        if pool:
+            sel(out, in_, [[0, count(out)]], A.is_equal, 0.0, 0, 0)
+        else:
+            cp(out, in_)
+
     nd = [0, 0]
 
     def dma(q, kind, args, rd, wr, nbytes):
@@ -204,9 +212,10 @@ def declare(guess):
     iota(vw("ci", 0, 1), [[1, 1]], 0, 1)
     sel(vw("B0"), one, [[-16, 8], [0, 16]], A.is_ge, 0.0, 0, 1)
     sel(vw("Bb"), vw("B0"), [[16, 8], [0, 16]], A.is_ge, 0.0, 15, -1)
-    iota(vw("tab", 0, NT), [[1, NT]], 0)
-    for n, k in ((256, 256), (512, 512), (1024, 512)):
-        lin(vw("tab", n, n + k), vw("tab", 0, k), 1.0, float(n))
+    iota(vw("tab", 0, TG), [[1, TG]], 0)
+    for n in (256, 512, 1024):
+        if n >= TG:
+            lin(vw("tab", n, min(2 * n, NV)), vw("tab", 0, min(n, NV - n)), 1.0, float(n))
     ts(vw("cj", 0, 1), vw("ci", 0, 1), 15, A.bitwise_and)
     cp(col(1), vw("cj", 0, 1))
     ts(vw("bc"), k16, col(1), A.is_equal, 4096.0, A.mult)
@@ -220,6 +229,11 @@ def declare(guess):
         lin(vw("nB3", 128 * k, 128 * k + 128), vw("Bb"), -s)
         lin(vw("s2", 8 * k, 8 * k + 8), blk, 2 * s)
     lin(vw("sm"), vw("s2"), -0.5)
+    nr = max(max(x) for x in ON["relu"])
+    if nr:
+        lin(vw("nB4"), vw("nB3"), 1.0)
+        for a in range(16 - nr, 16):
+            lin(vw("nB4", a, 384, 16), vw("nB3", a, 384, 16), -1.0)
     lin(vw("Rf", 0, 127), vw("If", 1, 128), 1.0)
     lin(vw("Rf", 15, 128, 16), vw("If", 0, 128, 16), 1.0)
     lin(vw("Rb", 1, 128), vw("If", 0, 127), 1.0)
@@ -247,13 +261,10 @@ def declare(guess):
     lin(col(10), bc(12), -2.0 ** -13, col(3))
     lin(col(4), bc(11), 2.0 ** -13)
     lin(col(11), bc(10), -2.0 ** -13, col(4))
-    lin(col(12), bc(10), 2.0 ** -13, col(4))
-    lin(col(13), bc(8), 1.0, 64.0)
     lin(col(14), col(11), 16 * KS)
     lin(vw("KW"), vw("Bb"), col(10))
     lin(vw("RW"), vw("Bb"), col(11))
     lin(vw("ZK"), vw("Zb"), col(10))
-    lin(vw("Zq"), vw("Zb"), col(12))
     lin(vw("sr"), blk, col(14))
     lin(col(15), col(11), 2.0 ** 90)
     ts(vw("Bq"), vw("Bb"), col(15), A.mult, 2.0 ** 26, A.mult)
@@ -266,7 +277,7 @@ def declare(guess):
         lin(vw("bits", 2 ** k, 2 ** (k + 1)), vw("bits", 0, 2 ** k), 1.0, bc(k))
     row = lambda name, p, c, lo=0, hi=128, n=1: ms(vw(name, lo, hi, p=(p, p + n)), c)
     fill(vw("cl"), 0)
-    for p, c in ((0, 2.0 ** 17 * KS), (32, KS), (64, -2.0), (96, 2112 * 4.0)):
+    for p, c in ((0, 2.0 ** 17 * KS), (32, KS), (64, -2.0), (96, 2048 * 4.0)):
         row("cl", p, c)
     iota(vw("cr", 0, 128), [[0, 8], [1, 16]], 0)
     iota(vw("cr", 0, 128, p=(0, 32)), [[-1, 8], [0, 16]], 7)
@@ -290,11 +301,20 @@ def declare(guess):
     lin(vw("ld", 1, 32, 2), vw("iL"), 1.0, float(NV))
     lin(vw("wd", 1, 32, 2), vw("iL"), 1.0, float(SO + NV))
     lin(vw("yc"), vw("iL"), 1.0, float(8 + NT))
-    lin(vw("db1", 0, 3), vw("dri", 0, 3), -1.0, 256.0)
-    lin(vw("db2", 0, 3), vw("dri", 0, 3), 1.0)
+    if ON["sg"]:
+        lin(vw("db1", 0, 3), vw("dri", 0, 3), -1.0, 256.0)
+        lin(vw("db2", 0, 3), vw("dri", 0, 3), 1.0)
+    else:
+        lin(vw("db1", 0, 3), vw("dri", 0, 3), 1.0, -255.5)
+        lin(vw("db2", 0, 3), vw("dri", 0, 3), 1.0, -128.0)
+        lin(vw("mI"), Ib, -128.0)
     lin(vw("db3", 0, 3), vw("dri", 0, 3), -1.0)
-    fill(vw("eb", 0, 8), 64)
-    fill(vw("eb", 8 + S0 + NT, EW), 64)
+    fill(vw("eb", 0, 8), 0)
+    if allv:
+        fill(vw("eb", 8 + S0 + NT, EW), 0)
+    else:
+        fill(vw("eb", 8 + NV, EW), 0)
+        act(vw("eb", 8 + S0 + NT, 8 + NV), vw("tab", 0, NT), AF.Silu, 0.0, 0.0, 1560)
     fill(vw("rct", NV, NV + NT), 0)
     fill(vw("sht", NV, NV + NT), 0)
     fill(vw("hy", 0, 8), 0)
@@ -302,11 +322,11 @@ def declare(guess):
     for k in range(4):
         sel(vw("sq", 128 * k, 128 * k + 128, p=(0, 32)), vw("one", p=(0, 32)), [[-4, 8], [0, 16]], A.is_equal, 0.0, -k, 1)
         mm(P(4 + k, 0, 384), vw("sq", 128 * k, 128 * k + 128, p=(0, 32)), vw("shph", p=(0, 32)))
-        act(vw("sht", 384 * k, 384 * k + 384), P(4 + k, 0, 384), AF.Identity if k or allv else AF.Silu, float(SO), 1.0, 0 if k or allv else 1560)
+        act(vw("sht", 384 * k, 384 * k + 384), P(4 + k, 0, 384), AF.Identity, float(SO))
     for k in range(3):
-        cp(vw("rct", 512 * k, 512 * k + 512), vw("reci", 512 * k, 512 * k + 512))
+        conv(vw("rct", 512 * k, 512 * k + 512), vw("reci", 512 * k, 512 * k + 512), k < ON["conv"][0])
     for k in range(2):
-        ts(vw("eb", 8 + 512 * k, 520 + 512 * k), vw("bndi", 512 * k, 512 * k + 512), 64.0, A.add)
+        conv(vw("eb", 8 + 512 * k, 520 + 512 * k), vw("bndi", 512 * k, 512 * k + 512), k < ON["conv"][1])
 
     def pairs(eq, W, Lf, wt, Sb, end):
         at = 0
@@ -321,7 +341,7 @@ def declare(guess):
             diag(P(6, 256, 272), Sb, "Zb")
 
     for t in range(RO):
-        o, v, vs = "o%d" % t, "v%d" % t, "vs%d" % t
+        o, v, vs, xs = "o%d" % t, "v%d" % t, "vs%d" % t, "XX"
         rot = t > 0
         hw = lambda name, h: vw(name, 128 * h, 128 * h + 128)
         hl_ = lambda name, h: vw(name, 8 * h, 8 * h + 8)
@@ -337,7 +357,7 @@ def declare(guess):
             cp(hw("xi", h), ind(vw("rct", 0, NV) if rot else vw("reci"), hl_(o, h)))
             ts(hw("c32", h), hw("xi", h), 4095, A.bitwise_and)
             ts(hw("p32", h), hw("xi", h), 12, A.arith_shift_right)
-            cp(hw("c16", h), hw("c32", h))
+            conv(hw("c16", h), hw("c32", h), ON["gc"][0] and h == HS[1])
 
         def main(h):
             bh = "bh%d" % h
@@ -350,7 +370,11 @@ def declare(guess):
 
             mm(P(h, 0, 128), Ib, hw(v, h))
             rows = (0, 128 if rot else 96)
-            mms([(P(e, 0, 384), hw(v, h), vw("nB3"), True, False), (P(e, 0, 256), vw("cl", p=rows), vw("cr", p=rows), False, False)])
+            na = 16 - ON["relu"][t][HS.index(h)]
+            d = lambda a, lo=0, hi=128: P(4 + h, 128 * (a - na) + lo, 128 * (a - na) + hi)
+            if na < 16:
+                mms([(d(a), vw("InI", 128, 256), hw(v, h), a == na, False) for a in range(na, 16)])
+            mms([(P(e, 0, 384), hw(v, h), vw("nB3" if na == 16 else "nB4"), True, False), (P(e, 0, 256), vw("cl", p=rows), vw("cr", p=rows), False, False)])
             for lo, hi, on in CUT[t][HS.index(h)]:
                 (cp if on else act)(vw(bh, 16 * lo, 16 * hi), ind(vw("boxt", 0, NB + NT * t), vw("c16", 128 * h + lo, 128 * h + hi)))
             if rot and h == HS[1]:
@@ -359,10 +383,14 @@ def declare(guess):
             if rot and h == HS[0]:
                 bounds()
             for k in range(0, 128, CH):
-                for q in range(4):
+                for q in range(0, na, 4):
                     calls = [(vw(bh, 2048 + 128 * a + k, 2048 + 128 * a + k + CH), vw(bh, 16 * k + a, 16 * (k + CH), 16), P(h, k, k + CH), A.max)
-                             for a in range(4 * q, 4 * q + 4)]
-                    add("V", "tt", calls, [vw(bh, 16 * k, 16 * (k + CH)), P(h, k, k + CH)], [x[0] for x in calls], 4 * max(64, CH))
+                             for a in range(q, min(q + 4, na))]
+                    add("V", "tt", calls, [vw(bh, 16 * k, 16 * (k + CH)), P(h, k, k + CH)], [x[0] for x in calls], len(calls) * max(64, CH))
+                if na < 16:
+                    mms([(d(a, k, k + CH), Ib, vw(bh, 16 * k + a, 16 * (k + CH), 16), False, a == 15 and k + CH == 128) for a in range(na, 16)])
+            for a in range(na, 16):
+                act(vw(bh, 2048 + 128 * a, 2176 + 128 * a), d(a), AF.Relu)
             for q in range(4):
                 if q == 3 and not rot:
                     bounds()
@@ -385,7 +413,7 @@ def declare(guess):
                 ts(W("hn"), ind(vw("bndi"), L("s16")), -4.0, A.mult)
                 return
             lin(W("hn"), ind(vw("eb", 0, 8 + S0 + NT), L("s16")), -4.0)
-            act(W("sgW"), W("hn"), AF.Sign, 4 * 4152.0)
+            act(W("sgW"), W("hn"), AF.Sign, 4 * 4088.0)
             for k in hs:
                 group(P(7, 8 * k, 8 * k + 8), (hw("sgW", k), vw("sr")), (vw("cl", p=(0, 32)), vw("cr", 0, 128, 16, p=(0, 32))))
             cp(W("cT", 16), P(7, 8 * lo, 8 * hi))
@@ -403,14 +431,12 @@ def declare(guess):
             cp(vw("yc16"), vw("ycol"))
             if t == 2:
                 ts(vw("n16"), vw("nLf"), 8.0 - SO, A.add)
-                act(vw("nsg"), ind(vw("eb", 0, 8 + NV), vw("n16")), AF.Sign, 4152.0, -1.0)
-                diag(P(7, 32, 48), "nsg", "Zq")
-                tt(vw("nqL"), vw("wL"), P(7, 32, 48), A.mult)
+                act(vw("nsg"), ind(vw("eb", 0, 8 + NV), vw("n16")), AF.Sign, 4088.0, -1.0)
 
         def owners():
-            for lo, hi in ((1, 2), (0, 1)) if ON["own"][t] else ((0, 2),):
+            for lo, hi in ((1, 2), (0, 1)) if rot else ((0, 2),):
                 cp(vw("oW", 128 * lo, 128 * hi), ind(vw("tab"), vw(o, 8 * lo, 8 * hi)))
-                cp(vw("lo", 16 * lo + 1, 16 * hi, 2), vw(o, 8 * lo, 8 * hi))
+                conv(vw("lo", 16 * lo + 1, 16 * hi, 2), vw(o, 8 * lo, 8 * hi), ON["gc"][1])
             pairs("eqo", "oW", lambda m: vw("lo", 2 * m + 1, 2 * m + 2), "wL", "So", lambda m: 128 * (m // 8 + 1))
             tt(vw("lo", 0, 32, 2), vw("wL"), P(6, 256, 272), A.is_le)
             scan(vw("lp"), vw("ld"), vw("lo"), 0.0, A.mult, A.max)
@@ -441,10 +467,14 @@ def declare(guess):
                 add("G", "send", (vw(ox, 0, 8), hl_("o%d" % (t + 1), h), "ao%d%d" % (t, h)), [vw(ox, 0, 8)], [],
                     900 + (2000 if (t, h) == (0, HS[0]) else 0), tag=("so", t, h))
             ts(hl_("nhL", h), P(w, 264, 272), 2048.0, A.is_ge)
-            tt(hl_("akw", h), hl_("nhL", h), hl_("nqL" if t == 2 else "wL", h), A.mult)
-            act(hw("XX", h), ind(vw("bh%d" % h), vw(ox, 8, 16)))
-            ts(hw("sg", h), hw("XX", h), bias("db1"), A.is_ge, -256.0, A.mult)
-            group(P(h, 256, 384), (Ib, hw("XX", h)), (Ib, hw("sg", h)))
+            tt(hl_("akw", h), hl_("nhL", h), hl_("wL", h), A.mult)
+            act(hw(xs, h), ind(vw("bh%d" % h), vw(ox, 8, 16)))
+            if ON["sg"]:
+                ts(hw("sg", h), hw(xs, h), bias("db1"), A.is_ge, -256.0, A.mult)
+                group(P(h, 256, 384), (Ib, hw(xs, h)), (Ib, hw("sg", h)))
+            else:
+                act(hw("sg", h), hw(xs, h), AF.Sign, bias("db1"))
+                group(P(h, 256, 384), (Ib, hw(xs, h)), (vw("mI"), hw("sg", h)))
             act(hw(vs, h), P(h, 256, 384), AF.Identity, bias("db2"))
             if t < 2:
                 add("G", "send", (hw(vs, h), hw("v%d" % (t + 1), h), "av%d%d" % (t, h)), [hw(vs, h)], [], 900, tag=("sv", t, h))
@@ -457,22 +487,25 @@ def declare(guess):
             else:
                 cp(ind(vw("rct"), hl_("ol", h)), hw("yy", h))
             if t < 2:
-                group(P(w, 0, 128), (Ib, hw("XX", h)), (Ib, hw(v, h)))
+                group(P(w, 0, 128), (Ib, hw(xs, h)), (Ib, hw(v, h)))
                 act(hw("bt", h), P(w, 0, 128), AF.Identity, MAGIC, 0.5 - 2.0 ** -11)
                 act(vw("boxt", NB + NT * t + 128 * h, NB + NT * t + 128 * h + 128), hw("bt", h), AF.Identity, -MAGIC)
 
         def makers():
             yo = vw("yo%d" % t)
             hs = vw("hy", 8 + NT, 8 + 2 * NT) if rot else vw("eb", 8 + S0, 8 + S0 + NT)
-            mms([(P(7, 128 * h, 128 * h + 128), hw("eS", h), vw("If"), True, True) for h in range(2)])
-            act(hs, P(7, 0, NT), AF.Identity, 0.0 if rot else 64.0)
+            for lo, hi in ((128, 256), (0, 128)) if ON["hs"][t] else ((0, 256),):
+                part_ = (hs[0], hs[1] + lo, hs[1] + hi, 1)
+                mms([(P(7, k, k + 128), vw("eS", k, k + 128), vw("If"), True, True) for k in range(lo, hi, 128)])
+                act(part_, P(7, lo, hi))
+                if rot:
+                    mm(P(7, 256 + lo, 256 + hi), vw("Rf"), part_)
+                    act(vw("hy", 8 + lo, 8 + hi), P(7, 256 + lo, 256 + hi))
             if rot:
-                mm(P(7, 256, 512), vw("Rf"), hs)
-                act(vw("hy", 8, 8 + NT), P(7, 256, 512))
                 (cp if ON["seen"] else act)(vw("seen"), ind(vw("hy"), vw("yc16")))
                 if t == 1:
                     group(P(7, 0, NT), (vw("Rb"), vw("seen")), (Ib, vw("bits")))
-                    act(vw("dat"), P(7, 0, NT), AF.Identity, col(13))
+                    act(vw("dat"), P(7, 0, NT), AF.Identity, bc(8))
             else:
                 lin(vw("ycol"), vw("iL"), 1.0, float(8 + S0))
                 group(P(7, 256, 512), (vw("Rb"), hs), (Ib, vw("bits")))
@@ -494,7 +527,7 @@ def declare(guess):
             if rot:
                 (cp if ON["yo"][t] else act)(yo, ind(vw("hy"), vw("yl")))
             else:
-                act(yo, ind(vw("eb", 0, 8 + S0 + NT), vw("yl")), AF.Identity, -64.0)
+                act(yo, ind(vw("eb", 0, 8 + S0 + NT), vw("yl")))
             tt(vw("nd", 1, 32, 2), vw("nLf" if rot else "sLf"), vw("wd", 1, 32, 2), A.subtract)
             scan(vw("ln"), vw("nd"), vw("wd"), 0.0, A.mult, A.add)
             ts(vw("nl"), vw("ln", 1, 32, 2), 8.0 - SO, A.add)
@@ -508,8 +541,8 @@ def declare(guess):
             else:
                 fn(h)
     dma("Q", "store", ("yv", "vs2", 0, 0, NT), [vw("vs2")], [], 65536)
-    dma("Q", "store", ("yr", "rct", 0, 0, 768), [vw("rct", 0, 768)], [], 393216)
-    dma("S", "store", ("yr", "rct", 768, 768, 768), [vw("rct", 768, NV)], [], 393216)
+    dma("Q", "store", ("yr", "rct", 0, 0, NV, 0, 64), [vw("rct", 0, NV)], [], 393216)
+    dma("S", "store", ("yr", "rct", 0, 0, NV, 64, 128), [vw("rct", 0, NV)], [], 393216)
     return ops, link(ops, HOP, NET)
 
 
@@ -709,7 +742,7 @@ def arrange(plans, rounds, seed):
     return sum(run(keep, 0, None, *tb)[0] for tb in tabs), keep
 
 
-GOALS = [["l00c16"], ["s00hn"], ["l10c16"], ["c00rp"], ["oo0ol"]]
+GOALS = [["s00sW"], ["oo0eqo"], ["l00c16"], ["s00hn"], ["l10c16"], ["c00rp"], ["oo0ol"]]
 for _t in range(2):
     GOALS += [[x % {"t": _t, "a": 2 * _t + HS[0], "b": 2 * _t + HS[1]}] for x in
               ("c0%(t)dox%(a)d", "c1%(t)dox%(b)d", "c0%(t)dvs%(t)d", "oo%(t)dsht", "c0%(t)drct", "c1%(t)drct", "c0%(t)dboxt", "c1%(t)dboxt",
@@ -717,7 +750,7 @@ for _t in range(2):
 GOALS += [["c02ox%d" % (4 + HS[0])], ["c12ox%d" % (4 + HS[1])], ["kk2rct"], ["kk2yo2", "kk2vs2"]]
 PLANS = [declare(x) for x in GUESS]
 OPS = PLANS[0][0]
-ORDER = min(arrange(PLANS, 20000, s) for s in (5, 77, 31, 8, 19, 23))[1]
+ORDER = min(arrange(PLANS, 40000, s) for s in (19, 5, 77, 8))[1]
 _pool = [i for i in ORDER if OPS[i]["kind"] in ("iota", "sel")]
 for _j, _i in zip(_pool, _pool[1:]):
     if any(len(OPS[k]["args"][0]) > 4 and OPS[k]["args"][0][4][0] for k in (_i, _j)):
@@ -791,7 +824,8 @@ def rank_program(g, core, T, topo):
         elif k == "load":
             ins = q.dma_start(T[a[0]][:, a[2]:a[3]], T[a[1]][:, a[2]:a[3]])
         elif k == "store":
-            ins = q.dma_start(T[a[0]][:, a[2]:a[2] + a[4]], T[a[1]][:, a[3]:a[3] + a[4]])
+            p0, p1 = a[5:] or (0, 128)
+            ins = q.dma_start(T[a[0]][p0:p1, a[2]:a[2] + a[4]], T[a[1]][p0:p1, a[3]:a[3] + a[4]])
         elif k == "cp":
             ins = q.tensor_copy(ap(a[0]), ap(a[1]))
         elif k == "tt":

import math
from concourse.mybir import AluOpType, ActivationFunctionType

NV, NB, S0, NT, RO = 1536, 3328, 1024, 256, 3
MAGIC = float(3 * 2 ** 22)
BETA = 1.8
SO = 512
EW = 8 + NV + NT
KS = 2.0 ** -22
HS = (1, 0)

F, B, H, I32, U = "float32", "bfloat16", "float16", "int32", "uint16"
_S = {
    "obi": (16, I32), "dri": (4, B), "reci": (NV, I32), "bndi": (S0, I32), "shpi": (384, I32), "shph": (384, H),
    "rct": (NV + NT, F), "boxt": (NB + 2 * NT, B), "eb": (EW, F), "sht": (NV + NT, F), "tab": (NV, F),
    "o0": (16, U), "o1": (16, U), "o2": (16, U), "v0": (NT, B), "v1": (NT, B), "v2": (NT, B),
    "ox0": (16, U), "ox1": (16, U), "ox2": (16, U), "ox3": (16, U), "ox4": (16, U), "ox5": (16, U),
    "vs0": (NT, B), "vs1": (NT, B), "vs2": (NT, B), "XX": (NT, B),
    "xi": (NT, I32), "c32": (NT, I32), "p32": (NT, I32), "c16": (NT, U),
    "bh0": (4096, B), "bh1": (4096, B),
    "sW": (NT, H), "nW": (NT, H), "oW": (NT, H), "nF": (NT, F), "hn": (NT, F), "sgW": (NT, B), "nsg": (NT, B), "rotW": (NT, B),
    "sLf": (16, F), "s16": (16, U), "nLf": (16, F), "n16": (16, U), "t3": (16, F), "ycol": (16, F), "nqL": (16, F),
    "cT": (NT, F), "rp": (NT, F), "sc": (288, F), "st": (288, B), "eS": (NT, F), "dg0": (NT, H), "dg1": (NT, H),
    "yy": (NT, F), "zz": (NT, F), "nhL": (16, F), "akw": (16, F), "sg": (NT, B), "bt": (NT, F),
    "eqo": (1152, B), "eqn": (2176, B), "So": (NT, B), "Sn": (NT, B),
    "lo": (32, F), "lp": (32, F), "ld": (32, F), "ol": (16, U), "wd": (32, F), "nd": (32, F), "ln": (32, F), "nl": (16, U),
    "y1": (16, F), "yl": (16, U),
    "hy": (8 + 2 * NT, F), "dat": (NT, F), "seen": (NT, F), "yc16": (16, U), "yo0": (NT, F), "yo1": (NT, F), "yo2": (NT, F),
    "cf": (32, F), "ci": (8, I32), "cj": (8, I32), "kq": (16, F),
    "InI": (384, B), "nI8k": (128, B), "B4k": (128, B), "B0": (128, B), "mI": (128, B),
    "If": (128, F), "Rf": (128, F), "Rb": (128, F), "RI": (128, F),
    "Bb": (128, B), "nB3": (384, B), "nB4": (384, B), "KW": (128, B), "Bq": (128, B), "Bm": (128, B), "wW": (NT, B), "RW": (128, B),
    "one": (128, B), "pm": (256, B), "s2": (24, B), "sm": (24, B), "sr": (8, B),
    "Zb": (144, B), "ZK": (144, B), "Zq": (144, B),
    "cl": (128, B), "cr": (256, B), "tl": (128, B), "tr": (256, B), "d0": (128, B), "bits": (NT, B),
    "sq": (512, B), "bc": (16, F), "fa": (16, F), "fb": (16, F), "fc": (16, F), "fd": (16, F), "fe": (16, F), "z16": (16, F),
    "iL": (16, F), "wL": (16, F), "c16i": (8, B), "yc": (16, F),
    "db1": (4, F), "db2": (4, F), "db3": (4, F),
}
PLACE = {}
SCRATCH = {}
for _k, (_n, _d) in _S.items():
    if _n <= 16 and _k not in ("obi", "dri", "o0", "o1", "o2", "ox0", "ox1", "ox2", "ox3"):
        _at = SCRATCH.get("pool_" + _d, (0, [128, 0]))[1][1]
        PLACE[_k] = ("pool_" + _d, _at)
        SCRATCH["pool_" + _d] = ("sbuf", [128, _at + 16], _d)
    else:
        SCRATCH[_k] = ("sbuf", [128, _n], _d)
for _b in range(8):
    SCRATCH["P%d" % _b] = ("psum", [128, 512], F)
_DMA = ["l%d" % k for k in range(16)]
_ARR = ["a%s%d%d" % (k, t, h) for k in "ov" for t in range(2) for h in range(2)]
SEMAPHORES = ["sV", "sS", "sP", "sG", "sent"] + _DMA + _ARR

A = AluOpType
AF = ActivationFunctionType
GUESS = ((1.56, 3.8, 0.5, 160, 3500, 300.0, 1300, 1.15), (1.3, 3.0, 0.58, 130, 2500, 400.0, 1000, 1.1), (1.8, 4.5, 0.5, 220, 4000, 240.0, 1600, 1.35),
         (1.4, 3.5, 0.5, 170, 4500, 210.0, 1900, 1.0))
Q4 = ((0, 32, 0), (32, 64, 0), (64, 96, 0), (96, 128, 0))
Q2 = ((0, 64, 0), (64, 128, 0))
Q3 = ((0, 64, 0), (64, 96, 0), (96, 128, 0))
V0 = ((0, 32, 0), (32, 64, 1), (64, 128, 0))
V1 = ((0, 32, 0), (32, 64, 0), (64, 96, 0), (96, 128, 1))
V2 = ((0, 40, 0), (40, 64, 1), (64, 104, 0), (104, 128, 1))
CUT = ((V0, Q2), (Q4, Q4), (Q4, Q4))
ON = {"conv": (3, 2), "relu": ((0, 0), (0, 0), (0, 0)), "hs": (0, 1, 1), "sg": 0, "gc": (0, 0), "sht": 0, "eb": (1, 1), "seen": 0, "yo": (0, 0, 0), "split": (0, 0, 0), "lin": 128, "fill": 72}
TG = 256
CH = 64


def vw(name, lo=0, hi=None, step=1, p=None):
    x = (name, lo, _S[name][0] if hi is None else hi, step)
    return x + (p,) if p else x


def ind(win, off):
    return ("@", win, off)


def wide(x):
    return x[0][0] == "P" or _S[x[0]][1] in (F, I32)


def count(x):
    return 16 * (x[2][2] - x[2][1]) if x[0] == "@" else (x[2] - x[1] + x[3] - 1) // x[3]


def declare(guess):
    RHO, SCAT, PEC, HOP, NET, RATE, FIX, SLOW = guess
    ops = []
    part = ["c"]
    allv = ON["sht"] and all(ON["eb"])

    def add(eng, kind, args, rd, wr, cost, **kw):
        r = []
        w = []
        for x in rd:
            if isinstance(x, tuple):
                r += [x[1], x[2]] if x[0] == "@" else [x]
        for x in wr:
            if x[0] == "@":
                w.append(x[1])
                r.append(x[2])
            else:
                w.append(x)
        name = part[0] + ((w or r or [("",)])[0][0] if part[0] != "c" else "")
        ops.append(dict(part=name, eng=eng, kind=kind, args=args, rd=r, wr=w, cost=cost * (1 if kind == "send" else SLOW), **kw))

    def vcost(out, in_, two=False):
        n = count(out)
        if out[0] == "@":
            return 60 + SCAT * n
        if in_[0] == "@":
            return 60 + RHO * n
        return max(64, n * (2 if two else (1 if wide(out) or wide(in_) else 0.5)))

    def cp(out, in_):
        add("V", "cp", (out, in_), [in_], [out], vcost(out, in_))

    def tt(out, a, b, op):
        psum = a[0][0] == "P" or b[0][0] == "P"
        add("V", "tt", [(out, a, b, op)], [a, b], [out], max(64, count(out)) if psum else vcost(out, a, True))

    def ts(out, a, s1, op0, s2=None, op1=None):
        add("V", "ts", (out, a, s1, s2, op0, op1), [a, s1, s2], [out], vcost(out, a))

    def ms(out, c):
        add("V", "ms", (out, c), [], [out], vcost(out, out))

    def scan(out, d0, d1, first, op0, op1):
        add("V", "scan", (out, d0, d1, first, op0, op1), [d0, d1, first], [out], max(64, count(out)))

    def act(out, in_, func=AF.Identity, bias=0.0, scale=1.0, more=0):
        n = count(out)
        cost = 80 + SCAT * n if out[0] == "@" else 80 + RHO * n if in_[0] == "@" else max(64, n)
        add("S", "act", (out, in_, func, bias, scale), [in_, bias, scale], [out], cost + more)

    def silu(out, in_):
        act(out, in_, AF.Silu)

    def mms(items):
        rd = []
        for x in items:
            rd += [y for y in x[1:3] if y not in rd]
        add("P", "mm", items, rd, [items[0][0]], sum(PEC * max(64, count(x[2])) * (4 if wide(x[1]) else 1) for x in items))

    def mm(out, l, r, start=True, stop=True):
        mms([(out, l, r, start, stop)])

    def group(out, *pairs_):
        mms([(out, l, r, k == 0, k == len(pairs_) - 1) for k, (l, r) in enumerate(pairs_)])

    def iota(out, pat, base, cm=0):
        add("G", "iota", (out, pat, base, cm), [], [out], 160 + 2 * count(out))

    def fill(out, c):
        if vcost(out, out) <= ON["fill"]:
            ms(out, float(c))
        else:
            iota(out, [[0, count(out)]], c)

    def sel(out, in_, pat, cmp, other, base, cm):
        add("G", "sel", (out, in_, pat, cmp, other, base, cm), [in_], [out], 200 + 2 * count(out))

    def conv(out, in_, pool):
        if pool:
            sel(out, in_, [[0, count(out)]], A.is_equal, 0.0, 0, 0)
        else:
            cp(out, in_)

    nd = [0, 0]

    def dma(q, kind, args, rd, wr, nbytes):
        nd[1] = nbytes + (nd[1] if kind != "store" or args[0] == "yr" else 0)
        add(q, kind, args, rd, wr, 60, sem=_DMA[nd[0]], lat=FIX + nd[1] / RATE)
        nd[0] += 1

    def P(b, lo, hi, step=1):
        return ("P%d" % b, lo, hi, step)

    def diag(out, src, z, extra=None, lo=0, hi=NT):
        mms([(out, vw(z, 15 - r, 143 - r), vw(src, lo + r, hi, 16), r == 0, r == 15 and extra is None) for r in range(16)]
            + ([extra + (False, True)] if extra else []))

    dma("S", "load", ("obi", "ob", 0, 16), [], [vw("obi")], 8192)
    dma("Q", "load", ("reci", "rec", 0, NV), [], [vw("reci")], 786432)
    dma("S", "shp", (), [], [vw("shpi")], 49152)
    dma("S", "load", ("v0", "tv", 0, NT), [], [vw("v0")], 65536)
    dma("S", "load", ("dri", "dr", 0, 3), [], [vw("dri", 0, 3)], 768)
    dma("Q", "load", ("boxt", "box", 0, NB), [], [vw("boxt", 0, NB)], 851968)
    dma("Q", "load", ("bndi", "bound", 0, S0), [vw("reci")], [vw("bndi")], 524288)
    ops[-1]["lat"] = 1490000 / RATE + FIX - 2000
    for k in range(1, 7):
        ops[k]["soft"] = {k - 1}
    cp(vw("o0"), vw("obi"))

    col = lambda k: vw("cf", k, k + 1)
    bc = lambda k: vw("bc", k, k + 1)

    def lin(out, in_, scale, bias=0.0):
        if in_[0] != "@" and count(out) >= ON["lin"] and not wide(out) and not wide(in_):
            ts(out, in_, scale, A.mult, bias, A.add)
        else:
            act(out, in_, AF.Identity, bias, scale)

    k16 = vw("kq")
    Ib, one = vw("InI", 0, 128), vw("one")
    blk = vw("Bb", 0, 128, 16)
    fill(one, 1)
    sel(Ib, one, [[-1, 128]], A.is_equal, 0.0, 0, 1)
    iota(k16, [[1, 16]], 0)
    iota(vw("ci", 0, 1), [[1, 1]], 0, 1)
    sel(vw("B0"), one, [[-16, 8], [0, 16]], A.is_ge, 0.0, 0, 1)
    sel(vw("Bb"), vw("B0"), [[16, 8], [0, 16]], A.is_ge, 0.0, 15, -1)
    iota(vw("tab", 0, TG), [[1, TG]], 0)
    for n in (256, 512, 1024):
        if n >= TG:
            lin(vw("tab", n, min(2 * n, NV)), vw("tab", 0, min(n, NV - n)), 1.0, float(n))
    ts(vw("cj", 0, 1), vw("ci", 0, 1), 15, A.bitwise_and)
    cp(col(1), vw("cj", 0, 1))
    ts(vw("bc"), k16, col(1), A.is_equal, 4096.0, A.mult)
    lin(col(9), col(1), 1.0, -2048.0)
    lin(vw("InI", 128, 256), Ib, -1.0)
    lin(vw("InI", 256, 384), Ib, 1.0)
    lin(vw("If"), Ib, 1.0)
    lin(vw("nI8k"), Ib, -8192.0)
    lin(vw("B4k"), vw("Bb"), 4096.0)
    for k, s in enumerate((32 * KS, 4.0, 1.0)):
        lin(vw("nB3", 128 * k, 128 * k + 128), vw("Bb"), -s)
        lin(vw("s2", 8 * k, 8 * k + 8), blk, 2 * s)
    lin(vw("sm"), vw("s2"), -0.5)
    nr = max(max(x) for x in ON["relu"])
    if nr:
        lin(vw("nB4"), vw("nB3"), 1.0)
        for a in range(16 - nr, 16):
            lin(vw("nB4", a, 384, 16), vw("nB3", a, 384, 16), -1.0)
    lin(vw("Rf", 0, 127), vw("If", 1, 128), 1.0)
    lin(vw("Rf", 15, 128, 16), vw("If", 0, 128, 16), 1.0)
    lin(vw("Rb", 1, 128), vw("If", 0, 127), 1.0)
    lin(vw("Rb", 0, 128, 16), vw("If", 15, 128, 16), 1.0)
    sel(vw("RI"), vw("Rf"), [[-1, 128]], A.not_equal, -1.0, 0, 1)
    fill(vw("Zb"), 0)
    lin(vw("Zb", 15, 143, 16), blk, 1.0)
    fill(vw("pm", 0, 128), 0.0625)
    fill(vw("pm", 128, 256), -0.0625)
    fill(vw("d0"), 0)
    lin(vw("d0", 0, 128, 16), vw("one", 0, 8), -1.0)
    for h in range(2):
        fill(vw("sc", 144 * h + 128, 144 * h + 144), 0)
    fill(vw("st", 0, 288, 144), 1)
    fill(vw("z16"), 0)
    ts(vw("fa"), k16, col(1), A.is_ge, 1.0 / BETA, A.max)
    scan(vw("fb"), vw("fa"), vw("z16"), BETA ** 64, A.mult, A.max)
    lin(vw("fc"), vw("one", 0, 16), BETA ** -16)
    lin(vw("fc", 0, 1), vw("one", 0, 1), BETA ** 64)
    scan(vw("wL"), vw("fc"), vw("z16"), vw("fb", 15, 16), A.mult, A.max)
    ts(vw("fd"), k16, col(1), A.is_lt, 1.0, A.add)
    scan(vw("fe"), vw("fd"), vw("z16"), -0.5, A.mult, A.min)
    ts(col(2), col(1), 10.5, A.is_lt, vw("fe", 15, 16), A.mult)
    lin(col(3), bc(11), 0.25, col(2))
    lin(col(10), bc(12), -2.0 ** -13, col(3))
    lin(col(4), bc(11), 2.0 ** -13)
    lin(col(11), bc(10), -2.0 ** -13, col(4))
    lin(col(14), col(11), 16 * KS)
    lin(vw("KW"), vw("Bb"), col(10))
    lin(vw("RW"), vw("Bb"), col(11))
    lin(vw("ZK"), vw("Zb"), col(10))
    lin(vw("sr"), blk, col(14))
    lin(col(15), col(11), 2.0 ** 90)
    ts(vw("Bq"), vw("Bb"), col(15), A.mult, 2.0 ** 26, A.mult)
    ts(vw("Bm"), vw("Bb"), -2.0 ** 90, A.mult, 2.0 ** 15, A.mult)
    act(vw("wW", 0, 1), vw("fc", 0, 1), AF.Identity, 0.0, -2.5 * BETA ** 64)
    for k in range(8):
        act(vw("wW", 2 ** k, 2 ** (k + 1)), vw("wW", 0, 2 ** k), AF.Identity, 0.0, BETA ** -(2 ** k))
    lin(vw("bits", 0, 1), bc(9), 1.0, bc(10))
    for k in range(8):
        lin(vw("bits", 2 ** k, 2 ** (k + 1)), vw("bits", 0, 2 ** k), 1.0, bc(k))
    row = lambda name, p, c, lo=0, hi=128, n=1: ms(vw(name, lo, hi, p=(p, p + n)), c)
    fill(vw("cl"), 0)
    for p, c in ((0, 2.0 ** 17 * KS), (32, KS), (64, -2.0), (96, 2048 * 4.0)):
        row("cl", p, c)
    iota(vw("cr", 0, 128), [[0, 8], [1, 16]], 0)
    iota(vw("cr", 0, 128, p=(0, 32)), [[-1, 8], [0, 16]], 7)
    row("cr", 64, 0.0, 0, 128, 64)
    fill(vw("cr", 128, 256), 0)
    row("cr", 64, 1.0, 128, 256, 64)
    fill(vw("tl"), 0)
    iota(vw("tl", p=(0, 1)), [[0, 8], [1, 16]], 0)
    for p, c in ((32, 1.0), (64, -2048.0), (96, 1.0)):
        row("tl", p, c)
    iota(vw("tr"), [[1, NT]], 0)
    fill(vw("tr", p=(0, 1)), 8192)
    lin(vw("tr", p=(64, 65)), vw("tr", p=(64, 65)), 0.0, 8192.0)
    mm(P(0, 256, 384), vw("cl", p=(0, 64)), vw("cr", 0, 128, p=(0, 64)))
    for h in range(2):
        act(vw("cT", 128 * h, 128 * h + 128), P(0, 256, 384))
    lin(vw("iL"), k16, 16.0, col(1))
    lin(vw("c16i"), vw("iL", 0, 8), 16.0, 2048.0)
    fill(vw("ld"), 0)
    fill(vw("nd"), 0)
    lin(vw("ld", 1, 32, 2), vw("iL"), 1.0, float(NV))
    lin(vw("wd", 1, 32, 2), vw("iL"), 1.0, float(SO + NV))
    lin(vw("yc"), vw("iL"), 1.0, float(8 + NT))
    if ON["sg"]:
        lin(vw("db1", 0, 3), vw("dri", 0, 3), -1.0, 256.0)
        lin(vw("db2", 0, 3), vw("dri", 0, 3), 1.0)
    else:
        lin(vw("db1", 0, 3), vw("dri", 0, 3), 1.0, -255.5)
        lin(vw("db2", 0, 3), vw("dri", 0, 3), 1.0, -128.0)
        lin(vw("mI"), Ib, -128.0)
    lin(vw("db3", 0, 3), vw("dri", 0, 3), -1.0)
    fill(vw("eb", 0, 8), 0)
    if allv:
        fill(vw("eb", 8 + S0 + NT, EW), 0)
    else:
        fill(vw("eb", 8 + NV, EW), 0)
        act(vw("eb", 8 + S0 + NT, 8 + NV), vw("tab", 0, NT), AF.Silu, 0.0, 0.0, 1560)
    fill(vw("rct", NV, NV + NT), 0)
    fill(vw("sht", NV, NV + NT), 0)
    fill(vw("hy", 0, 8), 0)
    cp(vw("shph", p=(0, 32)), vw("shpi", p=(0, 32)))
    for k in range(4):
        sel(vw("sq", 128 * k, 128 * k + 128, p=(0, 32)), vw("one", p=(0, 32)), [[-4, 8], [0, 16]], A.is_equal, 0.0, -k, 1)
        mm(P(4 + k, 0, 384), vw("sq", 128 * k, 128 * k + 128, p=(0, 32)), vw("shph", p=(0, 32)))
        act(vw("sht", 384 * k, 384 * k + 384), P(4 + k, 0, 384), AF.Identity, float(SO))
    for k in range(3):
        conv(vw("rct", 512 * k, 512 * k + 512), vw("reci", 512 * k, 512 * k + 512), k < ON["conv"][0])
    for k in range(2):
        conv(vw("eb", 8 + 512 * k, 520 + 512 * k), vw("bndi", 512 * k, 512 * k + 512), k < ON["conv"][1])

    def pairs(eq, W, Lf, wt, Sb, end):
        at = 0
        for k, m in enumerate([8 * h + x for h in HS for x in range(8)]):
            n = end(m) - 16 * m
            ts(vw(eq, at, at + n), vw(W, 16 * m, end(m)), Lf(m), A.is_equal, vw(wt, m, m + 1), A.mult)
            cuts = (0, 128, n) if m == 0 and n > 128 else (0, n)
            mms([(P(6, 16 * m + x, 16 * m + y), vw("Bb"), vw(eq, at + x, at + y), k == 0 and bool(Sb), k == 15) for x, y in zip(cuts, cuts[1:])])
            at += n
        if Sb:
            act(vw(Sb), P(6, 0, NT), AF.Identity, 0.0, 1.0 / 40)
            diag(P(6, 256, 272), Sb, "Zb")

    for t in range(RO):
        o, v, vs, xs = "o%d" % t, "v%d" % t, "vs%d" % t, "XX"
        rot = t > 0
        hw = lambda name, h: vw(name, 128 * h, 128 * h + 128)
        hl_ = lambda name, h: vw(name, 8 * h, 8 * h + 8)
        bias = lambda name: vw(name, t, t + 1)
        fill(vw("tr", p=(96, 97)), NB + NT * t)
        if rot:
            for h in range(2):
                add("X", "recv", ("ao%d%d" % (t - 1, h),), [], [hl_(o, h)], 0, after=("so", t - 1, h))
                add("X", "recv", ("av%d%d" % (t - 1, h),), [], [hw(v, h)], 0, after=("sv", t - 1, h))
            dma("Q", "store", ("yh", "yo%d" % (t - 1), NT * (t - 1), 0, NT), [vw("yo%d" % (t - 1)), vw(v)], [], 131072)

        def lists(h):
            cp(hw("xi", h), ind(vw("rct", 0, NV) if rot else vw("reci"), hl_(o, h)))
            ts(hw("c32", h), hw("xi", h), 4095, A.bitwise_and)
            ts(hw("p32", h), hw("xi", h), 12, A.arith_shift_right)
            conv(hw("c16", h), hw("c32", h), ON["gc"][0] and h == HS[1])

        def main(h):
            bh = "bh%d" % h
            e = 2 + h

            def bounds():
                mm(P(e, 128, 256), hw("hn", h), vw("If"), False, False)
                if rot:
                    mms([(P(e, 128, 256), hw("sgW", h), vw("nI8k"), False, False), (P(e, 0, 128, 16), hw("sgW", h), vw("sr"), False, False)])

            mm(P(h, 0, 128), Ib, hw(v, h))
            rows = (0, 128 if rot else 96)
            na = 16 - ON["relu"][t][HS.index(h)]
            d = lambda a, lo=0, hi=128: P(4 + h, 128 * (a - na) + lo, 128 * (a - na) + hi)
            if na < 16:
                mms([(d(a), vw("InI", 128, 256), hw(v, h), a == na, False) for a in range(na, 16)])
            mms([(P(e, 0, 384), hw(v, h), vw("nB3" if na == 16 else "nB4"), True, False), (P(e, 0, 256), vw("cl", p=rows), vw("cr", p=rows), False, False)])
            for lo, hi, on in CUT[t][HS.index(h)]:
                (cp if on else act)(vw(bh, 16 * lo, 16 * hi), ind(vw("boxt", 0, NB + NT * t), vw("c16", 128 * h + lo, 128 * h + hi)))
            if rot and h == HS[1]:
                bounds()
            mms([(P(e, a, 384, 16), vw(bh, a, 2048, 16), vw("sm"), False, False) for a in range(16)])
            if rot and h == HS[0]:
                bounds()
            for k in range(0, 128, CH):
                for q in range(0, na, 4):
                    calls = [(vw(bh, 2048 + 128 * a + k, 2048 + 128 * a + k + CH), vw(bh, 16 * k + a, 16 * (k + CH), 16), P(h, k, k + CH), A.max)
                             for a in range(q, min(q + 4, na))]
                    add("V", "tt", calls, [vw(bh, 16 * k, 16 * (k + CH)), P(h, k, k + CH)], [x[0] for x in calls], len(calls) * max(64, CH))
                if na < 16:
                    mms([(d(a, k, k + CH), Ib, vw(bh, 16 * k + a, 16 * (k + CH), 16), False, a == 15 and k + CH == 128) for a in range(na, 16)])
            for a in range(na, 16):
                act(vw(bh, 2048 + 128 * a, 2176 + 128 * a), d(a), AF.Relu)
            for q in range(4):
                if q == 3 and not rot:
                    bounds()
                mms([(P(e, a, 384, 16), vw(bh, 2048 + 128 * a, 2176 + 128 * a), vw("s2"), False, a == 15) for a in range(4 * q, 4 * q + 4)])
            act(vw(bh, 2048, 4096, 16), hw(v, h), AF.Identity, bias("db3"))

        def shapes(h):
            if not ON["split"][t] and h == HS[1]:
                return
            hs = (h,) if ON["split"][t] else HS
            lo, hi = min(hs), max(hs) + 1
            W = lambda name, step=1: vw(name, 128 * lo, 128 * hi, step)
            L = lambda name: vw(name, 8 * lo, 8 * hi)
            ps = P(4 + h, 272, 272 + 8 * (hi - lo))
            cp(W("sW"), ind(vw("sht", 0, NV), L(o)))
            diag(ps, "sW", "Zb", None, 128 * lo, 128 * hi)
            ts(L("s16"), ps, 0.0625, A.mult, (8.0 if rot else 0.0) - SO, A.add)
            act(L("sLf"), ps, AF.Identity, 0.0, 0.0625)
            if not rot:
                ts(W("hn"), ind(vw("bndi"), L("s16")), -4.0, A.mult)
                return
            lin(W("hn"), ind(vw("eb", 0, 8 + S0 + NT), L("s16")), -4.0)
            act(W("sgW"), W("hn"), AF.Sign, 4 * 4088.0)
            for k in hs:
                group(P(7, 8 * k, 8 * k + 8), (hw("sgW", k), vw("sr")), (vw("cl", p=(0, 32)), vw("cr", 0, 128, 16, p=(0, 32))))
            cp(W("cT", 16), P(7, 8 * lo, 8 * hi))
            if HS[1] not in hs:
                return
            pk = P(7, 16, 32)
            mm(P(7, 256, 512), vw("RW"), vw("sgW"))
            diag(pk, "sgW", "ZK")
            act(vw("rotW"), P(7, 256, 512))
            tt(vw("nLf"), vw("sLf"), pk, A.max)
            ts(vw("t3"), pk, 0.0, A.is_gt, -float(NT), A.mult)
            tt(vw("ycol"), vw("t3"), vw("yc"), A.add)
            mm(P(7, 256, 512), vw("KW"), vw("sgW"))
            tt(vw("nF" if t == 1 else "nW"), vw("sW"), P(7, 256, 512), A.max)
            cp(vw("yc16"), vw("ycol"))
            if t == 2:
                ts(vw("n16"), vw("nLf"), 8.0 - SO, A.add)
                act(vw("nsg"), ind(vw("eb", 0, 8 + NV), vw("n16")), AF.Sign, 4088.0, -1.0)

        def owners():
            for lo, hi in ((1, 2), (0, 1)) if rot else ((0, 2),):
                cp(vw("oW", 128 * lo, 128 * hi), ind(vw("tab"), vw(o, 8 * lo, 8 * hi)))
                conv(vw("lo", 16 * lo + 1, 16 * hi, 2), vw(o, 8 * lo, 8 * hi), ON["gc"][1])
            pairs("eqo", "oW", lambda m: vw("lo", 2 * m + 1, 2 * m + 2), "wL", "So", lambda m: 128 * (m // 8 + 1))
            tt(vw("lo", 0, 32, 2), vw("wL"), P(6, 256, 272), A.is_le)
            scan(vw("lp"), vw("ld"), vw("lo"), 0.0, A.mult, A.max)
            cp(vw("ol"), vw("lp", 1, 32, 2))
            if t == 1:
                for h in HS:
                    (cp if ON["sht"] else silu)(ind(vw("sht"), hl_("ol", h)), hw("nF", h))

        def choose(h):
            e, w = 2 + h, 4 + h
            dg = "dg%d" % h
            st = lambda k: vw("st", 144 * h + k, 144 * h + k + 128)
            tt(hw("rp", h), hw("cT", h), P(e, 128, 256), A.max)
            sc = lambda k: vw("sc", 144 * h + k, 144 * h + k + 128)
            scan(sc(0), hw("rp", h), P(e, 0, 128), 1.0, A.min, A.min)
            act(hw("eS", h), P(e, 256, 384))
            scan(P(h, 128, 256), vw("d0"), sc(15), 0.0, A.add, A.max)
            tt(st(1), sc(0), P(h, 128, 256), A.is_equal)
            mm(P(w, 0, 256), vw("Zb", 15, 143), vw("pm"), True, False)
            mm(P(w, 128, 256), hw("rp", h), vw("If"), False, False)
            mms([(P(w, 0, 256), st(1), vw("InI", 0, 256), False, False), (P(w, 0, 256), st(0), vw("InI", 128, 384), False, True)])
            tt(vw(dg, 0, 128), hw("p32", h), P(w, 0, 128), A.mult)
            ts(vw(dg, 128, 256), P(w, 128, 256), -0.5, A.is_lt, col(9), A.mult)
            diag(P(w, 256, 272), dg, "Zb", (P(w, 264, 272), Ib, vw("c16i")))
            ox = "ox%d" % (2 * t + h)
            cp(vw(ox), P(w, 256, 272))
            if t < 2:
                add("G", "send", (vw(ox, 0, 8), hl_("o%d" % (t + 1), h), "ao%d%d" % (t, h)), [vw(ox, 0, 8)], [],
                    900 + (2000 if (t, h) == (0, HS[0]) else 0), tag=("so", t, h))
            ts(hl_("nhL", h), P(w, 264, 272), 2048.0, A.is_ge)
            tt(hl_("akw", h), hl_("nhL", h), hl_("wL", h), A.mult)
            act(hw(xs, h), ind(vw("bh%d" % h), vw(ox, 8, 16)))
            if ON["sg"]:
                ts(hw("sg", h), hw(xs, h), bias("db1"), A.is_ge, -256.0, A.mult)
                group(P(h, 256, 384), (Ib, hw(xs, h)), (Ib, hw("sg", h)))
            else:
                act(hw("sg", h), hw(xs, h), AF.Sign, bias("db1"))
                group(P(h, 256, 384), (Ib, hw(xs, h)), (vw("mI"), hw("sg", h)))
            act(hw(vs, h), P(h, 256, 384), AF.Identity, bias("db2"))
            if t < 2:
                add("G", "send", (hw(vs, h), hw("v%d" % (t + 1), h), "av%d%d" % (t, h)), [hw(vs, h)], [], 900, tag=("sv", t, h))
            group(P(e, 384, 512), (vw("tl"), hw("tr", h)), (vw("nI8k"), vw(dg, 128, 256)), (vw("B4k"), vw(dg, 0, 128)))
            tt(hw("yy", h), hw("xi", h), P(e, 384, 512), A.max)
            if rot:
                mm(P(e, 0, 128), vw("RI"), hw("yy", h))
                tt(hw("zz", h), hw("rotW", h), P(e, 0, 128), A.mult)
                tt(ind(vw("rct"), hl_("ol", h)), hw("yy", h), hw("zz", h), A.add)
            else:
                cp(ind(vw("rct"), hl_("ol", h)), hw("yy", h))
            if t < 2:
                group(P(w, 0, 128), (Ib, hw(xs, h)), (Ib, hw(v, h)))
                act(hw("bt", h), P(w, 0, 128), AF.Identity, MAGIC, 0.5 - 2.0 ** -11)
                act(vw("boxt", NB + NT * t + 128 * h, NB + NT * t + 128 * h + 128), hw("bt", h), AF.Identity, -MAGIC)

        def makers():
            yo = vw("yo%d" % t)
            hs = vw("hy", 8 + NT, 8 + 2 * NT) if rot else vw("eb", 8 + S0, 8 + S0 + NT)
            for lo, hi in ((128, 256), (0, 128)) if ON["hs"][t] else ((0, 256),):
                part_ = (hs[0], hs[1] + lo, hs[1] + hi, 1)
                mms([(P(7, k, k + 128), vw("eS", k, k + 128), vw("If"), True, True) for k in range(lo, hi, 128)])
                act(part_, P(7, lo, hi))
                if rot:
                    mm(P(7, 256 + lo, 256 + hi), vw("Rf"), part_)
                    act(vw("hy", 8 + lo, 8 + hi), P(7, 256 + lo, 256 + hi))
            if rot:
                (cp if ON["seen"] else act)(vw("seen"), ind(vw("hy"), vw("yc16")))
                if t == 1:
                    group(P(7, 0, NT), (vw("Rb"), vw("seen")), (Ib, vw("bits")))
                    act(vw("dat"), P(7, 0, NT), AF.Identity, bc(8))
            else:
                lin(vw("ycol"), vw("iL"), 1.0, float(8 + S0))
                group(P(7, 256, 512), (vw("Rb"), hs), (Ib, vw("bits")))
                act(vw("dat"), P(7, 256, 512))
            if t == 2:
                mms([(P(6, 0, NT), Ib, vw("wW"), True, False), (P(6, 0, NT), vw("Bq"), vw("nsg"), False, False)])
                for h in HS:
                    mm(P(6, 128 * h, 128 * h + 128), vw("Bm"), vw("dg%d" % h, 128, 256), False, False)
                pairs("eqn", "nW", lambda m: vw("nLf", m, m + 1), "akw", None, lambda m: NT)
                ts(P(6, 256, 512), P(6, 0, NT), 0.0, A.is_lt)
                tt(yo, vw("seen"), P(6, 256, 512), A.mult)
                dma("Q", "store", ("yh", "yo2", NT * t, 0, NT), [yo], [], 131072)
                return
            pairs("eqn", "sW", lambda m: vw("sLf", m, m + 1), "akw", "Sn", lambda m: NT)
            wn = vw("wd", 0, 32, 2)
            tt(wn, vw("akw"), P(6, 256, 272), A.is_gt)
            tt(vw("y1"), wn, vw("ycol"), A.mult)
            cp(vw("yl"), vw("y1"))
            if rot:
                (cp if ON["yo"][t] else act)(yo, ind(vw("hy"), vw("yl")))
            else:
                act(yo, ind(vw("eb", 0, 8 + S0 + NT), vw("yl")))
            tt(vw("nd", 1, 32, 2), vw("nLf" if rot else "sLf"), vw("wd", 1, 32, 2), A.subtract)
            scan(vw("ln"), vw("nd"), vw("wd"), 0.0, A.mult, A.add)
            ts(vw("nl"), vw("ln", 1, 32, 2), 8.0 - SO, A.add)
            (cp if ON["eb"][t] else silu)(ind(vw("eb"), vw("nl")), vw("dat"))

        for name, fn, h in (("l0", lists, HS[0]), ("l1", lists, HS[1]), ("s0", shapes, HS[0]), ("m0", main, HS[0]), ("s1", shapes, HS[1]),
                            ("oo", owners, None), ("m1", main, HS[1]), ("c0", choose, HS[0]), ("c1", choose, HS[1]), ("kk", makers, None)):
            part[0] = "%s%d" % (name, t)
            if h is None:
                fn()
            else:
                fn(h)
    dma("Q", "store", ("yv", "vs2", 0, 0, NT), [vw("vs2")], [], 65536)
    dma("Q", "store", ("yr", "rct", 0, 0, NV, 0, 64), [vw("rct", 0, NV)], [], 393216)
    dma("S", "store", ("yr", "rct", 0, 0, NV, 64, 128), [vw("rct", 0, NV)], [], 393216)
    return ops, link(ops, HOP, NET)


def meet(x, y):
    if x[1] >= y[2] or y[1] >= x[2] or (x[3] == y[3] == 2 and (x[1] - y[1]) % 2):
        return False
    return len(x) < 5 or len(y) < 5 or (x[4][0] < y[4][1] and y[4][0] < x[4][1])


def link(ops, hop, net):
    last = {}
    tags = {}
    phase = {}
    for i, op in enumerate(ops):
        deps = set()
        sides = [(x, False) for x in op["rd"]] + [(x, True) for x in op["wr"]]
        for x, w in sides:
            if x[0][0] == "P":
                before, now = phase.get(x[0], ([], []))
                if now and ops[now[-1]]["eng"] != op["eng"]:
                    before, now = (now[-1:] if ops[now[-1]]["eng"] == "P" else now), []
                deps.update(before)
                if op["eng"] == "P":
                    op["soft"] = set(now[-1:])
                phase[x[0]] = (before, now + [i])
                if op["eng"] == "P":
                    continue
            for j, y, wj in last.get(x[0], []):
                if j != i and (w or wj) and meet(x, y):
                    deps.add(j)
        for x, w in sides:
            if x[0][0] == "P" and op["eng"] == "P":
                last[x[0]] = []
                continue
            old = last.get(x[0], [])
            if w and x[3] == 1 and len(x) < 5:
                old = [z for z in old if not (x[1] <= z[1][1] and z[1][2] <= x[2])]
            last[x[0]] = old + [(i, x, w)]
        op["deps"] = deps
        if "tag" in op:
            tags[op["tag"]] = i
    pre = []
    for op in ops:
        p = [(j, hop + ops[j].get("lat", 0)) for j in sorted(op["deps"])] + [(j, 0) for j in op.get("soft", ()) if j not in op["deps"]]
        if "after" in op:
            p.append((tags[op["after"]], net))
        pre.append(p)
    return pre


def place(cost, eng, before, key):
    n = len(cost)
    after = [[] for _ in cost]
    left = [len(p) for p in before]
    for i, p in enumerate(before):
        for j, l in p:
            after[j].append(i)
    ready = sorted((key[i], i) for i in range(n) if not left[i])
    slots = [[] for _ in range(6)]
    t0 = [0.0] * n
    while ready:
        i = ready.pop(0)[1]
        c = cost[i]
        s = max([t0[j] + cost[j] + l for j, l in before[i]] + [0.0])
        sl = slots[eng[i]]
        lo = 0
        while lo < len(sl) and sl[lo][1] <= s:
            lo += 1
        while lo < len(sl) and sl[lo][0] < s + c:
            s = max(s, sl[lo][1])
            lo += 1
        sl.insert(lo, (s, s + c))
        t0[i] = s
        for k in after[i]:
            left[k] -= 1
            if not left[k]:
                ready.append((key[k], k))
        ready.sort()
    return t0


def arrange(plans, rounds, seed):
    ops, pre = plans[0]
    n = len(ops)
    eng = ["VSPGQX".index(o["eng"]) for o in ops]
    tabs = [([o["cost"] for o in p[0]], [o.get("lat", 0) for o in p[0]], p[1]) for p in plans]
    state = [seed]

    def rnd(k):
        state[0] = (state[0] * 1103515245 + 12345) % 2147483648
        return (state[0] >> 8) % k

    cost = tabs[0][0]
    key = [None] * n
    for rank, goal in enumerate(GOALS):
        far = {i: cost[i] for i in range(n) if ops[i]["part"] in goal and key[i] is None}
        for i in range(n - 1, -1, -1):
            if i in far:
                for j, l in pre[i]:
                    if key[j] is None:
                        far[j] = max(far.get(j, 0), far[i] + l + cost[j])
        for i, d in far.items():
            key[i] = (rank, -d)
    best = place(cost, eng, pre, [k or (len(GOALS), i) for i, k in enumerate(key)])
    cur = sorted(range(n), key=lambda i: (best[i], i))
    above = [set(j for j, l in p) for p in pre]
    below = [set() for _ in ops]
    for i, p in enumerate(pre):
        for j, l in p:
            below[j].add(i)
    ends = [i for i in range(n) if not below[i]]

    def run(order, a, old, cost, lat, pre):
        t, why = (list(old[3]), list(old[1])) if old else ([0.0] * n, [0] * n)
        last = [-1] * 6
        for i in order[:a]:
            last[eng[i]] = i
        free = [t[i] if i >= 0 else 0.0 for i in last]
        for i in order[a:]:
            e = eng[i]
            s = free[e]
            w = -2 - last[e]
            for j, l in pre[i]:
                x = t[j] + l
                if x >= s:
                    s = x
                    w = j
            why[i] = w
            t[i] = free[e] = s + cost[i]
            last[e] = i
        top = max(ends, key=lambda i: t[i] + lat[i])
        return t[top] + lat[top], why, top, t

    res = [run(cur, 0, None, *tb) for tb in tabs]
    unit = [r[0] for r in res]
    now = low = float(len(res))
    keep = cur
    for k in range(rounds):
        _, why, i, _ = res[rnd(len(res))]
        held = []
        while why[i] != -1:
            if why[i] < -1:
                held.append((i, -2 - why[i]))
                i = -2 - why[i]
            else:
                i = why[i]
        if not held:
            continue
        i, j = held[rnd(len(held))]
        a = cur.index(j)
        b = cur.index(i)
        if rnd(2):
            for _ in range((0, 0, 0, 1, 2, 4, 8, 16)[rnd(8)]):
                p = a - 1
                while p >= 0 and eng[cur[p]] != eng[i]:
                    p -= 1
                if p >= 0:
                    a = p
            need = set(above[i])
            moved = [i]
            for x in cur[b - 1:a:-1]:
                if x in need:
                    moved.append(x)
                    need |= above[x]
            if cur[a] in need:
                continue
            inside = set(moved)
            new = cur[:a] + moved[::-1] + [x for x in cur[a:b] if x not in inside] + cur[b + 1:]
        else:
            for _ in range((0, 0, 1, 2, 4, 8, 16, 32)[rnd(8)]):
                p = b + 1
                while p < n and eng[cur[p]] != eng[i]:
                    p += 1
                if p < n:
                    b = p
            need = set(below[j])
            moved = [j]
            for x in cur[a + 1:b]:
                if x in need:
                    moved.append(x)
                    need |= below[x]
            if cur[b] in need:
                continue
            inside = set(moved)
            new = cur[:a] + [x for x in cur[a:b + 1] if x not in inside] + moved + cur[b + 1:]
        limit = now - (0.0015 * (1.0 - k / rounds) + 0.0001) * math.log((rnd(1000) + 1) / 1001.0)
        r = []
        for z, tb in enumerate(tabs):
            r.append(run(new, a, res[z], *tb))
            v = sum(x[0] / u for x, u in zip(r + res[z + 1:], unit))
            if v > limit + 0.004:
                break
        if v <= limit and len(r) == len(tabs):
            cur, now, res = new, v, r
            if v < low:
                keep, low = new, v
    return sum(run(keep, 0, None, *tb)[0] for tb in tabs), keep


GOALS = [["s00sW"], ["oo0eqo"], ["l00c16"], ["s00hn"], ["l10c16"], ["c00rp"], ["oo0ol"]]
for _t in range(2):
    GOALS += [[x % {"t": _t, "a": 2 * _t + HS[0], "b": 2 * _t + HS[1]}] for x in
              ("c0%(t)dox%(a)d", "c1%(t)dox%(b)d", "c0%(t)dvs%(t)d", "oo%(t)dsht", "c0%(t)drct", "c1%(t)drct", "c0%(t)dboxt", "c1%(t)dboxt",
               "kk%(t)deb", "c1%(t)dvs%(t)d")]
GOALS += [["c02ox%d" % (4 + HS[0])], ["c12ox%d" % (4 + HS[1])], ["kk2rct"], ["kk2yo2", "kk2vs2"]]
PLANS = [declare(x) for x in GUESS]
OPS = PLANS[0][0]
ORDER = min(arrange(PLANS, 40000, s) for s in (19, 5, 77, 8))[1]
_pool = [i for i in ORDER if OPS[i]["kind"] in ("iota", "sel")]
for _j, _i in zip(_pool, _pool[1:]):
    if any(len(OPS[k]["args"][0]) > 4 and OPS[k]["args"][0][4][0] for k in (_i, _j)):
        OPS[_i]["deps"].add(_j)


def rank_program(g, core, T, topo):
    rank = T.rank_of(core)
    if rank is None:
        return
    nxt = T.cores[(rank + 1) % len(T.cores)]
    prv = T.cores[(rank - 1) % len(T.cores)]
    rid, pid, _ = topo.addr(nxt)
    eng = topo.engines(core, nxt)[:8]
    mask = sum(1 << e for e in eng)
    n_in = len(topo.engines(prv, core)[:8])
    Q = {"V": g.vector, "S": g.scalar, "P": g.tensor, "G": g, "Q": g.sync}

    def ap(x):
        if not isinstance(x, tuple):
            return x
        if x[0] == "@":
            return ap(x[1]).indirect(ap(x[2]))
        name, at = PLACE.get(x[0], (x[0], 0))
        p0, p1 = x[4] if len(x) > 4 else (0, 128)
        return T[name][p0:p1, at + x[1]:at + x[2]] if x[3] == 1 else T[name][p0:p1, at + x[1]:at + x[2]:x[3]]

    needed = set()
    for op in OPS:
        needed |= op["deps"]
    mark = {}
    cnt = {e: 0 for e in "VSPG"}
    for i in ORDER:
        op = OPS[i]
        if op["kind"] == "recv":
            mark[i] = (op["args"][0], n_in)
        elif "sem" in op:
            mark[i] = (op["sem"], 16)
        elif i in needed:
            cnt[op["eng"]] += 1
            mark[i] = ("s" + op["eng"], cnt[op["eng"]])
    seen = {e: {} for e in Q}
    known = {}
    top = {}
    sends = 0
    for i in ORDER:
        op = OPS[i]
        e, k, a = op["eng"], op["kind"], op["args"]
        if k == "recv":
            top[a[0]] = n_in
            continue
        q = Q[e]
        want = {}
        for j in op["deps"]:
            s, c = mark[j]
            want[s] = max(want.get(s, 0), c)
        want = {s: c for s, c in want.items() if seen[e].get(s, 0) < c}
        for s in sorted(want):
            if not any(known.get((z, want[z]), {}).get(s, 0) >= want[s] for z in want if z != s):
                q.wait_ge(T.sem[s], want[s])
        for s in want:
            seen[e][s] = max(seen[e].get(s, 0), want[s])
            for z, c in known.get((s, want[s]), {}).items():
                seen[e][z] = max(seen[e].get(z, 0), c)
        if k == "send":
            g.remote_dma(ap(a[1]), ap(a[0]), T.sem[a[2]], T.sem.sent, pid, rid, mask)
            sends += 1
            continue
        if k == "shp":
            ins = q.dma_start(T.shpi[0:32, :], T.shp[:])
        elif k == "load":
            ins = q.dma_start(T[a[0]][:, a[2]:a[3]], T[a[1]][:, a[2]:a[3]])
        elif k == "store":
            p0, p1 = a[5:] or (0, 128)
            ins = q.dma_start(T[a[0]][p0:p1, a[2]:a[2] + a[4]], T[a[1]][p0:p1, a[3]:a[3] + a[4]])
        elif k == "cp":
            ins = q.tensor_copy(ap(a[0]), ap(a[1]))
        elif k == "tt":
            for x in a:
                ins = q.tensor_tensor(ap(x[0]), ap(x[1]), ap(x[2]), x[3])
        elif k == "ts":
            if a[5] is None:
                ins = q.tensor_scalar(ap(a[0]), ap(a[1]), ap(a[2]), None, a[4])
            else:
                ins = q.tensor_scalar(ap(a[0]), ap(a[1]), ap(a[2]), ap(a[3]), a[4], a[5])
        elif k == "ms":
            ins = q.memset(ap(a[0]), a[1])
        elif k == "scan":
            ins = q.tensor_tensor_scan(ap(a[0]), ap(a[1]), ap(a[2]), ap(a[3]), a[4], a[5])
        elif k == "act":
            if a[0][0] == "@":
                ins = q.activation(ap(a[0]), ap(a[1]), a[2])
            else:
                ins = q.activation(ap(a[0]), ap(a[1]), a[2], ap(a[3]), ap(a[4]))
        elif k == "mm":
            for x in a:
                ins = q.matmul(ap(x[0]), ap(x[1]), ap(x[2]), x[3], x[4])
        elif k == "sel":
            ins = q.affine_select(ap(a[0]), ap(a[1]), a[2], a[3], a[4], a[5], a[6])
        elif k == "iota":
            if _S[a[0][0]][1] == I32:
                ins = q.iota(ap(a[0]), a[1], a[2], a[3])
            else:
                ins = q.iota(ap(a[0]), a[1], a[2], a[3], allow_small_or_imprecise_dtypes=True)
        if i in mark:
            s, c = mark[i]
            ins.then_inc(T.sem[s], 16 if "sem" in op else 1)
            top[s] = c
            known[(s, c)] = dict(seen[e])
    top["sent"] = sends * len(eng)
    for s in sorted(top):
        g.wait_ge(T.sem[s], top[s])
